import numpy as np
import ml_dtypes


def mxq(x, axis, fmt="e4m3"):
    dtype, down = {"e4m3": (ml_dtypes.float8_e4m3fn, 7), "e5m2": (ml_dtypes.float8_e5m2, 14)}[fmt]
    v = np.moveaxis(np.asarray(x, np.float32).astype(ml_dtypes.bfloat16).astype(np.float64), axis, -1)
    blocks = v.reshape(v.shape[:-1] + (-1, 32))
    amax = np.abs(blocks).max(-1, keepdims=True)
    byte = np.maximum(np.where(amax > 0, np.frexp(amax)[1] - 1 + 127, 0) - down, 1)
    scale = np.exp2(byte - 127.0)
    codes = (blocks / scale).astype(np.float32).astype(dtype).astype(np.float64)
    return np.moveaxis((codes * scale).reshape(v.shape), -1, axis)


WIDE = False


def mx_kscale(k):
    if not WIDE:
        return np.ones(k)
    levels = np.array([24, -24, 12, -12, 0])
    if k % 512:
        return np.exp2(np.random.permutation(np.resize(levels, k // 32))).repeat(32)
    a = np.empty((k // 512, 16))
    for p in range(k // 512):
        a[p, :8] = np.random.permutation(np.resize(levels, 8))
        for g in range(8):
            far = levels[np.abs(levels - a[p, g]) >= 10]
            a[p, g + 8] = far[np.random.randint(len(far))]
    return np.exp2(a.ravel()).repeat(32)


def f64(x):
    return np.asarray(x).astype(np.float64)


def striped(idx):
    return np.tile(idx.reshape(-1, 16).T, (8, 1)).astype(np.uint16)


def unstriped(offs):
    return offs[:16].T.reshape(-1).astype(np.int64)


E2M1 = np.array([0.0, 0.5, 1.0, 1.5, 2.0, 3.0, 4.0, 6.0, -0.0, -0.5, -1.0, -1.5, -2.0, -3.0, -4.0, -6.0])


def pack_weight(w, fmt):
    k, n = w.shape
    w = f64(np.asarray(w, np.float32).astype(ml_dtypes.bfloat16)).reshape(k // 32, 32, n)
    amax = np.abs(w).max(1)
    if fmt == "e4m3":
        byte = np.frexp(amax)[1] - 1 + 127 - 7
    else:
        mant, ex = np.frexp(amax / 6.0)
        byte = np.where(mant > 0.5, ex, ex - 1) + 127
    byte = np.clip(np.where(amax > 0, byte, 1), 1, 254)
    scaled = (w * np.exp2(127.0 - byte)[:, None, :]).reshape(k, n).astype(np.float32)
    by_word = np.ascontiguousarray(scaled.reshape(k // 512, 128, 4, n).transpose(0, 1, 3, 2))
    if fmt == "e4m3":
        words = by_word.astype(ml_dtypes.float8_e4m3fn).view(np.uint8)
    else:
        c = by_word.astype(ml_dtypes.float4_e2m1fn).view(np.uint8) & 0xF
        words = (c[..., 0::2] | (c[..., 1::2] << 4)).reshape(k // 512, 128, 2 * n)
    return np.ascontiguousarray(words), np.ascontiguousarray(byte.astype(np.uint8).reshape(k // 512, 16, n))


def unpack_weight(words, scales, fmt):
    g, _, n = scales.shape
    words = np.ascontiguousarray(words).reshape(g, 128, n, -1)
    if fmt == "e4m3":
        vals = words.view(ml_dtypes.float8_e4m3fn).astype(np.float64)
    else:
        nib = np.empty((g, 128, n, 4), np.uint8)
        nib[..., 0::2] = words & 0xF
        nib[..., 1::2] = words >> 4
        vals = E2M1[nib]
    vals = vals * np.repeat(np.exp2(scales.astype(np.float64) - 127.0), 8, axis=1)[..., None]
    return vals.transpose(0, 1, 3, 2).reshape(g * 512, n)


def gelu(f):
    return 0.5 * f * (1.0 + np.tanh(np.sqrt(2.0 / np.pi) * (f + 0.044715 * f**3)))


K, R, T, M, J = 512, 1024, 2048, 512, 1024


def setup_inputs():
    n = np.random.standard_normal
    s = mx_kscale(K)[:, None]
    u = mx_kscale(R)[:, None]
    p_tab = pack_weight(n((K, T)) * s, "e4m3")
    p_tab2 = pack_weight(n((K, T)) * s, "e4m3")
    p_wa = pack_weight(n((K, R)) / np.sqrt(K) / s, "e4m3")
    p_wb = pack_weight(n((K, R)) / np.sqrt(K) / s, "e2m1")
    return {
        "tab_words": p_tab[0],
        "tab_scales": p_tab[1],
        "tab2_words": p_tab2[0],
        "tab2_scales": p_tab2[1],
        "wa_words": p_wa[0],
        "wa_scales": p_wa[1],
        "wb_words": p_wb[0],
        "wb_scales": p_wb[1],
        "sa": (np.random.uniform(0.5, 2.0, R) * u[:, 0]).astype(np.float32),
        "sb": (np.random.uniform(0.5, 2.0, R) / u[:, 0]).astype(np.float32),
        "offs": striped(np.random.permutation(T)[:M]),
        "offs2": striped(np.random.permutation(T)[:J]),
    }


def reference(tab_words, tab_scales, tab2_words, tab2_scales, wa_words, wa_scales, wb_words, wb_scales, sa, sb, offs, offs2):
    idx = unstriped(offs)
    idx2 = unstriped(offs2)
    tab_ = unpack_weight(tab_words, tab_scales, "e4m3")[:, idx]
    tab2_ = unpack_weight(tab2_words, tab2_scales, "e4m3")[:, idx2]
    wa_ = unpack_weight(wa_words, wa_scales, "e4m3")
    wb_ = unpack_weight(wb_words, wb_scales, "e2m1")
    za = wa_.T @ tab_
    zb = wb_.T @ tab2_
    ha = f64(sa)[:, None] * gelu(za)
    hb = f64(sb)[:, None] * gelu(zb)
    ha_ = mxq(ha, 0, "e4m3")
    hb_ = mxq(hb, 0, "e4m3")
    y = ha_.T @ hb_
    return np.exp(y * 0.015625)

@@ -1,0 +1,199 @@
+from contextlib import ExitStack
+
+import concourse.mybir as mybir
+from concourse.masks import make_identity
+
+K, R, T, M, J = 512, 1024, 2048, 512, 1024
+FLOPS = 2 * K * R * M + 2 * K * R * J + 2 * R * M * J
+
+F32 = mybir.dt.float32
+BF16 = mybir.dt.bfloat16
+I32 = mybir.dt.int32
+U32 = mybir.dt.uint32
+U16 = mybir.dt.uint16
+U8 = mybir.dt.uint8
+FP8X4 = mybir.dt.float8_e4m3fn_x4
+FP4X4 = mybir.dt.float4_e2m1fn_x4
+ACT = mybir.ActivationFunctionType
+MULT = mybir.AluOpType.mult
+
+P = 128
+SLOTS = 4
+PASSES = R // 512
+NB = 128
+ON_GPSIMD = 4
+
+
+def tile_list_biaff_gelu_exp_kernel(tc, tab_words, tab_scales, tab2_words, tab2_scales, wa_words, wa_scales, wb_words, wb_scales, sa, sb, offs, offs2, out):
+    nc = tc.nc
+    with ExitStack() as ctx:
+        lists = ctx.enter_context(tc.tile_pool(name="lists", bufs=1))
+        keep = ctx.enter_context(tc.tile_pool(name="keep", bufs=1))
+        psum = ctx.enter_context(tc.psum_pool(name="psum", bufs=1))
+
+        offs_a = lists.tile([P, M // 16], U16, name="offs_a")
+        offs_b = lists.tile([P, J // 16], U16, name="offs_b")
+
+        def plane(name, cols):
+            return keep.tile([P, cols // 4], I32, name=name, align_bytes=64)
+
+        wb_s = keep.tile([P, R // 4], I32, name="wb_s", align_bytes=64)
+        tb_s = plane("tb_s", T)
+        ta_s = plane("ta_s", T)
+        wa_s = plane("wa_s", R)
+        s_rows = keep.tile([P, 2 * P], F32, name="s_rows")
+        ident = keep.tile([P, P], F32, name="ident")
+        nc.gpsimd.memset(wb_s[:], 0)
+        nc.vector.memset(tb_s[:], 0)
+        nc.vector.memset(s_rows[:], 0.0)
+        nc.vector.memset(ta_s[:], 0)
+        nc.vector.memset(wa_s[:], 0)
+
+        wb_w = keep.tile([P, R // 2], I32, name="wb_w", align_bytes=64)
+        tb_w = keep.tile([P, T], I32, name="tb_w", align_bytes=64)
+
+        def load_scales(dst, src, which=range(4), eng=nc.sync):
+            rows = src[0].bitcast(I32)
+            for q in which:
+                eng.dma_start(dst[32 * q : 32 * q + 4, :], rows[4 * q : 4 * q + 4, :])
+
+        def load_words(dst, src):
+            nc.sync.dma_start(dst[:], src[0].rearrange("p t i -> p (t i)").bitcast(I32))
+
+        def load_factor(first, vec):
+            nc.sync.dma_start(
+                s_rows[first : first + SLOTS, :].rearrange("t (b i) -> t b i", i=8),
+                vec.rearrange("(b t i) -> t b i", t=SLOTS, i=8),
+            )
+
+        nc.sync.dma_start(wb_w[:], wb_words[0].bitcast(I32))
+        load_scales(wb_s, wb_scales, [3])
+        load_words(tb_w, tab2_words)
+        nc.sync.dma_start(offs_b[:], offs2)
+        load_scales(tb_s, tab2_scales, eng=nc.scalar)
+        load_scales(wb_s, wb_scales, [0, 1, 2], eng=nc.scalar)
+        warm = keep.tile([P, 1], F32, name="warm")
+        nc.scalar.activation(warm[32:64, :], s_rows[32:64, 0:1], ACT.Gelu_apprx_tanh)
+        make_identity(nc, ident[:])
+        load_factor(0, sa)
+        load_factor(SLOTS, sb)
+        nc.sync.dma_start(offs_a[:], offs)
+
+        s_ps = psum.tile([P, PASSES, P], F32, name="s_ps")
+
+        def permute(name, src, run):
+            dst = keep.tile([P, src.shape[1]], I32, name=name, align_bytes=64)
+            nc.vector.tensor_copy(
+                dst[:].rearrange("p (t b i) -> p t b i", t=SLOTS, i=run),
+                src[:].rearrange("p (b t i) -> p t b i", t=SLOTS, i=run),
+            )
+            return dst
+
+        def gather(name, words, scales, offsets, n):
+            gw = keep.tile([P, n], U32, name=name + "_w", align_bytes=64)
+            gs = keep.tile([P, n], U8, name=name + "_s", align_bytes=64)
+            nc.vector.tensor_copy(gw[:], words[:].bitcast(U32).indirect(offsets))
+            nc.vector.tensor_copy(gs[:], scales[:].bitcast(U8).indirect(offsets))
+            return gw, gs
+
+        ta_w = keep.tile([P, T], I32, name="ta_w", align_bytes=64)
+        wa_w = keep.tile([P, R], I32, name="wa_w", align_bytes=64)
+        load_words(ta_w, tab_words)
+        load_scales(ta_s, tab_scales, eng=nc.scalar)
+        load_words(wa_w, wa_words)
+        load_scales(wa_s, wa_scales)
+        s_sb = keep.tile([P, PASSES, 2 * SLOTS], F32, name="s_sb")
+        GB = 256
+        gb = [gather("gb0", tb_w, tb_s, offs_b[:, 0 : GB // 16], GB)]
+        wb_wp = permute("wb_wp", wb_w, 4)
+        wb_sp = permute("wb_sp", wb_s, 2)
+        gb += [gather("gb%d" % g, tb_w, tb_s, offs_b[:, g * GB // 16 : (g + 1) * GB // 16], GB) for g in range(1, J // GB)]
+        ga = gather("ga", ta_w, ta_s, offs_a[:], M)
+        wa_wp = permute("wa_wp", wa_w, 8)
+        wa_sp = permute("wa_sp", wa_s, 2)
+
+        def wb_tile(a, t):
+            c = (t * PASSES + a) * P
+            return wb_wp[:].bitcast(U8)[:, 2 * c : 2 * c + 2 * P].bitcast(FP4X4), wb_sp[:].bitcast(U8)[:, c : c + P]
+
+        def wa_tile(a, t):
+            c = (t * PASSES + a) * P
+            return wa_wp[:, c : c + P].bitcast(FP8X4), wa_sp[:].bitcast(U8)[:, c : c + P]
+
+        def hidden(weights, a, g, c0, dst):
+            z = psum.tile([P, SLOTS, NB], F32, name="z", tag="z", bufs=3)
+            for t in range(SLOTS):
+                w, ws = weights(a, t)
+                nc.tensor.matmul_mx(
+                    out=z[:, t, :], lhsT=w, lhsT_scale=ws,
+                    rhs=g[0][:, c0 : c0 + NB].bitcast(FP8X4), rhs_scale=g[1][:, c0 : c0 + NB],
+                    start=True, stop=True,
+                )
+            nc.scalar.activation(dst, z[:].rearrange("p t n -> p n t"), ACT.Gelu_apprx_tanh)
+
+        hb_w = keep.tile([P, PASSES, J], U32, name="hb_w", align_bytes=64)
+        hb_s = keep.tile([P, PASSES, J], U8, name="hb_s", align_bytes=64)
+        ha_w = keep.tile([P, M // P, PASSES, P], U32, name="ha_w", align_bytes=64)
+        ha_s = keep.tile([P, M // P, PASSES, P], U8, name="ha_s", align_bytes=64)
+
+        hb16 = keep.tile([P, PASSES, J, SLOTS], BF16, name="hb16", align_bytes=64)
+        ha16 = keep.tile([P, M // P, PASSES, NB, SLOTS], BF16, name="ha16", align_bytes=64)
+        units = []
+        for g in range(J // GB):
+            for a in range(PASSES):
+                gel = keep.tile([P, 2, NB, SLOTS], F32, name="gel_b%d_%d" % (g, a))
+                for h in range(2):
+                    hidden(wb_tile, a, gb[g], h * NB, gel[:, h])
+                if g == 0 and a == 0:
+                    for c in range(PASSES):
+                        nc.tensor.transpose(s_ps[:, c, :], s_rows[:, c * P : (c + 1) * P], ident[:])
+                    nc.scalar.copy(s_sb[:], s_ps[:, :, 0 : 2 * SLOTS])
+                src = s_sb if len(units) < ON_GPSIMD else s_ps
+                fac = src[:, a, SLOTS : 2 * SLOTS].unsqueeze(1).to_broadcast([P, 2 * NB, SLOTS])
+                units.append((hb16[:, a, g * GB : (g + 1) * GB, :], gel[:].rearrange("p h n t -> p (h n) t"), fac))
+        for mt in range(M // P):
+            gel = keep.tile([P, PASSES, NB, SLOTS], F32, name="gel_a%d" % mt)
+            for a in range(PASSES):
+                hidden(wa_tile, a, ga, mt * NB, gel[:, a])
+            fac = s_ps[:, :, 0:SLOTS].unsqueeze(2).to_broadcast([P, PASSES, NB, SLOTS])
+            units.append((ha16[:, mt], gel[:], fac))
+
+        def scale(u):
+            eng = nc.gpsimd if u < ON_GPSIMD else nc.vector
+            eng.tensor_tensor(units[u][0], units[u][1], units[u][2], MULT)
+
+        def quantize_b(a):
+            nc.vector.quantize_mx(out=hb_w[:, a, :].bitcast(FP8X4), scales=hb_s[:, a, :], in_=hb16[:, a].rearrange("p j t -> p (j t)"))
+
+        def quantize_a(mt):
+            nc.vector.quantize_mx(
+                out=ha_w[:, mt].rearrange("p a n -> p (a n)").bitcast(FP8X4),
+                scales=ha_s[:, mt].rearrange("p a n -> p (a n)"),
+                in_=ha16[:, mt].rearrange("p a n t -> p (a n t)"),
+            )
+
+        def scores(mt):
+            for jh in range(J // 512):
+                cols = slice(jh * 512, (jh + 1) * 512)
+                y = psum.tile([P, 512], F32, name="y", tag="y", bufs=4)
+                for a in range(PASSES):
+                    nc.tensor.matmul_mx(
+                        out=y[:], lhsT=ha_w[:, mt, a, :].bitcast(FP8X4), lhsT_scale=ha_s[:, mt, a, :],
+                        rhs=hb_w[:, a, cols].bitcast(FP8X4), rhs_scale=hb_s[:, a, cols],
+                        start=(a == 0), stop=(a == PASSES - 1),
+                    )
+                res = keep.tile([P, 512], F32, name="res%d_%d" % (mt, jh))
+                nc.scalar.activation(res[:], y[:], ACT.Exp, scale=0.015625)
+                nc.sync.dma_start(out[mt * P : (mt + 1) * P, cols], res[:])
+
+        first_a = len(units) - M // P
+        for u in range(first_a):
+            scale(u)
+        quantize_b(0)
+        scale(first_a)
+        quantize_b(1)
+        for mt in range(M // P):
+            if mt + 1 < M // P:
+                scale(first_a + mt + 1)
+            quantize_a(mt)
+            scores(mt)

@@ -21,7 +21,7 @@ P = 128
 SLOTS = 4
 PASSES = R // 512
 NB = 128
-ON_GPSIMD = 4
+ON_GPSIMD = 3
 
 
 def tile_list_biaff_gelu_exp_kernel(tc, tab_words, tab_scales, tab2_words, tab2_scales, wa_words, wa_scales, wb_words, wb_scales, sa, sb, offs, offs2, out):
@@ -67,16 +67,14 @@ def tile_list_biaff_gelu_exp_kernel(tc, tab_words, tab_scales, tab2_words, tab2_
             )
 
         nc.sync.dma_start(wb_w[:], wb_words[0].bitcast(I32))
-        load_scales(wb_s, wb_scales, [3])
+        load_scales(wb_s, wb_scales, [2, 3])
         load_words(tb_w, tab2_words)
         nc.sync.dma_start(offs_b[:], offs2)
         load_scales(tb_s, tab2_scales, eng=nc.scalar)
-        load_scales(wb_s, wb_scales, [0, 1, 2], eng=nc.scalar)
+        load_scales(wb_s, wb_scales, [0, 1], eng=nc.scalar)
         warm = keep.tile([P, 1], F32, name="warm")
         nc.scalar.activation(warm[32:64, :], s_rows[32:64, 0:1], ACT.Gelu_apprx_tanh)
         make_identity(nc, ident[:])
-        load_factor(0, sa)
-        load_factor(SLOTS, sb)
         nc.sync.dma_start(offs_a[:], offs)
 
         s_ps = psum.tile([P, PASSES, P], F32, name="s_ps")
@@ -98,10 +96,13 @@ def tile_list_biaff_gelu_exp_kernel(tc, tab_words, tab_scales, tab2_words, tab2_
 
         ta_w = keep.tile([P, T], I32, name="ta_w", align_bytes=64)
         wa_w = keep.tile([P, R], I32, name="wa_w", align_bytes=64)
+        load_scales(wa_s, wa_scales, eng=nc.scalar)
+        load_scales(ta_s, tab_scales, [0, 1], eng=nc.scalar)
+        load_scales(ta_s, tab_scales, [2, 3])
         load_words(ta_w, tab_words)
-        load_scales(ta_s, tab_scales, eng=nc.scalar)
         load_words(wa_w, wa_words)
-        load_scales(wa_s, wa_scales)
+        load_factor(0, sa)
+        load_factor(SLOTS, sb)
         s_sb = keep.tile([P, PASSES, 2 * SLOTS], F32, name="s_sb")
         GB = 256
         gb = [gather("gb0", tb_w, tb_s, offs_b[:, 0 : GB // 16], GB)]
@@ -147,7 +148,7 @@ def tile_list_biaff_gelu_exp_kernel(tc, tab_words, tab_scales, tab2_words, tab2_
                 if g == 0 and a == 0:
                     for c in range(PASSES):
                         nc.tensor.transpose(s_ps[:, c, :], s_rows[:, c * P : (c + 1) * P], ident[:])
-                    nc.scalar.copy(s_sb[:], s_ps[:, :, 0 : 2 * SLOTS])
+                    nc.vector.tensor_copy(s_sb[:], s_ps[:, :, 0 : 2 * SLOTS])
                 src = s_sb if len(units) < ON_GPSIMD else s_ps
                 fac = src[:, a, SLOTS : 2 * SLOTS].unsqueeze(1).to_broadcast([P, 2 * NB, SLOTS])
                 units.append((hb16[:, a, g * GB : (g + 1) * GB, :], gel[:].rearrange("p h n t -> p (h n) t"), fac))
@@ -189,10 +190,13 @@ def tile_list_biaff_gelu_exp_kernel(tc, tab_words, tab_scales, tab2_words, tab2_
         first_a = len(units) - M // P
         for u in range(first_a):
             scale(u)
-        quantize_b(0)
         scale(first_a)
+        quantize_b(0)
+        quantize_a(0)
         quantize_b(1)
-        for mt in range(M // P):
+        scores(0)
+        scale(first_a + 1)
+        for mt in range(1, M // P):
             if mt + 1 < M // P:
                 scale(first_a + mt + 1)
             quantize_a(mt)

@@ -22,6 +22,7 @@ SLOTS = 4
 PASSES = R // 512
 NB = 128
 ON_GPSIMD = 3
+AHEAD = 5
 
 
 def tile_list_biaff_gelu_exp_kernel(tc, tab_words, tab_scales, tab2_words, tab2_scales, wa_words, wa_scales, wb_words, wb_scales, sa, sb, offs, offs2, out):
@@ -37,10 +38,10 @@ def tile_list_biaff_gelu_exp_kernel(tc, tab_words, tab_scales, tab2_words, tab2_
         def plane(name, cols):
             return keep.tile([P, cols // 4], I32, name=name, align_bytes=64)
 
-        wb_s = keep.tile([P, R // 4], I32, name="wb_s", align_bytes=64)
+        wb_s = keep.tile([P, R // 4], I32, name="wb_s", tag="early", align_bytes=64)
         tb_s = plane("tb_s", T)
         ta_s = plane("ta_s", T)
-        wa_s = plane("wa_s", R)
+        wa_s = keep.tile([P, R // 4], I32, name="wa_s", tag="late", align_bytes=64)
         s_rows = keep.tile([P, 2 * P], F32, name="s_rows")
         ident = keep.tile([P, P], F32, name="ident")
         nc.gpsimd.memset(wb_s[:], 0)
@@ -66,16 +67,16 @@ def tile_list_biaff_gelu_exp_kernel(tc, tab_words, tab_scales, tab2_words, tab2_
                 vec.rearrange("(b t i) -> t b i", t=SLOTS, i=8),
             )
 
-        nc.sync.dma_start(wb_w[:], wb_words[0].bitcast(I32))
-        load_scales(wb_s, wb_scales, [2, 3])
-        load_words(tb_w, tab2_words)
         nc.sync.dma_start(offs_b[:], offs2)
-        load_scales(tb_s, tab2_scales, eng=nc.scalar)
-        load_scales(wb_s, wb_scales, [0, 1], eng=nc.scalar)
+        nc.sync.dma_start(wb_w[:], wb_words[0].bitcast(I32))
+        load_scales(tb_s, tab2_scales)
+        load_words(tb_w, tab2_words)
+        load_scales(wb_s, wb_scales)
         warm = keep.tile([P, 1], F32, name="warm")
         nc.scalar.activation(warm[32:64, :], s_rows[32:64, 0:1], ACT.Gelu_apprx_tanh)
         make_identity(nc, ident[:])
-        nc.sync.dma_start(offs_a[:], offs)
+        load_factor(0, sa)
+        load_factor(SLOTS, sb)
 
         s_ps = psum.tile([P, PASSES, P], F32, name="s_ps")
 
@@ -87,8 +88,8 @@ def tile_list_biaff_gelu_exp_kernel(tc, tab_words, tab_scales, tab2_words, tab2_
             )
             return dst
 
-        def gather(name, words, scales, offsets, n):
-            gw = keep.tile([P, n], U32, name=name + "_w", align_bytes=64)
+        def gather(name, words, scales, offsets, n, tag=""):
+            gw = keep.tile([P, n], U32, name=name + "_w", tag=tag, align_bytes=64)
             gs = keep.tile([P, n], U8, name=name + "_s", align_bytes=64)
             nc.vector.tensor_copy(gw[:], words[:].bitcast(U32).indirect(offsets))
             nc.vector.tensor_copy(gs[:], scales[:].bitcast(U8).indirect(offsets))
@@ -96,19 +97,17 @@ def tile_list_biaff_gelu_exp_kernel(tc, tab_words, tab_scales, tab2_words, tab2_
 
         ta_w = keep.tile([P, T], I32, name="ta_w", align_bytes=64)
         wa_w = keep.tile([P, R], I32, name="wa_w", align_bytes=64)
-        load_scales(wa_s, wa_scales, eng=nc.scalar)
-        load_scales(ta_s, tab_scales, [0, 1], eng=nc.scalar)
-        load_scales(ta_s, tab_scales, [2, 3])
         load_words(ta_w, tab_words)
+        nc.sync.dma_start(offs_a[:], offs)
+        load_scales(ta_s, tab_scales)
         load_words(wa_w, wa_words)
-        load_factor(0, sa)
-        load_factor(SLOTS, sb)
-        s_sb = keep.tile([P, PASSES, 2 * SLOTS], F32, name="s_sb")
+        load_scales(wa_s, wa_scales)
+        s_sb = keep.tile([P, PASSES, SLOTS], F32, name="s_sb")
         GB = 256
         gb = [gather("gb0", tb_w, tb_s, offs_b[:, 0 : GB // 16], GB)]
         wb_wp = permute("wb_wp", wb_w, 4)
         wb_sp = permute("wb_sp", wb_s, 2)
-        gb += [gather("gb%d" % g, tb_w, tb_s, offs_b[:, g * GB // 16 : (g + 1) * GB // 16], GB) for g in range(1, J // GB)]
+        gb.append(gather("gb1", tb_w, tb_s, offs_b[:, GB // 16 :], J - GB, "early"))
         ga = gather("ga", ta_w, ta_s, offs_a[:], M)
         wa_wp = permute("wa_wp", wa_w, 8)
         wa_sp = permute("wa_sp", wa_s, 2)
@@ -132,72 +131,81 @@ def tile_list_biaff_gelu_exp_kernel(tc, tab_words, tab_scales, tab2_words, tab2_
                 )
             nc.scalar.activation(dst, z[:].rearrange("p t n -> p n t"), ACT.Gelu_apprx_tanh)
 
-        hb_w = keep.tile([P, PASSES, J], U32, name="hb_w", align_bytes=64)
         hb_s = keep.tile([P, PASSES, J], U8, name="hb_s", align_bytes=64)
-        ha_w = keep.tile([P, M // P, PASSES, P], U32, name="ha_w", align_bytes=64)
         ha_s = keep.tile([P, M // P, PASSES, P], U8, name="ha_s", align_bytes=64)
 
-        hb16 = keep.tile([P, PASSES, J, SLOTS], BF16, name="hb16", align_bytes=64)
+        hb16 = keep.tile([P, PASSES, J, SLOTS], BF16, name="hb16", tag="late", align_bytes=64)
         ha16 = keep.tile([P, M // P, PASSES, NB, SLOTS], BF16, name="ha16", align_bytes=64)
         units = []
         for g in range(J // GB):
             for a in range(PASSES):
                 gel = keep.tile([P, 2, NB, SLOTS], F32, name="gel_b%d_%d" % (g, a))
                 for h in range(2):
-                    hidden(wb_tile, a, gb[g], h * NB, gel[:, h])
+                    hidden(wb_tile, a, gb[min(g, 1)], max(g - 1, 0) * GB + h * NB, gel[:, h])
                 if g == 0 and a == 0:
                     for c in range(PASSES):
                         nc.tensor.transpose(s_ps[:, c, :], s_rows[:, c * P : (c + 1) * P], ident[:])
-                    nc.vector.tensor_copy(s_sb[:], s_ps[:, :, 0 : 2 * SLOTS])
-                src = s_sb if len(units) < ON_GPSIMD else s_ps
-                fac = src[:, a, SLOTS : 2 * SLOTS].unsqueeze(1).to_broadcast([P, 2 * NB, SLOTS])
+                    nc.vector.tensor_copy(s_sb[:], s_ps[:, :, SLOTS : 2 * SLOTS])
+                src = s_sb[:, a, :] if len(units) < ON_GPSIMD else s_ps[:, a, SLOTS : 2 * SLOTS]
+                fac = src.unsqueeze(1).to_broadcast([P, 2 * NB, SLOTS])
                 units.append((hb16[:, a, g * GB : (g + 1) * GB, :], gel[:].rearrange("p h n t -> p (h n) t"), fac))
         for mt in range(M // P):
-            gel = keep.tile([P, PASSES, NB, SLOTS], F32, name="gel_a%d" % mt)
             for a in range(PASSES):
-                hidden(wa_tile, a, ga, mt * NB, gel[:, a])
-            fac = s_ps[:, :, 0:SLOTS].unsqueeze(2).to_broadcast([P, PASSES, NB, SLOTS])
-            units.append((ha16[:, mt], gel[:], fac))
+                tag = "codes" if mt * PASSES + a == AHEAD - 1 else ""
+                gel = keep.tile([P, NB, SLOTS], F32, name="gel_a%d_%d" % (mt, a), tag=tag, align_bytes=64)
+                hidden(wa_tile, a, ga, mt * NB, gel[:])
+                fac = s_ps[:, a, 0:SLOTS].unsqueeze(1).to_broadcast([P, NB, SLOTS])
+                units.append((ha16[:, mt, a], gel[:], fac))
 
         def scale(u):
             eng = nc.gpsimd if u < ON_GPSIMD else nc.vector
             eng.tensor_tensor(units[u][0], units[u][1], units[u][2], MULT)
 
-        def quantize_b(a):
-            nc.vector.quantize_mx(out=hb_w[:, a, :].bitcast(FP8X4), scales=hb_s[:, a, :], in_=hb16[:, a].rearrange("p j t -> p (j t)"))
+        def quantize_b(a, jh):
+            cols = slice(jh * 512, (jh + 1) * 512)
+            nc.vector.quantize_mx(out=hb_w[:, a, cols].bitcast(FP8X4), scales=hb_s[:, a, cols], in_=hb16[:, a, cols, :].rearrange("p j t -> p (j t)"))
 
-        def quantize_a(mt):
-            nc.vector.quantize_mx(
-                out=ha_w[:, mt].rearrange("p a n -> p (a n)").bitcast(FP8X4),
-                scales=ha_s[:, mt].rearrange("p a n -> p (a n)"),
-                in_=ha16[:, mt].rearrange("p a n t -> p (a n t)"),
+        def quantize_a(mt, a):
+            nc.vector.quantize_mx(out=ha_w[:, mt, a, :].bitcast(FP8X4), scales=ha_s[:, mt, a, :], in_=ha16[:, mt, a].rearrange("p n t -> p (n t)"))
+
+        banks = {}
+
+        def scores(mt, jh, a):
+            cols = slice(jh * 512, (jh + 1) * 512)
+            if a == 0:
+                banks[mt, jh] = psum.tile([P, 512], F32, name="y", tag="y", bufs=4)
+            y = banks[mt, jh]
+            nc.tensor.matmul_mx(
+                out=y[:], lhsT=ha_w[:, mt, a, :].bitcast(FP8X4), lhsT_scale=ha_s[:, mt, a, :],
+                rhs=hb_w[:, a, cols].bitcast(FP8X4), rhs_scale=hb_s[:, a, cols],
+                start=(a == 0), stop=(a == PASSES - 1),
             )
-
-        def scores(mt):
-            for jh in range(J // 512):
-                cols = slice(jh * 512, (jh + 1) * 512)
-                y = psum.tile([P, 512], F32, name="y", tag="y", bufs=4)
-                for a in range(PASSES):
-                    nc.tensor.matmul_mx(
-                        out=y[:], lhsT=ha_w[:, mt, a, :].bitcast(FP8X4), lhsT_scale=ha_s[:, mt, a, :],
-                        rhs=hb_w[:, a, cols].bitcast(FP8X4), rhs_scale=hb_s[:, a, cols],
-                        start=(a == 0), stop=(a == PASSES - 1),
-                    )
+            if a == PASSES - 1:
                 res = keep.tile([P, 512], F32, name="res%d_%d" % (mt, jh))
                 nc.scalar.activation(res[:], y[:], ACT.Exp, scale=0.015625)
                 nc.sync.dma_start(out[mt * P : (mt + 1) * P, cols], res[:])
 
-        first_a = len(units) - M // P
-        for u in range(first_a):
+        first_a = PASSES * J // GB
+        for u in range(first_a + AHEAD):
             scale(u)
-        scale(first_a)
-        quantize_b(0)
-        quantize_a(0)
-        quantize_b(1)
-        scores(0)
-        scale(first_a + 1)
-        for mt in range(1, M // P):
-            if mt + 1 < M // P:
-                scale(first_a + mt + 1)
-            quantize_a(mt)
-            scores(mt)
+        codes = keep.tile([P, PASSES * (J + M)], U32, name="codes", tag="codes", align_bytes=64)
+        hb_w = codes[:, : PASSES * J].rearrange("p (a j) -> p a j", a=PASSES)
+        ha_w = codes[:, PASSES * J :].rearrange("p (m a n) -> p m a n", a=PASSES, n=P)
+        for a in range(PASSES):
+            quantize_b(a, 0)
+            quantize_a(0, a)
+            scores(0, 0, a)
+        for a in range(PASSES):
+            quantize_a(1, a)
+            scores(1, 0, a)
+        for a in range(PASSES):
+            quantize_b(a, 1)
+            scores(0, 1, a)
+            scores(1, 1, a)
+        for h in range(2 * PASSES, PASSES * M // P):
+            mt, a = divmod(h, PASSES)
+            if h + 1 < PASSES * M // P:
+                scale(first_a + h + 1)
+            quantize_a(mt, a)
+            for jh in range(J // 512):
+                scores(mt, jh, a)

@@ -22,7 +22,7 @@ SLOTS = 4
 PASSES = R // 512
 NB = 128
 ON_GPSIMD = 3
-AHEAD = 5
+AHEAD = 4
 
 
 def tile_list_biaff_gelu_exp_kernel(tc, tab_words, tab_scales, tab2_words, tab2_scales, wa_words, wa_scales, wb_words, wb_scales, sa, sb, offs, offs2, out):
@@ -198,6 +198,7 @@ def tile_list_biaff_gelu_exp_kernel(tc, tab_words, tab_scales, tab2_words, tab2_
         for a in range(PASSES):
             quantize_a(1, a)
             scores(1, 0, a)
+        scale(first_a + AHEAD)
         for a in range(PASSES):
             quantize_b(a, 1)
             scores(0, 1, a)

@@ -21,8 +21,6 @@ P = 128
 SLOTS = 4
 PASSES = R // 512
 NB = 128
-ON_GPSIMD = 3
-AHEAD = 4
 
 
 def tile_list_biaff_gelu_exp_kernel(tc, tab_words, tab_scales, tab2_words, tab2_scales, wa_words, wa_scales, wb_words, wb_scales, sa, sb, offs, offs2, out):
@@ -44,8 +42,8 @@ def tile_list_biaff_gelu_exp_kernel(tc, tab_words, tab_scales, tab2_words, tab2_
         wa_s = keep.tile([P, R // 4], I32, name="wa_s", tag="late", align_bytes=64)
         s_rows = keep.tile([P, 2 * P], F32, name="s_rows")
         ident = keep.tile([P, P], F32, name="ident")
-        nc.gpsimd.memset(wb_s[:], 0)
         nc.vector.memset(tb_s[:], 0)
+        nc.vector.memset(wb_s[:], 0)
         nc.vector.memset(s_rows[:], 0.0)
         nc.vector.memset(ta_s[:], 0)
         nc.vector.memset(wa_s[:], 0)
@@ -67,16 +65,16 @@ def tile_list_biaff_gelu_exp_kernel(tc, tab_words, tab_scales, tab2_words, tab2_
                 vec.rearrange("(b t i) -> t b i", t=SLOTS, i=8),
             )
 
-        nc.sync.dma_start(offs_b[:], offs2)
         nc.sync.dma_start(wb_w[:], wb_words[0].bitcast(I32))
+        nc.sync.dma_start(offs_b[:], offs2)
         load_scales(tb_s, tab2_scales)
         load_words(tb_w, tab2_words)
+        load_factor(0, sa)
+        load_factor(SLOTS, sb)
         load_scales(wb_s, wb_scales)
         warm = keep.tile([P, 1], F32, name="warm")
         nc.scalar.activation(warm[32:64, :], s_rows[32:64, 0:1], ACT.Gelu_apprx_tanh)
         make_identity(nc, ident[:])
-        load_factor(0, sa)
-        load_factor(SLOTS, sb)
 
         s_ps = psum.tile([P, PASSES, P], F32, name="s_ps")
 
@@ -88,12 +86,15 @@ def tile_list_biaff_gelu_exp_kernel(tc, tab_words, tab_scales, tab2_words, tab2_
             )
             return dst
 
-        def gather(name, words, scales, offsets, n, tag=""):
-            gw = keep.tile([P, n], U32, name=name + "_w", tag=tag, align_bytes=64)
-            gs = keep.tile([P, n], U8, name=name + "_s", align_bytes=64)
+        def gather_words(name, words, offsets, n, tag=""):
+            gw = keep.tile([P, n], U32, name=name, tag=tag, align_bytes=64)
             nc.vector.tensor_copy(gw[:], words[:].bitcast(U32).indirect(offsets))
+            return gw
+
+        def gather_scales(name, scales, offsets, n):
+            gs = keep.tile([P, n], U8, name=name, align_bytes=64)
             nc.vector.tensor_copy(gs[:], scales[:].bitcast(U8).indirect(offsets))
-            return gw, gs
+            return gs
 
         ta_w = keep.tile([P, T], I32, name="ta_w", align_bytes=64)
         wa_w = keep.tile([P, R], I32, name="wa_w", align_bytes=64)
@@ -102,13 +103,18 @@ def tile_list_biaff_gelu_exp_kernel(tc, tab_words, tab_scales, tab2_words, tab2_
         load_scales(ta_s, tab_scales)
         load_words(wa_w, wa_words)
         load_scales(wa_s, wa_scales)
-        s_sb = keep.tile([P, PASSES, SLOTS], F32, name="s_sb")
+        s_sb = keep.tile([P, PASSES, 2 * SLOTS], F32, name="s_sb")
+        for c in range(PASSES):
+            nc.tensor.transpose(s_ps[:, c, :], s_rows[:, c * P : (c + 1) * P], ident[:])
+        nc.scalar.copy(s_sb[:], s_ps[:, :, 0 : 2 * SLOTS])
         GB = 256
-        gb = [gather("gb0", tb_w, tb_s, offs_b[:, 0 : GB // 16], GB)]
         wb_wp = permute("wb_wp", wb_w, 4)
+        gb_s = gather_scales("gb_s", tb_s, offs_b[:], J)
+        gb = [(gather_words("gb0_w", tb_w, offs_b[:, 0 : GB // 16], GB)[:], gb_s[:, :GB])]
         wb_sp = permute("wb_sp", wb_s, 2)
-        gb.append(gather("gb1", tb_w, tb_s, offs_b[:, GB // 16 :], J - GB, "early"))
-        ga = gather("ga", ta_w, ta_s, offs_a[:], M)
+        gb.append((gather_words("gb1_w", tb_w, offs_b[:, GB // 16 :], J - GB, "early")[:], gb_s[:, GB:]))
+        ga_w = gather_words("ga_w", ta_w, offs_a[:], M)
+        ga = (ga_w[:], gather_scales("ga_s", ta_s, offs_a[:], M)[:])
         wa_wp = permute("wa_wp", wa_w, 8)
         wa_sp = permute("wa_sp", wa_s, 2)
 
@@ -134,39 +140,50 @@ def tile_list_biaff_gelu_exp_kernel(tc, tab_words, tab_scales, tab2_words, tab2_
         hb_s = keep.tile([P, PASSES, J], U8, name="hb_s", align_bytes=64)
         ha_s = keep.tile([P, M // P, PASSES, P], U8, name="ha_s", align_bytes=64)
 
-        hb16 = keep.tile([P, PASSES, J, SLOTS], BF16, name="hb16", tag="late", align_bytes=64)
-        ha16 = keep.tile([P, M // P, PASSES, NB, SLOTS], BF16, name="ha16", align_bytes=64)
-        units = []
+        hb16 = keep.tile([P, J // 512, PASSES, 512, SLOTS], BF16, name="hb16", tag="late", align_bytes=64)
+        hb16_first = keep.tile([P, GB, SLOTS], BF16, name="hb16_first", tag="first", align_bytes=64)
+        gel_b = []
         for g in range(J // GB):
+            gel = keep.tile([P, PASSES, GB, SLOTS], F32, name="gel_b%d" % g, tag="codes" if g == J // GB - 1 else "", align_bytes=64)
             for a in range(PASSES):
-                gel = keep.tile([P, 2, NB, SLOTS], F32, name="gel_b%d_%d" % (g, a))
-                for h in range(2):
-                    hidden(wb_tile, a, gb[min(g, 1)], max(g - 1, 0) * GB + h * NB, gel[:, h])
-                if g == 0 and a == 0:
-                    for c in range(PASSES):
-                        nc.tensor.transpose(s_ps[:, c, :], s_rows[:, c * P : (c + 1) * P], ident[:])
-                    nc.vector.tensor_copy(s_sb[:], s_ps[:, :, SLOTS : 2 * SLOTS])
-                src = s_sb[:, a, :] if len(units) < ON_GPSIMD else s_ps[:, a, SLOTS : 2 * SLOTS]
-                fac = src.unsqueeze(1).to_broadcast([P, 2 * NB, SLOTS])
-                units.append((hb16[:, a, g * GB : (g + 1) * GB, :], gel[:].rearrange("p h n t -> p (h n) t"), fac))
+                for h in range(GB // NB):
+                    hidden(wb_tile, a, gb[min(g, 1)], max(g - 1, 0) * GB + h * NB, gel[:, a, h * NB : (h + 1) * NB, :])
+            gel_b.append(gel)
+        gel_a = []
         for mt in range(M // P):
+            gel = keep.tile([P, PASSES, NB, SLOTS], F32, name="gel_a%d" % mt)
             for a in range(PASSES):
-                tag = "codes" if mt * PASSES + a == AHEAD - 1 else ""
-                gel = keep.tile([P, NB, SLOTS], F32, name="gel_a%d_%d" % (mt, a), tag=tag, align_bytes=64)
-                hidden(wa_tile, a, ga, mt * NB, gel[:])
-                fac = s_ps[:, a, 0:SLOTS].unsqueeze(1).to_broadcast([P, NB, SLOTS])
-                units.append((ha16[:, mt, a], gel[:], fac))
+                hidden(wa_tile, a, ga, mt * NB, gel[:, a])
+            gel_a.append(gel)
 
-        def scale(u):
-            eng = nc.gpsimd if u < ON_GPSIMD else nc.vector
-            eng.tensor_tensor(units[u][0], units[u][1], units[u][2], MULT)
+        def factor(eng, first, a0, a1, n):
+            src = s_sb if eng is nc.gpsimd else s_ps
+            return src[:, a0:a1, first : first + SLOTS].unsqueeze(2).to_broadcast([P, a1 - a0, n, SLOTS])
 
-        def quantize_b(a, jh):
-            cols = slice(jh * 512, (jh + 1) * 512)
-            nc.vector.quantize_mx(out=hb_w[:, a, cols].bitcast(FP8X4), scales=hb_s[:, a, cols], in_=hb16[:, a, cols, :].rearrange("p j t -> p (j t)"))
+        def rounded_b(g, a):
+            c = g % 2 * GB
+            return hb16_first[:] if (g, a) == (0, 0) else hb16[:, g // 2, a, c : c + GB, :]
 
-        def quantize_a(mt, a):
-            nc.vector.quantize_mx(out=ha_w[:, mt, a, :].bitcast(FP8X4), scales=ha_s[:, mt, a, :], in_=ha16[:, mt, a].rearrange("p n t -> p (n t)"))
+        def scale_b(eng, g, a):
+            eng.tensor_tensor(rounded_b(g, a).unsqueeze(1), gel_b[g][:, a : a + 1], factor(eng, SLOTS, a, a + 1, GB), MULT)
+
+        ha16 = {}
+
+        def scale_a(eng, mt, a0, a1):
+            if mt not in ha16:
+                ha16[mt] = keep.tile([P, PASSES, NB, SLOTS], BF16, name="ha16_%d" % mt, tag=["", "first", "late", ""][mt], align_bytes=64)
+            eng.tensor_tensor(ha16[mt][:, a0:a1], gel_a[mt][:, a0:a1], factor(eng, 0, a0, a1, NB), MULT)
+
+        def quantize_b(a, c0, src):
+            cols = slice(c0, c0 + src.shape[1])
+            nc.vector.quantize_mx(out=hb_w[:, a, cols].bitcast(FP8X4), scales=hb_s[:, a, cols], in_=src.rearrange("p j t -> p (j t)"))
+
+        def quantize_a(mt):
+            nc.vector.quantize_mx(
+                out=ha_w[:, mt].rearrange("p a n -> p (a n)").bitcast(FP8X4),
+                scales=ha_s[:, mt].rearrange("p a n -> p (a n)"),
+                in_=ha16[mt][:].rearrange("p a n t -> p (a n t)"),
+            )
 
         banks = {}
 
@@ -185,28 +202,35 @@ def tile_list_biaff_gelu_exp_kernel(tc, tab_words, tab_scales, tab2_words, tab2_
                 nc.scalar.activation(res[:], y[:], ACT.Exp, scale=0.015625)
                 nc.sync.dma_start(out[mt * P : (mt + 1) * P, cols], res[:])
 
-        first_a = PASSES * J // GB
-        for u in range(first_a + AHEAD):
-            scale(u)
-        codes = keep.tile([P, PASSES * (J + M)], U32, name="codes", tag="codes", align_bytes=64)
-        hb_w = codes[:, : PASSES * J].rearrange("p (a j) -> p a j", a=PASSES)
-        ha_w = codes[:, PASSES * J :].rearrange("p (m a n) -> p m a n", a=PASSES, n=P)
+        ha_w = keep.tile([P, M // P, PASSES, P], U32, name="ha_w", align_bytes=64)
+        units = [(g, a) for g in range(J // GB) for a in range(PASSES)]
+        for u, (g, a) in enumerate(units):
+            scale_b(nc.gpsimd if u < 3 else nc.vector, g, a)
+        hb_w = keep.tile([P, PASSES, J], U32, name="hb_w", tag="codes", align_bytes=64)
+        quantize_b(1, 0, hb16[:, 0, 1])
+        quantize_b(0, GB, rounded_b(1, 0))
+        quantize_b(0, 0, rounded_b(0, 0))
+        scale_a(nc.vector, 0, 0, PASSES)
+        scale_a(nc.gpsimd, 1, 0, 1)
+        scale_a(nc.vector, 1, 1, 2)
+        for mt in range(2):
+            quantize_a(mt)
+            for a in range(PASSES):
+                scores(mt, 0, a)
         for a in range(PASSES):
-            quantize_b(a, 0)
-            quantize_a(0, a)
-            scores(0, 0, a)
-        for a in range(PASSES):
-            quantize_a(1, a)
-            scores(1, 0, a)
-        scale(first_a + AHEAD)
-        for a in range(PASSES):
-            quantize_b(a, 1)
-            scores(0, 1, a)
-            scores(1, 1, a)
-        for h in range(2 * PASSES, PASSES * M // P):
-            mt, a = divmod(h, PASSES)
-            if h + 1 < PASSES * M // P:
-                scale(first_a + h + 1)
-            quantize_a(mt, a)
-            for jh in range(J // 512):
-                scores(mt, jh, a)
+            quantize_b(a, 512, hb16[:, 1, a])
+        for mt in range(2):
+            for a in range(PASSES):
+                scores(mt, 1, a)
+        scale_a(nc.gpsimd, 2, 0, 1)
+        scale_a(nc.vector, 2, 1, 2)
+        scale_a(nc.vector, 3, 0, 1)
+        quantize_a(2)
+        scale_a(nc.vector, 3, 1, 2)
+        for jh in range(J // 512):
+            for a in range(PASSES):
+                scores(2, jh, a)
+        quantize_a(3)
+        for jh in range(J // 512):
+            for a in range(PASSES):
+                scores(3, jh, a)

@@ -40,7 +40,8 @@ def tile_list_biaff_gelu_exp_kernel(tc, tab_words, tab_scales, tab2_words, tab2_
         tb_s = plane("tb_s", T)
         ta_s = plane("ta_s", T)
         wa_s = keep.tile([P, R // 4], I32, name="wa_s", tag="late", align_bytes=64)
-        s_rows = keep.tile([P, 2 * P], F32, name="s_rows")
+        s_raw = keep.tile([2 * PASSES, 512], F32, name="s_raw")
+        s_rows = keep.tile([P, SLOTS, P], F32, name="s_rows")
         ident = keep.tile([P, P], F32, name="ident")
         nc.vector.memset(tb_s[:], 0)
         nc.vector.memset(wb_s[:], 0)
@@ -49,7 +50,7 @@ def tile_list_biaff_gelu_exp_kernel(tc, tab_words, tab_scales, tab2_words, tab2_
         nc.vector.memset(wa_s[:], 0)
 
         wb_w = keep.tile([P, R // 2], I32, name="wb_w", align_bytes=64)
-        tb_w = keep.tile([P, T], I32, name="tb_w", align_bytes=64)
+        tb_w = keep.tile([P, T], I32, name="tb_w", tag="table", align_bytes=64)
 
         def load_scales(dst, src, which=range(4), eng=nc.sync):
             rows = src[0].bitcast(I32)
@@ -59,24 +60,20 @@ def tile_list_biaff_gelu_exp_kernel(tc, tab_words, tab_scales, tab2_words, tab2_
         def load_words(dst, src):
             nc.sync.dma_start(dst[:], src[0].rearrange("p t i -> p (t i)").bitcast(I32))
 
-        def load_factor(first, vec):
-            nc.sync.dma_start(
-                s_rows[first : first + SLOTS, :].rearrange("t (b i) -> t b i", i=8),
-                vec.rearrange("(b t i) -> t b i", t=SLOTS, i=8),
-            )
+        def load_factor(side, vec):
+            nc.sync.dma_start(s_raw[side * PASSES : (side + 1) * PASSES, :], vec.rearrange("(a c) -> a c", a=PASSES))
 
         nc.sync.dma_start(wb_w[:], wb_words[0].bitcast(I32))
         nc.sync.dma_start(offs_b[:], offs2)
         load_scales(tb_s, tab2_scales)
         load_words(tb_w, tab2_words)
         load_factor(0, sa)
-        load_factor(SLOTS, sb)
+        load_factor(1, sb)
         load_scales(wb_s, wb_scales)
         warm = keep.tile([P, 1], F32, name="warm")
-        nc.scalar.activation(warm[32:64, :], s_rows[32:64, 0:1], ACT.Gelu_apprx_tanh)
+        nc.scalar.activation(warm[32:64, :], s_rows[32:64, 0, 0:1], ACT.Gelu_apprx_tanh)
         make_identity(nc, ident[:])
 
-        s_ps = psum.tile([P, PASSES, P], F32, name="s_ps")
 
         def permute(name, src, run):
             dst = keep.tile([P, src.shape[1]], I32, name=name, align_bytes=64)
@@ -97,26 +94,29 @@ def tile_list_biaff_gelu_exp_kernel(tc, tab_words, tab_scales, tab2_words, tab2_
             return gs
 
         ta_w = keep.tile([P, T], I32, name="ta_w", align_bytes=64)
-        wa_w = keep.tile([P, R], I32, name="wa_w", align_bytes=64)
+        wa_w = keep.tile([P, R], I32, name="wa_w", tag="middle", align_bytes=64)
         load_words(ta_w, tab_words)
         nc.sync.dma_start(offs_a[:], offs)
         load_scales(ta_s, tab_scales)
         load_words(wa_w, wa_words)
         load_scales(wa_s, wa_scales)
-        s_sb = keep.tile([P, PASSES, 2 * SLOTS], F32, name="s_sb")
-        for c in range(PASSES):
-            nc.tensor.transpose(s_ps[:, c, :], s_rows[:, c * P : (c + 1) * P], ident[:])
-        nc.scalar.copy(s_sb[:], s_ps[:, :, 0 : 2 * SLOTS])
+        nc.scalar.copy(
+            s_rows[0 : 2 * PASSES].rearrange("x t (q i) -> x t q i", i=8),
+            s_raw[:].rearrange("x (q t i) -> x t q i", t=SLOTS, i=8),
+        )
         GB = 256
         wb_wp = permute("wb_wp", wb_w, 4)
         gb_s = gather_scales("gb_s", tb_s, offs_b[:], J)
-        gb = [(gather_words("gb0_w", tb_w, offs_b[:, 0 : GB // 16], GB)[:], gb_s[:, :GB])]
+        gb_first = gather_words("gb_first", tb_w, offs_b[:, 0 : GB // 16], GB)
         wb_sp = permute("wb_sp", wb_s, 2)
-        gb.append((gather_words("gb1_w", tb_w, offs_b[:, GB // 16 :], J - GB, "early")[:], gb_s[:, GB:]))
+        gb_middle = gather_words("gb_middle", tb_w, offs_b[:, GB // 16 : 3 * GB // 16], 2 * GB, "early")
         ga_w = gather_words("ga_w", ta_w, offs_a[:], M)
         ga = (ga_w[:], gather_scales("ga_s", ta_s, offs_a[:], M)[:])
         wa_wp = permute("wa_wp", wa_w, 8)
         wa_sp = permute("wa_sp", wa_s, 2)
+        gb_last = gather_words("gb_last", tb_w, offs_b[:, 3 * GB // 16 :], GB, "late")
+        gb_w = [gb_first[:], gb_middle[:, :GB], gb_middle[:, GB:], gb_last[:]]
+        gb = [(gb_w[g], gb_s[:, g * GB : (g + 1) * GB]) for g in range(J // GB)]
 
         def wb_tile(a, t):
             c = (t * PASSES + a) * P
@@ -126,8 +126,8 @@ def tile_list_biaff_gelu_exp_kernel(tc, tab_words, tab_scales, tab2_words, tab2_
             c = (t * PASSES + a) * P
             return wa_wp[:, c : c + P].bitcast(FP8X4), wa_sp[:].bitcast(U8)[:, c : c + P]
 
-        def hidden(weights, a, g, c0, dst):
-            z = psum.tile([P, SLOTS, NB], F32, name="z", tag="z", bufs=3)
+        def hidden(weights, a, g, c0, dst, tag="z", bufs=3):
+            z = psum.tile([P, SLOTS, NB], F32, name="z", tag=tag, bufs=bufs)
             for t in range(SLOTS):
                 w, ws = weights(a, t)
                 nc.tensor.matmul_mx(
@@ -137,100 +137,112 @@ def tile_list_biaff_gelu_exp_kernel(tc, tab_words, tab_scales, tab2_words, tab2_
                 )
             nc.scalar.activation(dst, z[:].rearrange("p t n -> p n t"), ACT.Gelu_apprx_tanh)
 
-        hb_s = keep.tile([P, PASSES, J], U8, name="hb_s", align_bytes=64)
-        ha_s = keep.tile([P, M // P, PASSES, P], U8, name="ha_s", align_bytes=64)
-
-        hb16 = keep.tile([P, J // 512, PASSES, 512, SLOTS], BF16, name="hb16", tag="late", align_bytes=64)
-        hb16_first = keep.tile([P, GB, SLOTS], BF16, name="hb16_first", tag="first", align_bytes=64)
         gel_b = []
-        for g in range(J // GB):
-            gel = keep.tile([P, PASSES, GB, SLOTS], F32, name="gel_b%d" % g, tag="codes" if g == J // GB - 1 else "", align_bytes=64)
+        for g in range(3):
+            gel = keep.tile([P, PASSES, GB, SLOTS], F32, name="gel_b%d" % g)
             for a in range(PASSES):
                 for h in range(GB // NB):
-                    hidden(wb_tile, a, gb[min(g, 1)], max(g - 1, 0) * GB + h * NB, gel[:, a, h * NB : (h + 1) * NB, :])
+                    place = ("factors", 1) if (g, a, h) == (0, 0, 1) else ("z", 3)
+                    hidden(wb_tile, a, gb[g], h * NB, gel[:, a, h * NB : (h + 1) * NB, :], *place)
             gel_b.append(gel)
-        gel_a = []
+            if g == 0:
+                s_ps = psum.tile([P, P, SLOTS], F32, name="s_ps", tag="factors", bufs=1)
+                for t in range(SLOTS):
+                    nc.tensor.transpose(s_ps[:, :, t], s_rows[:, t, :], ident[:])
+                s_cols = s_ps[:, 0 : 2 * PASSES, :]
+                s_sb = keep.tile([P, 2 * PASSES, SLOTS], F32, name="s_sb", tag="middle", align_bytes=64)
+                nc.vector.tensor_copy(s_sb[:], s_cols)
+        gel_a = keep.tile([P, 3, PASSES, NB, SLOTS], F32, name="gel_a")
+        gel_a3 = [keep.tile([P, NB, SLOTS], F32, name="gel_a3_%d" % a, tag="codes" if a == 0 else "", align_bytes=64) for a in range(PASSES)]
         for mt in range(M // P):
-            gel = keep.tile([P, PASSES, NB, SLOTS], F32, name="gel_a%d" % mt)
             for a in range(PASSES):
-                hidden(wa_tile, a, ga, mt * NB, gel[:, a])
-            gel_a.append(gel)
-
-        def factor(eng, first, a0, a1, n):
-            src = s_sb if eng is nc.gpsimd else s_ps
-            return src[:, a0:a1, first : first + SLOTS].unsqueeze(2).to_broadcast([P, a1 - a0, n, SLOTS])
-
-        def rounded_b(g, a):
-            c = g % 2 * GB
-            return hb16_first[:] if (g, a) == (0, 0) else hb16[:, g // 2, a, c : c + GB, :]
-
-        def scale_b(eng, g, a):
-            eng.tensor_tensor(rounded_b(g, a).unsqueeze(1), gel_b[g][:, a : a + 1], factor(eng, SLOTS, a, a + 1, GB), MULT)
-
-        ha16 = {}
-
-        def scale_a(eng, mt, a0, a1):
-            if mt not in ha16:
-                ha16[mt] = keep.tile([P, PASSES, NB, SLOTS], BF16, name="ha16_%d" % mt, tag=["", "first", "late", ""][mt], align_bytes=64)
-            eng.tensor_tensor(ha16[mt][:, a0:a1], gel_a[mt][:, a0:a1], factor(eng, 0, a0, a1, NB), MULT)
-
-        def quantize_b(a, c0, src):
-            cols = slice(c0, c0 + src.shape[1])
-            nc.vector.quantize_mx(out=hb_w[:, a, cols].bitcast(FP8X4), scales=hb_s[:, a, cols], in_=src.rearrange("p j t -> p (j t)"))
-
-        def quantize_a(mt):
-            nc.vector.quantize_mx(
-                out=ha_w[:, mt].rearrange("p a n -> p (a n)").bitcast(FP8X4),
-                scales=ha_s[:, mt].rearrange("p a n -> p (a n)"),
-                in_=ha16[mt][:].rearrange("p a n t -> p (a n t)"),
-            )
-
-        banks = {}
-
-        def scores(mt, jh, a):
-            cols = slice(jh * 512, (jh + 1) * 512)
-            if a == 0:
-                banks[mt, jh] = psum.tile([P, 512], F32, name="y", tag="y", bufs=4)
-            y = banks[mt, jh]
-            nc.tensor.matmul_mx(
-                out=y[:], lhsT=ha_w[:, mt, a, :].bitcast(FP8X4), lhsT_scale=ha_s[:, mt, a, :],
-                rhs=hb_w[:, a, cols].bitcast(FP8X4), rhs_scale=hb_s[:, a, cols],
-                start=(a == 0), stop=(a == PASSES - 1),
-            )
-            if a == PASSES - 1:
-                res = keep.tile([P, 512], F32, name="res%d_%d" % (mt, jh))
-                nc.scalar.activation(res[:], y[:], ACT.Exp, scale=0.015625)
-                nc.sync.dma_start(out[mt * P : (mt + 1) * P, cols], res[:])
-
-        ha_w = keep.tile([P, M // P, PASSES, P], U32, name="ha_w", align_bytes=64)
-        units = [(g, a) for g in range(J // GB) for a in range(PASSES)]
-        for u, (g, a) in enumerate(units):
-            scale_b(nc.gpsimd if u < 3 else nc.vector, g, a)
-        hb_w = keep.tile([P, PASSES, J], U32, name="hb_w", tag="codes", align_bytes=64)
-        quantize_b(1, 0, hb16[:, 0, 1])
-        quantize_b(0, GB, rounded_b(1, 0))
-        quantize_b(0, 0, rounded_b(0, 0))
-        scale_a(nc.vector, 0, 0, PASSES)
-        scale_a(nc.gpsimd, 1, 0, 1)
-        scale_a(nc.vector, 1, 1, 2)
-        for mt in range(2):
-            quantize_a(mt)
+                hidden(wa_tile, a, ga, mt * NB, gel_a[:, mt, a] if mt < 3 else gel_a3[a][:])
+        gel_end = keep.tile([P, GB // NB, PASSES, NB, SLOTS], F32, name="gel_end")
+        for h in range(GB // NB):
             for a in range(PASSES):
-                scores(mt, 0, a)
+                hidden(wb_tile, a, gb[3], h * NB, gel_end[:, h, a])
+
+        def scale(eng, dst, src, side, a0):
+            factors = s_sb[:] if eng is nc.gpsimd else s_cols
+            count, n = src.shape[1], src.shape[2]
+            x = side * PASSES + a0
+            fac = factors[:, x : x + count, :].unsqueeze(2).to_broadcast([P, count, n, SLOTS])
+            eng.tensor_tensor(dst, src, fac, MULT)
+
+        def quantize(dst, src):
+            nc.vector.quantize_mx(out=dst[0].bitcast(FP8X4), scales=dst[1], in_=src)
+
+        hb16 = keep.tile([P, PASSES * 768, SLOTS], BF16, name="hb16", tag="table", align_bytes=64)
+        hb16_wide = hb16[:, : PASSES * 512].rearrange("p (a j) t -> p a j t", a=PASSES)
+        hb16_next = hb16[:, PASSES * 512 :].rearrange("p (a j) t -> p a j t", a=PASSES)
+        ha16 = keep.tile([P, M // P, PASSES, NB, SLOTS], BF16, name="ha16", align_bytes=64)
+        for g, a in [(0, 0), (1, 0), (0, 1), (1, 1)]:
+            eng = nc.vector if (g, a) == (1, 1) else nc.gpsimd
+            scale(eng, hb16_wide[:, a : a + 1, g * GB : (g + 1) * GB], gel_b[g][:, a : a + 1], 1, a)
         for a in range(PASSES):
-            quantize_b(a, 512, hb16[:, 1, a])
+            scale(nc.vector, hb16_next[:, a : a + 1], gel_b[2][:, a : a + 1], 1, a)
+        for mt in range(3):
+            scale(nc.vector, ha16[:, mt], gel_a[:, mt], 0, 0)
+        scale(nc.vector, ha16[:, 3, 0:1], gel_a3[0][:].unsqueeze(1), 0, 0)
+
+        codes = keep.tile([P, PASSES * (J + M)], U32, name="codes", tag="codes", align_bytes=64)
+        planes = keep.tile([P, PASSES * (J + M)], U8, name="planes", align_bytes=64)
+
+        def operand(c0, n):
+            return codes[:, c0 : c0 + n], planes[:, c0 : c0 + n]
+
+        def hb(j0, n, a):
+            return operand(PASSES * j0 + a * n, n)
+
+        def ha(mt, a):
+            return operand(PASSES * J + (PASSES * mt + a) * P, P)
+
+        def score(dst, mt, j0, n, a, start, stop):
+            nc.tensor.matmul_mx(
+                out=dst, lhsT=ha(mt, a)[0].bitcast(FP8X4), lhsT_scale=ha(mt, a)[1],
+                rhs=hb(j0, n, a)[0].bitcast(FP8X4), rhs_scale=hb(j0, n, a)[1],
+                start=start, stop=stop,
+            )
+
+        rows = out.rearrange("(m p) j -> p m j", p=P)
+
+        def finish(y, m0, j0, n):
+            res = keep.tile([P, 512], F32, name="res%d_%d" % (m0, j0))
+            nc.scalar.activation(res[:], y[:], ACT.Exp, scale=0.015625)
+            nc.sync.dma_start(rows[:, m0 : m0 + 512 // n, j0 : j0 + n], res[:].rearrange("p (m j) -> p m j", j=n))
+
+        def bank(m0, j0, n):
+            y = psum.tile([P, 512], F32, name="y", tag="y", bufs=4)
+            for i in range(512 // n):
+                for a in range(PASSES):
+                    score(y[:, i * n : (i + 1) * n], m0 + i, j0, n, a, a == 0, a == PASSES - 1)
+            finish(y, m0, j0, n)
+
+        quantize(operand(PASSES * J, 2 * PASSES * P), ha16[:, 0:2].rearrange("p m a n t -> p (m a n t)"))
+        quantize(hb(0, 512, 0), hb16_wide[:, 0].rearrange("p j t -> p (j t)"))
+        first = [psum.tile([P, 512], F32, name="y", tag="y", bufs=4) for mt in range(2)]
         for mt in range(2):
-            for a in range(PASSES):
-                scores(mt, 1, a)
-        scale_a(nc.gpsimd, 2, 0, 1)
-        scale_a(nc.vector, 2, 1, 2)
-        scale_a(nc.vector, 3, 0, 1)
-        quantize_a(2)
-        scale_a(nc.vector, 3, 1, 2)
-        for jh in range(J // 512):
-            for a in range(PASSES):
-                scores(2, jh, a)
-        quantize_a(3)
-        for jh in range(J // 512):
-            for a in range(PASSES):
-                scores(3, jh, a)
+            score(first[mt][:], mt, 0, 512, 0, True, False)
+        scale(nc.vector, ha16[:, 3, 1:2], gel_a3[1][:].unsqueeze(1), 0, 1)
+        quantize(hb(0, 512, 1), hb16_wide[:, 1].rearrange("p j t -> p (j t)"))
+        for mt in range(2):
+            score(first[mt][:], mt, 0, 512, 1, False, True)
+            finish(first[mt], mt, 0, 512)
+        quantize(operand(PASSES * J + 2 * PASSES * P, 2 * PASSES * P), ha16[:, 2:4].rearrange("p m a n t -> p (m a n t)"))
+        for mt in range(2, 4):
+            bank(mt, 0, 512)
+        quantize(operand(PASSES * 512, PASSES * GB), hb16_next.rearrange("p a j t -> p (a j t)"))
+        for m0 in range(0, 4, 2):
+            bank(m0, 512, GB)
+        hb16_end = keep.tile([P, GB // NB, PASSES, NB, SLOTS], BF16, name="hb16_end", tag="table", align_bytes=64)
+        scale(nc.vector, hb16_end[:, 0], gel_end[:, 0], 1, 0)
+        scale(nc.vector, hb16_end[:, 1, 0:1], gel_end[:, 1, 0:1], 1, 0)
+        quantize(operand(PASSES * 768, PASSES * NB), hb16_end[:, 0].rearrange("p a j t -> p (a j t)"))
+        bank(0, 768, NB)
+        scale(nc.vector, hb16_end[:, 1, 1:2], gel_end[:, 1, 1:2], 1, 1)
+        last = psum.tile([P, 512], F32, name="y", tag="y", bufs=4)
+        for a in range(PASSES):
+            quantize(hb(896, NB, a), hb16_end[:, 1, a].rearrange("p j t -> p (j t)"))
+            for mt in range(M // P):
+                score(last[:, mt * NB : (mt + 1) * NB], mt, 896, NB, a, (a, mt) == (0, 0), (a, mt) == (PASSES - 1, M // P - 1))
+        finish(last, 0, 896, NB)

@@ -20,6 +20,7 @@ MULT = mybir.AluOpType.mult
 P = 128
 SLOTS = 4
 PASSES = R // 512
+TILES = PASSES * SLOTS
 NB = 128
 
 
@@ -40,8 +41,7 @@ def tile_list_biaff_gelu_exp_kernel(tc, tab_words, tab_scales, tab2_words, tab2_
         tb_s = plane("tb_s", T)
         ta_s = plane("ta_s", T)
         wa_s = keep.tile([P, R // 4], I32, name="wa_s", tag="late", align_bytes=64)
-        s_raw = keep.tile([2 * PASSES, 512], F32, name="s_raw")
-        s_rows = keep.tile([P, SLOTS, P], F32, name="s_rows")
+        s_rows = keep.tile([P, P], F32, name="s_rows")
         ident = keep.tile([P, P], F32, name="ident")
         nc.vector.memset(tb_s[:], 0)
         nc.vector.memset(wb_s[:], 0)
@@ -61,25 +61,27 @@ def tile_list_biaff_gelu_exp_kernel(tc, tab_words, tab_scales, tab2_words, tab2_
             nc.sync.dma_start(dst[:], src[0].rearrange("p t i -> p (t i)").bitcast(I32))
 
         def load_factor(side, vec):
-            nc.sync.dma_start(s_raw[side * PASSES : (side + 1) * PASSES, :], vec.rearrange("(a c) -> a c", a=PASSES))
+            nc.sync.dma_start(
+                s_rows[side * TILES : (side + 1) * TILES, :].rearrange("u (q i) -> u q i", i=8),
+                vec.rearrange("(q u i) -> u q i", u=TILES, i=8),
+            )
 
         nc.sync.dma_start(wb_w[:], wb_words[0].bitcast(I32))
         nc.sync.dma_start(offs_b[:], offs2)
         load_scales(tb_s, tab2_scales)
         load_words(tb_w, tab2_words)
-        load_factor(0, sa)
-        load_factor(1, sb)
+        nc.sync.dma_start(offs_a[:], offs)
         load_scales(wb_s, wb_scales)
         warm = keep.tile([P, 1], F32, name="warm")
-        nc.scalar.activation(warm[32:64, :], s_rows[32:64, 0, 0:1], ACT.Gelu_apprx_tanh)
+        nc.scalar.activation(warm[32:64, :], s_rows[32:64, 0:1], ACT.Gelu_apprx_tanh)
         make_identity(nc, ident[:])
 
 
         def permute(name, src, run):
             dst = keep.tile([P, src.shape[1]], I32, name=name, align_bytes=64)
             nc.vector.tensor_copy(
-                dst[:].rearrange("p (t b i) -> p t b i", t=SLOTS, i=run),
-                src[:].rearrange("p (b t i) -> p t b i", t=SLOTS, i=run),
+                dst[:].rearrange("p (u q i) -> p u q i", u=TILES, i=run),
+                src[:].rearrange("p (q u i) -> p u q i", u=TILES, i=run),
             )
             return dst
 
@@ -94,16 +96,13 @@ def tile_list_biaff_gelu_exp_kernel(tc, tab_words, tab_scales, tab2_words, tab2_
             return gs
 
         ta_w = keep.tile([P, T], I32, name="ta_w", align_bytes=64)
-        wa_w = keep.tile([P, R], I32, name="wa_w", tag="middle", align_bytes=64)
+        wa_w = keep.tile([P, R], I32, name="wa_w", align_bytes=64)
         load_words(ta_w, tab_words)
-        nc.sync.dma_start(offs_a[:], offs)
+        load_factor(0, sa)
+        load_factor(1, sb)
         load_scales(ta_s, tab_scales)
         load_words(wa_w, wa_words)
         load_scales(wa_s, wa_scales)
-        nc.scalar.copy(
-            s_rows[0 : 2 * PASSES].rearrange("x t (q i) -> x t q i", i=8),
-            s_raw[:].rearrange("x (q t i) -> x t q i", t=SLOTS, i=8),
-        )
         GB = 256
         wb_wp = permute("wb_wp", wb_w, 4)
         gb_s = gather_scales("gb_s", tb_s, offs_b[:], J)
@@ -119,15 +118,15 @@ def tile_list_biaff_gelu_exp_kernel(tc, tab_words, tab_scales, tab2_words, tab2_
         gb = [(gb_w[g], gb_s[:, g * GB : (g + 1) * GB]) for g in range(J // GB)]
 
         def wb_tile(a, t):
-            c = (t * PASSES + a) * P
+            c = (a * SLOTS + t) * P
             return wb_wp[:].bitcast(U8)[:, 2 * c : 2 * c + 2 * P].bitcast(FP4X4), wb_sp[:].bitcast(U8)[:, c : c + P]
 
         def wa_tile(a, t):
-            c = (t * PASSES + a) * P
+            c = (a * SLOTS + t) * P
             return wa_wp[:, c : c + P].bitcast(FP8X4), wa_sp[:].bitcast(U8)[:, c : c + P]
 
-        def hidden(weights, a, g, c0, dst, tag="z", bufs=3):
-            z = psum.tile([P, SLOTS, NB], F32, name="z", tag=tag, bufs=bufs)
+        def hidden(weights, a, g, c0, dst):
+            z = psum.tile([P, SLOTS, NB], F32, name="z", tag="z", bufs=3)
             for t in range(SLOTS):
                 w, ws = weights(a, t)
                 nc.tensor.matmul_mx(
@@ -142,16 +141,14 @@ def tile_list_biaff_gelu_exp_kernel(tc, tab_words, tab_scales, tab2_words, tab2_
             gel = keep.tile([P, PASSES, GB, SLOTS], F32, name="gel_b%d" % g)
             for a in range(PASSES):
                 for h in range(GB // NB):
-                    place = ("factors", 1) if (g, a, h) == (0, 0, 1) else ("z", 3)
-                    hidden(wb_tile, a, gb[g], h * NB, gel[:, a, h * NB : (h + 1) * NB, :], *place)
+                    hidden(wb_tile, a, gb[g], h * NB, gel[:, a, h * NB : (h + 1) * NB, :])
             gel_b.append(gel)
             if g == 0:
-                s_ps = psum.tile([P, P, SLOTS], F32, name="s_ps", tag="factors", bufs=1)
-                for t in range(SLOTS):
-                    nc.tensor.transpose(s_ps[:, :, t], s_rows[:, t, :], ident[:])
-                s_cols = s_ps[:, 0 : 2 * PASSES, :]
-                s_sb = keep.tile([P, 2 * PASSES, SLOTS], F32, name="s_sb", tag="middle", align_bytes=64)
-                nc.vector.tensor_copy(s_sb[:], s_cols)
+                s_ps = psum.tile([P, P], F32, name="s_ps")
+                nc.tensor.transpose(s_ps[:], s_rows[:], ident[:])
+                s_cols = s_ps[:, 0 : 2 * TILES].rearrange("p (x t) -> p x t", t=SLOTS)
+                s_sb = keep.tile([P, 2 * PASSES, SLOTS], F32, name="s_sb")
+                nc.scalar.copy(s_sb[:], s_cols)
         gel_a = keep.tile([P, 3, PASSES, NB, SLOTS], F32, name="gel_a")
         gel_a3 = [keep.tile([P, NB, SLOTS], F32, name="gel_a3_%d" % a, tag="codes" if a == 0 else "", align_bytes=64) for a in range(PASSES)]
         for mt in range(M // P):

@@ -158,6 +158,10 @@ def tile_list_biaff_gelu_exp_kernel(tc, tab_words, tab_scales, tab2_words, tab2_
         for h in range(GB // NB):
             for a in range(PASSES):
                 hidden(wb_tile, a, gb[3], h * NB, gel_end[:, h, a])
+        for i in range(2):
+            idle = psum.tile([P, M], F32, name="idle", tag="z", bufs=3)
+            w, ws = wa_tile(0, i)
+            nc.tensor.matmul_mx(out=idle[:], lhsT=w, lhsT_scale=ws, rhs=ga[0].bitcast(FP8X4), rhs_scale=ga[1], start=True, stop=True)
 
         def scale(eng, dst, src, side, a0):
             factors = s_sb[:] if eng is nc.gpsimd else s_cols

@@ -48,9 +48,10 @@ def tile_list_biaff_gelu_exp_kernel(tc, tab_words, tab_scales, tab2_words, tab2_
         nc.vector.memset(s_rows[:], 0.0)
         nc.vector.memset(ta_s[:], 0)
         nc.vector.memset(wa_s[:], 0)
+        nc.vector.memset(ident[:], 0.0)
 
         wb_w = keep.tile([P, R // 2], I32, name="wb_w", align_bytes=64)
-        tb_w = keep.tile([P, T], I32, name="tb_w", tag="table", align_bytes=64)
+        tb_w = keep.tile([P, T], I32, name="tb_w", align_bytes=64)
 
         def load_scales(dst, src, which=range(4), eng=nc.sync):
             rows = src[0].bitcast(I32)
@@ -74,7 +75,7 @@ def tile_list_biaff_gelu_exp_kernel(tc, tab_words, tab_scales, tab2_words, tab2_
         load_scales(wb_s, wb_scales)
         warm = keep.tile([P, 1], F32, name="warm")
         nc.scalar.activation(warm[32:64, :], s_rows[32:64, 0:1], ACT.Gelu_apprx_tanh)
-        make_identity(nc, ident[:])
+        make_identity(nc, ident[:], nomemset=True)
 
 
         def permute(name, src, run):
@@ -90,8 +91,8 @@ def tile_list_biaff_gelu_exp_kernel(tc, tab_words, tab_scales, tab2_words, tab2_
             nc.vector.tensor_copy(gw[:], words[:].bitcast(U32).indirect(offsets))
             return gw
 
-        def gather_scales(name, scales, offsets, n):
-            gs = keep.tile([P, n], U8, name=name, align_bytes=64)
+        def gather_scales(name, scales, offsets, n, tag=""):
+            gs = keep.tile([P, n], U8, name=name, tag=tag, align_bytes=64)
             nc.vector.tensor_copy(gs[:], scales[:].bitcast(U8).indirect(offsets))
             return gs
 
@@ -105,17 +106,20 @@ def tile_list_biaff_gelu_exp_kernel(tc, tab_words, tab_scales, tab2_words, tab2_
         load_scales(wa_s, wa_scales)
         GB = 256
         wb_wp = permute("wb_wp", wb_w, 4)
-        gb_s = gather_scales("gb_s", tb_s, offs_b[:], J)
+        gb_s = gather_scales("gb_s", tb_s, offs_b[:, 0 : 3 * GB // 16], 3 * GB)
+        gb_s_end = gather_scales("gb_s_end", tb_s, offs_b[:, 3 * GB // 16 :], GB, "rounded")
         gb_first = gather_words("gb_first", tb_w, offs_b[:, 0 : GB // 16], GB)
         wb_sp = permute("wb_sp", wb_s, 2)
-        gb_middle = gather_words("gb_middle", tb_w, offs_b[:, GB // 16 : 3 * GB // 16], 2 * GB, "early")
+        gb_rest = gather_words("gb_rest", tb_w, offs_b[:, GB // 16 :], J - GB, "early")
         ga_w = gather_words("ga_w", ta_w, offs_a[:], M)
         ga = (ga_w[:], gather_scales("ga_s", ta_s, offs_a[:], M)[:])
         wa_wp = permute("wa_wp", wa_w, 8)
         wa_sp = permute("wa_sp", wa_s, 2)
-        gb_last = gather_words("gb_last", tb_w, offs_b[:, 3 * GB // 16 :], GB, "late")
-        gb_w = [gb_first[:], gb_middle[:, :GB], gb_middle[:, GB:], gb_last[:]]
-        gb = [(gb_w[g], gb_s[:, g * GB : (g + 1) * GB]) for g in range(J // GB)]
+        gb_s_held = keep.tile([P, GB // 4], I32, name="gb_s_held", tag="late", align_bytes=64)
+        nc.vector.tensor_copy(gb_s_held[:], gb_s_end[:].bitcast(I32))
+        gb = [(gb_first[:], gb_s[:, :GB])]
+        gb.extend([(gb_rest[:, g * GB : (g + 1) * GB], gb_s[:, (g + 1) * GB : (g + 2) * GB]) for g in range(2)])
+        gb.append((gb_rest[:, 2 * GB :], gb_s_held[:].bitcast(U8)))
 
         def wb_tile(a, t):
             c = (a * SLOTS + t) * P
@@ -173,7 +177,7 @@ def tile_list_biaff_gelu_exp_kernel(tc, tab_words, tab_scales, tab2_words, tab2_
         def quantize(dst, src):
             nc.vector.quantize_mx(out=dst[0].bitcast(FP8X4), scales=dst[1], in_=src)
 
-        hb16 = keep.tile([P, PASSES * 768, SLOTS], BF16, name="hb16", tag="table", align_bytes=64)
+        hb16 = keep.tile([P, PASSES * 768, SLOTS], BF16, name="hb16", tag="rounded", align_bytes=64)
         hb16_wide = hb16[:, : PASSES * 512].rearrange("p (a j) t -> p a j t", a=PASSES)
         hb16_next = hb16[:, PASSES * 512 :].rearrange("p (a j) t -> p a j t", a=PASSES)
         ha16 = keep.tile([P, M // P, PASSES, NB, SLOTS], BF16, name="ha16", align_bytes=64)
@@ -207,43 +211,50 @@ def tile_list_biaff_gelu_exp_kernel(tc, tab_words, tab_scales, tab2_words, tab2_
 
         rows = out.rearrange("(m p) j -> p m j", p=P)
 
-        def finish(y, m0, j0, n):
-            res = keep.tile([P, 512], F32, name="res%d_%d" % (m0, j0))
-            nc.scalar.activation(res[:], y[:], ACT.Exp, scale=0.015625)
-            nc.sync.dma_start(rows[:, m0 : m0 + 512 // n, j0 : j0 + n], res[:].rearrange("p (m j) -> p m j", j=n))
+        def finish(y, m0, count, j0, n):
+            res = keep.tile([P, count * n], F32, name="res%d_%d" % (m0, j0))
+            nc.scalar.activation(res[:], y, ACT.Exp, scale=0.015625)
+            nc.sync.dma_start(rows[:, m0 : m0 + count, j0 : j0 + n], res[:].rearrange("p (m j) -> p m j", j=n))
 
-        def bank(m0, j0, n):
-            y = psum.tile([P, 512], F32, name="y", tag="y", bufs=4)
-            for i in range(512 // n):
-                for a in range(PASSES):
-                    score(y[:, i * n : (i + 1) * n], m0 + i, j0, n, a, a == 0, a == PASSES - 1)
-            finish(y, m0, j0, n)
+        def new_bank():
+            return psum.tile([P, 512], F32, name="y", tag="y", bufs=4)
 
         quantize(operand(PASSES * J, 2 * PASSES * P), ha16[:, 0:2].rearrange("p m a n t -> p (m a n t)"))
         quantize(hb(0, 512, 0), hb16_wide[:, 0].rearrange("p j t -> p (j t)"))
-        first = [psum.tile([P, 512], F32, name="y", tag="y", bufs=4) for mt in range(2)]
+        first = [new_bank() for mt in range(2)]
         for mt in range(2):
             score(first[mt][:], mt, 0, 512, 0, True, False)
         scale(nc.vector, ha16[:, 3, 1:2], gel_a3[1][:].unsqueeze(1), 0, 1)
         quantize(hb(0, 512, 1), hb16_wide[:, 1].rearrange("p j t -> p (j t)"))
         for mt in range(2):
             score(first[mt][:], mt, 0, 512, 1, False, True)
-            finish(first[mt], mt, 0, 512)
+            finish(first[mt][:], mt, 1, 0, 512)
         quantize(operand(PASSES * J + 2 * PASSES * P, 2 * PASSES * P), ha16[:, 2:4].rearrange("p m a n t -> p (m a n t)"))
         for mt in range(2, 4):
-            bank(mt, 0, 512)
+            y = new_bank()
+            for a in range(PASSES):
+                score(y[:], mt, 0, 512, a, a == 0, a == PASSES - 1)
+            finish(y[:], mt, 1, 0, 512)
         quantize(operand(PASSES * 512, PASSES * GB), hb16_next.rearrange("p a j t -> p (a j t)"))
-        for m0 in range(0, 4, 2):
-            bank(m0, 512, GB)
-        hb16_end = keep.tile([P, GB // NB, PASSES, NB, SLOTS], BF16, name="hb16_end", tag="table", align_bytes=64)
+        for m0 in range(0, M // P, 2):
+            y = new_bank()
+            for i in range(2):
+                for a in range(PASSES):
+                    score(y[:, i * GB : (i + 1) * GB], m0 + i, 512, GB, a, a == 0, a == PASSES - 1)
+            finish(y[:], m0, 2, 512, GB)
+        hb16_end = keep.tile([P, GB // NB, PASSES, NB, SLOTS], BF16, name="hb16_end", tag="rounded", align_bytes=64)
         scale(nc.vector, hb16_end[:, 0], gel_end[:, 0], 1, 0)
         scale(nc.vector, hb16_end[:, 1, 0:1], gel_end[:, 1, 0:1], 1, 0)
         quantize(operand(PASSES * 768, PASSES * NB), hb16_end[:, 0].rearrange("p a j t -> p (a j t)"))
-        bank(0, 768, NB)
+        y = new_bank()
+        for mt in range(M // P):
+            for a in range(PASSES):
+                score(y[:, mt * NB : (mt + 1) * NB], mt, 768, NB, a, a == 0, a == PASSES - 1)
+        finish(y[:], 0, M // P, 768, NB)
         scale(nc.vector, hb16_end[:, 1, 1:2], gel_end[:, 1, 1:2], 1, 1)
-        last = psum.tile([P, 512], F32, name="y", tag="y", bufs=4)
+        last = new_bank()
         for a in range(PASSES):
             quantize(hb(896, NB, a), hb16_end[:, 1, a].rearrange("p j t -> p (j t)"))
             for mt in range(M // P):
                 score(last[:, mt * NB : (mt + 1) * NB], mt, 896, NB, a, (a, mt) == (0, 0), (a, mt) == (PASSES - 1, M // P - 1))
-        finish(last, 0, 896, NB)
+        finish(last[:], 0, M // P, 896, NB)

@@ -19,9 +19,19 @@ MULT = mybir.AluOpType.mult
 
 P = 128
 SLOTS = 4
+RUN = 8
 PASSES = R // 512
 TILES = PASSES * SLOTS
-NB = 128
+BANK = 512
+NB = BANK // SLOTS
+GB = 256
+GROUPS = J // GB
+A_TILES = M // P
+PER_COLUMN = 16
+Z_BANKS = 3
+Y_BANKS = 4
+KEEP_WARM = 2
+A_SIDE, B_SIDE = 0, 1
 
 
 def tile_list_biaff_gelu_exp_kernel(tc, tab_words, tab_scales, tab2_words, tab2_scales, wa_words, wa_scales, wb_words, wb_scales, sa, sb, offs, offs2, out):
@@ -31,16 +41,13 @@ def tile_list_biaff_gelu_exp_kernel(tc, tab_words, tab_scales, tab2_words, tab2_
         keep = ctx.enter_context(tc.tile_pool(name="keep", bufs=1))
         psum = ctx.enter_context(tc.psum_pool(name="psum", bufs=1))
 
-        offs_a = lists.tile([P, M // 16], U16, name="offs_a")
-        offs_b = lists.tile([P, J // 16], U16, name="offs_b")
+        offs_a = lists.tile([P, M // PER_COLUMN], U16, name="offs_a")
+        offs_b = lists.tile([P, J // PER_COLUMN], U16, name="offs_b")
 
-        def plane(name, cols):
-            return keep.tile([P, cols // 4], I32, name=name, align_bytes=64)
-
-        wb_s = keep.tile([P, R // 4], I32, name="wb_s", tag="early", align_bytes=64)
-        tb_s = plane("tb_s", T)
-        ta_s = plane("ta_s", T)
-        wa_s = keep.tile([P, R // 4], I32, name="wa_s", tag="late", align_bytes=64)
+        wb_s = keep.tile([P, R // 4], I32, name="wb_s", tag="after_wb_scales", align_bytes=64)
+        tb_s = keep.tile([P, T // 4], I32, name="tb_s", align_bytes=64)
+        ta_s = keep.tile([P, T // 4], I32, name="ta_s", align_bytes=64)
+        wa_s = keep.tile([P, R // 4], I32, name="wa_s", tag="after_wa_scales", align_bytes=64)
         s_rows = keep.tile([P, P], F32, name="s_rows")
         ident = keep.tile([P, P], F32, name="ident")
         nc.vector.memset(tb_s[:], 0)
@@ -49,36 +56,40 @@ def tile_list_biaff_gelu_exp_kernel(tc, tab_words, tab_scales, tab2_words, tab2_
         nc.vector.memset(ta_s[:], 0)
         nc.vector.memset(wa_s[:], 0)
         nc.vector.memset(ident[:], 0.0)
+        make_identity(nc, ident[:], nomemset=True)
 
-        wb_w = keep.tile([P, R // 2], I32, name="wb_w", align_bytes=64)
-        tb_w = keep.tile([P, T], I32, name="tb_w", align_bytes=64)
-
-        def load_scales(dst, src, which=range(4), eng=nc.sync):
+        def load_scales(dst, src):
             rows = src[0].bitcast(I32)
-            for q in which:
-                eng.dma_start(dst[32 * q : 32 * q + 4, :], rows[4 * q : 4 * q + 4, :])
+            for quadrant in range(4):
+                nc.sync.dma_start(dst[32 * quadrant : 32 * quadrant + 4, :], rows[4 * quadrant : 4 * quadrant + 4, :])
 
         def load_words(dst, src):
-            nc.sync.dma_start(dst[:], src[0].rearrange("p t i -> p (t i)").bitcast(I32))
+            nc.sync.dma_start(dst[:], src[0].rearrange("p c i -> p (c i)").bitcast(I32))
 
         def load_factor(side, vec):
             nc.sync.dma_start(
-                s_rows[side * TILES : (side + 1) * TILES, :].rearrange("u (q i) -> u q i", i=8),
-                vec.rearrange("(q u i) -> u q i", u=TILES, i=8),
+                s_rows[side * TILES : (side + 1) * TILES, :].rearrange("u (q i) -> u q i", i=RUN),
+                vec.rearrange("(q u i) -> u q i", u=TILES, i=RUN),
             )
 
+        wb_w = keep.tile([P, R // 2], I32, name="wb_w", align_bytes=64)
+        tb_w = keep.tile([P, T], I32, name="tb_w", align_bytes=64)
+        ta_w = keep.tile([P, T], I32, name="ta_w", align_bytes=64)
+        wa_w = keep.tile([P, R], I32, name="wa_w", align_bytes=64)
         nc.sync.dma_start(wb_w[:], wb_words[0].bitcast(I32))
         nc.sync.dma_start(offs_b[:], offs2)
         load_scales(tb_s, tab2_scales)
         load_words(tb_w, tab2_words)
-        nc.sync.dma_start(offs_a[:], offs)
         load_scales(wb_s, wb_scales)
-        warm = keep.tile([P, 1], F32, name="warm")
-        nc.scalar.activation(warm[32:64, :], s_rows[32:64, 0:1], ACT.Gelu_apprx_tanh)
-        make_identity(nc, ident[:], nomemset=True)
+        nc.sync.dma_start(offs_a[:], offs)
+        load_words(ta_w, tab_words)
+        load_factor(A_SIDE, sa)
+        load_factor(B_SIDE, sb)
+        load_scales(ta_s, tab_scales)
+        load_words(wa_w, wa_words)
+        load_scales(wa_s, wa_scales)
 
-
-        def permute(name, src, run):
+        def reorder(name, src, run):
             dst = keep.tile([P, src.shape[1]], I32, name=name, align_bytes=64)
             nc.vector.tensor_copy(
                 dst[:].rearrange("p (u q i) -> p u q i", u=TILES, i=run),
@@ -86,175 +97,164 @@ def tile_list_biaff_gelu_exp_kernel(tc, tab_words, tab_scales, tab2_words, tab2_
             )
             return dst
 
-        def gather_words(name, words, offsets, n, tag=""):
-            gw = keep.tile([P, n], U32, name=name, tag=tag, align_bytes=64)
-            nc.vector.tensor_copy(gw[:], words[:].bitcast(U32).indirect(offsets))
-            return gw
+        def gather(name, dtype, table, offsets, n0, n1, tag=""):
+            dst = keep.tile([P, n1 - n0], dtype, name=name, tag=tag, align_bytes=64)
+            nc.vector.tensor_copy(dst[:], table[:].bitcast(dtype).indirect(offsets[:, n0 // PER_COLUMN : n1 // PER_COLUMN]))
+            return dst
 
-        def gather_scales(name, scales, offsets, n, tag=""):
-            gs = keep.tile([P, n], U8, name=name, tag=tag, align_bytes=64)
-            nc.vector.tensor_copy(gs[:], scales[:].bitcast(U8).indirect(offsets))
-            return gs
+        last_group = J - GB
+        wb_wr = reorder("wb_wr", wb_w, RUN // 2)
+        gb_s = gather("gb_s", U8, tb_s, offs_b, 0, last_group)
+        gb_s_last = gather("gb_s_last", U8, tb_s, offs_b, last_group, J, "after_gathers")
+        gb_first = gather("gb_first", U32, tb_w, offs_b, 0, GB)
+        wb_sr = reorder("wb_sr", wb_s, RUN // 4)
+        gb_rest = gather("gb_rest", U32, tb_w, offs_b, GB, J, "after_wb_scales")
+        ga_w = gather("ga_w", U32, ta_w, offs_a, 0, M)
+        ga_s = gather("ga_s", U8, ta_s, offs_a, 0, M)
+        wa_wr = reorder("wa_wr", wa_w, RUN)
+        wa_sr = reorder("wa_sr", wa_s, RUN // 4)
+        gb_s_held = keep.tile([P, GB // 4], I32, name="gb_s_held", tag="after_wa_scales", align_bytes=64)
+        nc.vector.tensor_copy(gb_s_held[:], gb_s_last[:].bitcast(I32))
 
-        ta_w = keep.tile([P, T], I32, name="ta_w", align_bytes=64)
-        wa_w = keep.tile([P, R], I32, name="wa_w", align_bytes=64)
-        load_words(ta_w, tab_words)
-        load_factor(0, sa)
-        load_factor(1, sb)
-        load_scales(ta_s, tab_scales)
-        load_words(wa_w, wa_words)
-        load_scales(wa_s, wa_scales)
-        GB = 256
-        wb_wp = permute("wb_wp", wb_w, 4)
-        gb_s = gather_scales("gb_s", tb_s, offs_b[:, 0 : 3 * GB // 16], 3 * GB)
-        gb_s_end = gather_scales("gb_s_end", tb_s, offs_b[:, 3 * GB // 16 :], GB, "rounded")
-        gb_first = gather_words("gb_first", tb_w, offs_b[:, 0 : GB // 16], GB)
-        wb_sp = permute("wb_sp", wb_s, 2)
-        gb_rest = gather_words("gb_rest", tb_w, offs_b[:, GB // 16 :], J - GB, "early")
-        ga_w = gather_words("ga_w", ta_w, offs_a[:], M)
-        ga = (ga_w[:], gather_scales("ga_s", ta_s, offs_a[:], M)[:])
-        wa_wp = permute("wa_wp", wa_w, 8)
-        wa_sp = permute("wa_sp", wa_s, 2)
-        gb_s_held = keep.tile([P, GB // 4], I32, name="gb_s_held", tag="late", align_bytes=64)
-        nc.vector.tensor_copy(gb_s_held[:], gb_s_end[:].bitcast(I32))
+        ga = (ga_w[:], ga_s[:])
         gb = [(gb_first[:], gb_s[:, :GB])]
-        gb.extend([(gb_rest[:, g * GB : (g + 1) * GB], gb_s[:, (g + 1) * GB : (g + 2) * GB]) for g in range(2)])
-        gb.append((gb_rest[:, 2 * GB :], gb_s_held[:].bitcast(U8)))
+        gb.extend([(gb_rest[:, (g - 1) * GB : g * GB], gb_s[:, g * GB : (g + 1) * GB]) for g in range(1, GROUPS - 1)])
+        gb.append((gb_rest[:, last_group - GB :], gb_s_held[:].bitcast(U8)))
 
-        def wb_tile(a, t):
-            c = (a * SLOTS + t) * P
-            return wb_wp[:].bitcast(U8)[:, 2 * c : 2 * c + 2 * P].bitcast(FP4X4), wb_sp[:].bitcast(U8)[:, c : c + P]
+        def wb_tile(ps, t):
+            c = (ps * SLOTS + t) * P
+            return wb_wr[:].bitcast(U8)[:, 2 * c : 2 * c + 2 * P].bitcast(FP4X4), wb_sr[:].bitcast(U8)[:, c : c + P]
 
-        def wa_tile(a, t):
-            c = (a * SLOTS + t) * P
-            return wa_wp[:, c : c + P].bitcast(FP8X4), wa_sp[:].bitcast(U8)[:, c : c + P]
+        def wa_tile(ps, t):
+            c = (ps * SLOTS + t) * P
+            return wa_wr[:, c : c + P].bitcast(FP8X4), wa_sr[:].bitcast(U8)[:, c : c + P]
 
-        def hidden(weights, a, g, c0, dst):
-            z = psum.tile([P, SLOTS, NB], F32, name="z", tag="z", bufs=3)
+        def hidden(weights, ps, gathered, c0, dst):
+            z = psum.tile([P, SLOTS, NB], F32, name="z", tag="z", bufs=Z_BANKS)
             for t in range(SLOTS):
-                w, ws = weights(a, t)
+                w, ws = weights(ps, t)
                 nc.tensor.matmul_mx(
                     out=z[:, t, :], lhsT=w, lhsT_scale=ws,
-                    rhs=g[0][:, c0 : c0 + NB].bitcast(FP8X4), rhs_scale=g[1][:, c0 : c0 + NB],
+                    rhs=gathered[0][:, c0 : c0 + NB].bitcast(FP8X4), rhs_scale=gathered[1][:, c0 : c0 + NB],
                     start=True, stop=True,
                 )
             nc.scalar.activation(dst, z[:].rearrange("p t n -> p n t"), ACT.Gelu_apprx_tanh)
 
-        gel_b = []
-        for g in range(3):
-            gel = keep.tile([P, PASSES, GB, SLOTS], F32, name="gel_b%d" % g)
-            for a in range(PASSES):
-                for h in range(GB // NB):
-                    hidden(wb_tile, a, gb[g], h * NB, gel[:, a, h * NB : (h + 1) * NB, :])
-            gel_b.append(gel)
-            if g == 0:
-                s_ps = psum.tile([P, P], F32, name="s_ps")
-                nc.tensor.transpose(s_ps[:], s_rows[:], ident[:])
-                s_cols = s_ps[:, 0 : 2 * TILES].rearrange("p (x t) -> p x t", t=SLOTS)
-                s_sb = keep.tile([P, 2 * PASSES, SLOTS], F32, name="s_sb")
-                nc.scalar.copy(s_sb[:], s_cols)
-        gel_a = keep.tile([P, 3, PASSES, NB, SLOTS], F32, name="gel_a")
-        gel_a3 = [keep.tile([P, NB, SLOTS], F32, name="gel_a3_%d" % a, tag="codes" if a == 0 else "", align_bytes=64) for a in range(PASSES)]
-        for mt in range(M // P):
-            for a in range(PASSES):
-                hidden(wa_tile, a, ga, mt * NB, gel_a[:, mt, a] if mt < 3 else gel_a3[a][:])
-        gel_end = keep.tile([P, GB // NB, PASSES, NB, SLOTS], F32, name="gel_end")
-        for h in range(GB // NB):
-            for a in range(PASSES):
-                hidden(wb_tile, a, gb[3], h * NB, gel_end[:, h, a])
-        for i in range(2):
-            idle = psum.tile([P, M], F32, name="idle", tag="z", bufs=3)
-            w, ws = wa_tile(0, i)
-            nc.tensor.matmul_mx(out=idle[:], lhsT=w, lhsT_scale=ws, rhs=ga[0].bitcast(FP8X4), rhs_scale=ga[1], start=True, stop=True)
+        s_psum = psum.tile([P, P], F32, name="s_psum")
+        nc.tensor.transpose(s_psum[:], s_rows[:], ident[:])
+        s_cols = s_psum[:, 0 : 2 * TILES].rearrange("p (x t) -> p x t", t=SLOTS)
+        s_sb = keep.tile([P, 2 * PASSES, SLOTS], F32, name="s_sb")
+        nc.scalar.copy(s_sb[:], s_cols)
 
-        def scale(eng, dst, src, side, a0):
+        gel_b = []
+        for g in range(GROUPS - 1):
+            gel = keep.tile([P, PASSES, GB, SLOTS], F32, name="gel_b%d" % g)
+            for ps in range(PASSES):
+                for h in range(GB // NB):
+                    hidden(wb_tile, ps, gb[g], h * NB, gel[:, ps, h * NB : (h + 1) * NB, :])
+            gel_b.append(gel)
+
+        end = A_TILES - 1
+        gel_a = keep.tile([P, end, PASSES, NB, SLOTS], F32, name="gel_a")
+        gel_a_end = [keep.tile([P, 1, NB, SLOTS], F32, name="gel_a_end%d" % ps, tag="after_multiplies" if ps == 0 else "", align_bytes=64) for ps in range(PASSES)]
+        for mt in range(A_TILES):
+            for ps in range(PASSES):
+                hidden(wa_tile, ps, ga, mt * NB, gel_a[:, mt, ps] if mt < end else gel_a_end[ps][:, 0])
+        gel_last = keep.tile([P, GB // NB, PASSES, NB, SLOTS], F32, name="gel_last")
+        for h in range(GB // NB):
+            for ps in range(PASSES):
+                hidden(wb_tile, ps, gb[GROUPS - 1], h * NB, gel_last[:, h, ps])
+
+        for t in range(KEEP_WARM):
+            unread = psum.tile([P, M], F32, name="unread", tag="z", bufs=Z_BANKS)
+            w, ws = wa_tile(0, t)
+            nc.tensor.matmul_mx(out=unread[:], lhsT=w, lhsT_scale=ws, rhs=ga[0].bitcast(FP8X4), rhs_scale=ga[1], start=True, stop=True)
+
+        def scale(eng, dst, src, side, ps0):
             factors = s_sb[:] if eng is nc.gpsimd else s_cols
             count, n = src.shape[1], src.shape[2]
-            x = side * PASSES + a0
-            fac = factors[:, x : x + count, :].unsqueeze(2).to_broadcast([P, count, n, SLOTS])
-            eng.tensor_tensor(dst, src, fac, MULT)
+            x = side * PASSES + ps0
+            eng.tensor_tensor(dst, src, factors[:, x : x + count, :].unsqueeze(2).to_broadcast([P, count, n, SLOTS]), MULT)
 
-        def quantize(dst, src):
-            nc.vector.quantize_mx(out=dst[0].bitcast(FP8X4), scales=dst[1], in_=src)
+        hb16 = keep.tile([P, PASSES * last_group, SLOTS], BF16, name="hb16", tag="after_gathers", align_bytes=64)
+        hb16_wide = hb16[:, : PASSES * BANK].rearrange("p (ps j) t -> p ps j t", ps=PASSES)
+        hb16_next = hb16[:, PASSES * BANK :].rearrange("p (ps j) t -> p ps j t", ps=PASSES)
+        ha16 = keep.tile([P, A_TILES, PASSES, NB, SLOTS], BF16, name="ha16", align_bytes=64)
+        pieces = [(g, ps) for ps in range(PASSES) for g in range(BANK // GB)]
+        for g, ps in pieces:
+            eng = nc.vector if (g, ps) == pieces[-1] else nc.gpsimd
+            scale(eng, hb16_wide[:, ps : ps + 1, g * GB : (g + 1) * GB], gel_b[g][:, ps : ps + 1], B_SIDE, ps)
+        for ps in range(PASSES):
+            scale(nc.vector, hb16_next[:, ps : ps + 1], gel_b[BANK // GB][:, ps : ps + 1], B_SIDE, ps)
+        for mt in range(end):
+            scale(nc.vector, ha16[:, mt], gel_a[:, mt], A_SIDE, 0)
+        scale(nc.vector, ha16[:, end, 0:1], gel_a_end[0][:], A_SIDE, 0)
 
-        hb16 = keep.tile([P, PASSES * 768, SLOTS], BF16, name="hb16", tag="rounded", align_bytes=64)
-        hb16_wide = hb16[:, : PASSES * 512].rearrange("p (a j) t -> p a j t", a=PASSES)
-        hb16_next = hb16[:, PASSES * 512 :].rearrange("p (a j) t -> p a j t", a=PASSES)
-        ha16 = keep.tile([P, M // P, PASSES, NB, SLOTS], BF16, name="ha16", align_bytes=64)
-        for g, a in [(0, 0), (1, 0), (0, 1), (1, 1)]:
-            eng = nc.vector if (g, a) == (1, 1) else nc.gpsimd
-            scale(eng, hb16_wide[:, a : a + 1, g * GB : (g + 1) * GB], gel_b[g][:, a : a + 1], 1, a)
-        for a in range(PASSES):
-            scale(nc.vector, hb16_next[:, a : a + 1], gel_b[2][:, a : a + 1], 1, a)
-        for mt in range(3):
-            scale(nc.vector, ha16[:, mt], gel_a[:, mt], 0, 0)
-        scale(nc.vector, ha16[:, 3, 0:1], gel_a3[0][:].unsqueeze(1), 0, 0)
-
-        codes = keep.tile([P, PASSES * (J + M)], U32, name="codes", tag="codes", align_bytes=64)
+        codes = keep.tile([P, PASSES * (J + M)], U32, name="codes", tag="after_multiplies", align_bytes=64)
         planes = keep.tile([P, PASSES * (J + M)], U8, name="planes", align_bytes=64)
 
-        def operand(c0, n):
-            return codes[:, c0 : c0 + n], planes[:, c0 : c0 + n]
+        def columns(c0, n):
+            return codes[:, c0 : c0 + n].bitcast(FP8X4), planes[:, c0 : c0 + n]
 
-        def hb(j0, n, a):
-            return operand(PASSES * j0 + a * n, n)
+        def hb(j0, n, ps, count=1):
+            return columns(PASSES * j0 + ps * n, count * n)
 
-        def ha(mt, a):
-            return operand(PASSES * J + (PASSES * mt + a) * P, P)
+        def ha(mt, ps, count=1):
+            return columns(PASSES * J + (PASSES * mt + ps) * P, count * P)
 
-        def score(dst, mt, j0, n, a, start, stop):
-            nc.tensor.matmul_mx(
-                out=dst, lhsT=ha(mt, a)[0].bitcast(FP8X4), lhsT_scale=ha(mt, a)[1],
-                rhs=hb(j0, n, a)[0].bitcast(FP8X4), rhs_scale=hb(j0, n, a)[1],
-                start=start, stop=stop,
-            )
+        def quantize(dst, src):
+            nc.vector.quantize_mx(out=dst[0], scales=dst[1], in_=src)
 
-        rows = out.rearrange("(m p) j -> p m j", p=P)
+        def quantize_a(m0, m1):
+            quantize(ha(m0, 0, PASSES * (m1 - m0)), ha16[:, m0:m1].rearrange("p m ps n t -> p (m ps n t)"))
 
-        def finish(y, m0, count, j0, n):
-            res = keep.tile([P, count * n], F32, name="res%d_%d" % (m0, j0))
-            nc.scalar.activation(res[:], y, ACT.Exp, scale=0.015625)
-            nc.sync.dma_start(rows[:, m0 : m0 + count, j0 : j0 + n], res[:].rearrange("p (m j) -> p m j", j=n))
+        def score(dst, mt, j0, n, ps, start, stop):
+            nc.tensor.matmul_mx(out=dst, lhsT=ha(mt, ps)[0], lhsT_scale=ha(mt, ps)[1], rhs=hb(j0, n, ps)[0], rhs_scale=hb(j0, n, ps)[1], start=start, stop=stop)
 
         def new_bank():
-            return psum.tile([P, 512], F32, name="y", tag="y", bufs=4)
+            return psum.tile([P, BANK], F32, name="y", tag="y", bufs=Y_BANKS)
 
-        quantize(operand(PASSES * J, 2 * PASSES * P), ha16[:, 0:2].rearrange("p m a n t -> p (m a n t)"))
-        quantize(hb(0, 512, 0), hb16_wide[:, 0].rearrange("p j t -> p (j t)"))
-        first = [new_bank() for mt in range(2)]
-        for mt in range(2):
-            score(first[mt][:], mt, 0, 512, 0, True, False)
-        scale(nc.vector, ha16[:, 3, 1:2], gel_a3[1][:].unsqueeze(1), 0, 1)
-        quantize(hb(0, 512, 1), hb16_wide[:, 1].rearrange("p j t -> p (j t)"))
-        for mt in range(2):
-            score(first[mt][:], mt, 0, 512, 1, False, True)
-            finish(first[mt][:], mt, 1, 0, 512)
-        quantize(operand(PASSES * J + 2 * PASSES * P, 2 * PASSES * P), ha16[:, 2:4].rearrange("p m a n t -> p (m a n t)"))
-        for mt in range(2, 4):
+        out_rows = out.rearrange("(m p) j -> p m j", p=P)
+
+        def finish(y, m0, j0, n):
+            res = keep.tile([P, BANK], F32, name="res%d_%d" % (m0, j0))
+            nc.scalar.activation(res[:], y[:], ACT.Exp, scale=1.0 / 64)
+            nc.sync.dma_start(out_rows[:, m0 : m0 + BANK // n, j0 : j0 + n], res[:].rearrange("p (m j) -> p m j", j=n))
+
+        def scores(m0, j0, n):
             y = new_bank()
-            for a in range(PASSES):
-                score(y[:], mt, 0, 512, a, a == 0, a == PASSES - 1)
-            finish(y[:], mt, 1, 0, 512)
-        quantize(operand(PASSES * 512, PASSES * GB), hb16_next.rearrange("p a j t -> p (a j t)"))
-        for m0 in range(0, M // P, 2):
-            y = new_bank()
-            for i in range(2):
-                for a in range(PASSES):
-                    score(y[:, i * GB : (i + 1) * GB], m0 + i, 512, GB, a, a == 0, a == PASSES - 1)
-            finish(y[:], m0, 2, 512, GB)
-        hb16_end = keep.tile([P, GB // NB, PASSES, NB, SLOTS], BF16, name="hb16_end", tag="rounded", align_bytes=64)
-        scale(nc.vector, hb16_end[:, 0], gel_end[:, 0], 1, 0)
-        scale(nc.vector, hb16_end[:, 1, 0:1], gel_end[:, 1, 0:1], 1, 0)
-        quantize(operand(PASSES * 768, PASSES * NB), hb16_end[:, 0].rearrange("p a j t -> p (a j t)"))
+            for place in range(BANK // n):
+                for ps in range(PASSES):
+                    score(y[:, place * n : (place + 1) * n], m0 + place, j0, n, ps, ps == 0, ps == PASSES - 1)
+            finish(y, m0, j0, n)
+
+        early = 2
+        quantize_a(0, early)
+        first = [new_bank() for mt in range(early)]
+        for ps in range(PASSES):
+            quantize(hb(0, BANK, ps), hb16_wide[:, ps].rearrange("p j t -> p (j t)"))
+            for mt in range(early):
+                score(first[mt][:], mt, 0, BANK, ps, ps == 0, ps == PASSES - 1)
+        for mt in range(early):
+            finish(first[mt], mt, 0, BANK)
+        quantize_a(early, end)
+        scores(early, 0, BANK)
+        scale(nc.vector, ha16[:, end, 1:2], gel_a_end[1][:], A_SIDE, 1)
+        quantize(hb(BANK, GB, 0, PASSES), hb16_next.rearrange("p ps j t -> p (ps j t)"))
+        quantize_a(end, A_TILES)
+        scores(end, 0, BANK)
+        for m0 in range(0, A_TILES, BANK // GB):
+            scores(m0, BANK, GB)
+
+        hb16_last = keep.tile([P, GB // NB, PASSES, NB, SLOTS], BF16, name="hb16_last", tag="after_gathers", align_bytes=64)
+        scale(nc.vector, hb16_last[:, 0], gel_last[:, 0], B_SIDE, 0)
+        scale(nc.vector, hb16_last[:, 1, 0:1], gel_last[:, 1, 0:1], B_SIDE, 0)
+        quantize(hb(last_group, NB, 0, PASSES), hb16_last[:, 0].rearrange("p ps j t -> p (ps j t)"))
+        scores(0, last_group, NB)
+        scale(nc.vector, hb16_last[:, 1, 1:2], gel_last[:, 1, 1:2], B_SIDE, 1)
         y = new_bank()
-        for mt in range(M // P):
-            for a in range(PASSES):
-                score(y[:, mt * NB : (mt + 1) * NB], mt, 768, NB, a, a == 0, a == PASSES - 1)
-        finish(y[:], 0, M // P, 768, NB)
-        scale(nc.vector, hb16_end[:, 1, 1:2], gel_end[:, 1, 1:2], 1, 1)
-        last = new_bank()
-        for a in range(PASSES):
-            quantize(hb(896, NB, a), hb16_end[:, 1, a].rearrange("p j t -> p (j t)"))
-            for mt in range(M // P):
-                score(last[:, mt * NB : (mt + 1) * NB], mt, 896, NB, a, (a, mt) == (0, 0), (a, mt) == (PASSES - 1, M // P - 1))
-        finish(last[:], 0, M // P, 896, NB)
+        for ps in range(PASSES):
+            quantize(hb(J - NB, NB, ps), hb16_last[:, 1, ps].rearrange("p j t -> p (j t)"))
+            for mt in range(A_TILES):
+                score(y[:, mt * NB : (mt + 1) * NB], mt, J - NB, NB, ps, (ps, mt) == (0, 0), (ps, mt) == (PASSES - 1, A_TILES - 1))
+        finish(y, 0, J - NB, NB)

@@ -23,14 +23,13 @@ RUN = 8
 PASSES = R // 512
 TILES = PASSES * SLOTS
 BANK = 512
+BANK_BYTES = 2048
 NB = BANK // SLOTS
 GB = 256
 GROUPS = J // GB
 A_TILES = M // P
 PER_COLUMN = 16
-Z_BANKS = 3
-Y_BANKS = 4
-KEEP_WARM = 2
+Z_BANKS = 4
 A_SIDE, B_SIDE = 0, 1
 
 
@@ -39,15 +38,17 @@ def tile_list_biaff_gelu_exp_kernel(tc, tab_words, tab_scales, tab2_words, tab2_
     with ExitStack() as ctx:
         lists = ctx.enter_context(tc.tile_pool(name="lists", bufs=1))
         keep = ctx.enter_context(tc.tile_pool(name="keep", bufs=1))
+        shared = ctx.enter_context(tc.tile_pool(name="shared", bufs=1))
         psum = ctx.enter_context(tc.psum_pool(name="psum", bufs=1))
 
         offs_a = lists.tile([P, M // PER_COLUMN], U16, name="offs_a")
         offs_b = lists.tile([P, J // PER_COLUMN], U16, name="offs_b")
 
-        wb_s = keep.tile([P, R // 4], I32, name="wb_s", tag="after_wb_scales", align_bytes=64)
+        at_wb_s, at_wa_s, at_codes = 0, 4096, 20480
+        wb_s = shared.tile([P, R // 4], I32, name="wb_s", offset=at_wb_s, align_bytes=64)
         tb_s = keep.tile([P, T // 4], I32, name="tb_s", align_bytes=64)
         ta_s = keep.tile([P, T // 4], I32, name="ta_s", align_bytes=64)
-        wa_s = keep.tile([P, R // 4], I32, name="wa_s", tag="after_wa_scales", align_bytes=64)
+        wa_s = shared.tile([P, R // 4], I32, name="wa_s", offset=at_wa_s, align_bytes=64)
         s_rows = keep.tile([P, P], F32, name="s_rows")
         ident = keep.tile([P, P], F32, name="ident")
         nc.vector.memset(tb_s[:], 0)
@@ -58,13 +59,13 @@ def tile_list_biaff_gelu_exp_kernel(tc, tab_words, tab_scales, tab2_words, tab2_
         nc.vector.memset(ident[:], 0.0)
         make_identity(nc, ident[:], nomemset=True)
 
-        def load_scales(dst, src):
+        def load_scales(dst, src, quadrants=range(4)):
             rows = src[0].bitcast(I32)
-            for quadrant in range(4):
+            for quadrant in quadrants:
                 nc.sync.dma_start(dst[32 * quadrant : 32 * quadrant + 4, :], rows[4 * quadrant : 4 * quadrant + 4, :])
 
-        def load_words(dst, src):
-            nc.sync.dma_start(dst[:], src[0].rearrange("p c i -> p (c i)").bitcast(I32))
+        def load_words(dst, src, c0, c1):
+            nc.sync.dma_start(dst[:, c0:c1], src[0].rearrange("p c i -> p (c i)").bitcast(I32)[:, c0:c1])
 
         def load_factor(side, vec):
             nc.sync.dma_start(
@@ -78,15 +79,15 @@ def tile_list_biaff_gelu_exp_kernel(tc, tab_words, tab_scales, tab2_words, tab2_
         wa_w = keep.tile([P, R], I32, name="wa_w", align_bytes=64)
         nc.sync.dma_start(wb_w[:], wb_words[0].bitcast(I32))
         nc.sync.dma_start(offs_b[:], offs2)
-        load_scales(tb_s, tab2_scales)
-        load_words(tb_w, tab2_words)
+        load_scales(tb_s, tab2_scales, quadrants=(0, 2, 1, 3))
+        load_words(tb_w, tab2_words, 0, T)
         load_scales(wb_s, wb_scales)
         nc.sync.dma_start(offs_a[:], offs)
-        load_words(ta_w, tab_words)
+        load_words(ta_w, tab_words, 0, T)
         load_factor(A_SIDE, sa)
         load_factor(B_SIDE, sb)
         load_scales(ta_s, tab_scales)
-        load_words(wa_w, wa_words)
+        load_words(wa_w, wa_words, 0, R)
         load_scales(wa_s, wa_scales)
 
         def reorder(name, src, run):
@@ -97,29 +98,32 @@ def tile_list_biaff_gelu_exp_kernel(tc, tab_words, tab_scales, tab2_words, tab2_
             )
             return dst
 
-        def gather(name, dtype, table, offsets, n0, n1, tag=""):
-            dst = keep.tile([P, n1 - n0], dtype, name=name, tag=tag, align_bytes=64)
-            nc.vector.tensor_copy(dst[:], table[:].bitcast(dtype).indirect(offsets[:, n0 // PER_COLUMN : n1 // PER_COLUMN]))
-            return dst
+        def gather(dst, table, offsets, n0):
+            n1 = n0 + dst.shape[1]
+            nc.vector.tensor_copy(dst[:], table[:].bitcast(dst.dtype).indirect(offsets[:, n0 // PER_COLUMN : n1 // PER_COLUMN]))
 
         last_group = J - GB
         wb_wr = reorder("wb_wr", wb_w, RUN // 2)
-        gb_s = gather("gb_s", U8, tb_s, offs_b, 0, last_group)
-        gb_s_last = gather("gb_s_last", U8, tb_s, offs_b, last_group, J, "after_gathers")
-        gb_first = gather("gb_first", U32, tb_w, offs_b, 0, GB)
+        gb_s = keep.tile([P, J], U8, name="gb_s", align_bytes=64)
+        gather(gb_s, tb_s, offs_b, 0)
+        gb_w0 = keep.tile([P, GB], U32, name="gb_w0", align_bytes=64)
+        gather(gb_w0, tb_w, offs_b, 0)
         wb_sr = reorder("wb_sr", wb_s, RUN // 4)
-        gb_rest = gather("gb_rest", U32, tb_w, offs_b, GB, J, "after_wb_scales")
-        ga_w = gather("ga_w", U32, ta_w, offs_a, 0, M)
-        ga_s = gather("ga_s", U8, ta_s, offs_a, 0, M)
+        gb_w1 = shared.tile([P, J - GB], U32, name="gb_w1", offset=at_wb_s, align_bytes=64)
+        gather(gb_w1, tb_w, offs_b, GB)
+        ga_w = keep.tile([P, M], U32, name="ga_w", align_bytes=64)
+        gather(ga_w, ta_w, offs_a, 0)
+        ga_s = keep.tile([P, M], U8, name="ga_s", align_bytes=64)
+        gather(ga_s, ta_s, offs_a, 0)
         wa_wr = reorder("wa_wr", wa_w, RUN)
         wa_sr = reorder("wa_sr", wa_s, RUN // 4)
-        gb_s_held = keep.tile([P, GB // 4], I32, name="gb_s_held", tag="after_wa_scales", align_bytes=64)
-        nc.vector.tensor_copy(gb_s_held[:], gb_s_last[:].bitcast(I32))
 
-        ga = (ga_w[:], ga_s[:])
-        gb = [(gb_first[:], gb_s[:, :GB])]
-        gb.extend([(gb_rest[:, (g - 1) * GB : g * GB], gb_s[:, g * GB : (g + 1) * GB]) for g in range(1, GROUPS - 1)])
-        gb.append((gb_rest[:, last_group - GB :], gb_s_held[:].bitcast(U8)))
+        def a_entries(n0, n):
+            return ga_w[:, n0 : n0 + n].bitcast(FP8X4), ga_s[:, n0 : n0 + n]
+
+        def b_entries(n0, n):
+            words = gb_w0[:, n0 : n0 + n] if n0 < GB else gb_w1[:, n0 - GB : n0 - GB + n]
+            return words.bitcast(FP8X4), gb_s[:, n0 : n0 + n]
 
         def wb_tile(ps, t):
             c = (ps * SLOTS + t) * P
@@ -129,46 +133,65 @@ def tile_list_biaff_gelu_exp_kernel(tc, tab_words, tab_scales, tab2_words, tab2_
             c = (ps * SLOTS + t) * P
             return wa_wr[:, c : c + P].bitcast(FP8X4), wa_sr[:].bitcast(U8)[:, c : c + P]
 
-        def hidden(weights, ps, gathered, c0, dst):
-            z = psum.tile([P, SLOTS, NB], F32, name="z", tag="z", bufs=Z_BANKS)
+        used = []
+
+        def z_bank(shape):
+            used.append(0)
+            return psum.tile(shape, F32, name="z%d" % len(used), offset=(1 + (len(used) - 1) % Z_BANKS) * BANK_BYTES)
+
+        def first_layer(dst, weights, ps, t, moving):
+            w, ws = weights(ps, t)
+            nc.tensor.matmul_mx(out=dst, lhsT=w, lhsT_scale=ws, rhs=moving[0], rhs_scale=moving[1], start=True, stop=True)
+
+        def hidden_pairs(weights, ps, moving, dst):
+            for h in range(2):
+                z = z_bank([P, 2, GB])
+                for t in range(2):
+                    first_layer(z[:, t, :], weights, ps, 2 * h + t, moving)
+                nc.scalar.activation(dst[:, h], z[:].rearrange("p t n -> p n t"), ACT.Gelu_apprx_tanh)
+
+        def hidden(weights, ps, moving, dst):
+            z = z_bank([P, SLOTS, NB])
             for t in range(SLOTS):
-                w, ws = weights(ps, t)
-                nc.tensor.matmul_mx(
-                    out=z[:, t, :], lhsT=w, lhsT_scale=ws,
-                    rhs=gathered[0][:, c0 : c0 + NB].bitcast(FP8X4), rhs_scale=gathered[1][:, c0 : c0 + NB],
-                    start=True, stop=True,
-                )
+                first_layer(z[:, t, :], weights, ps, t, moving)
             nc.scalar.activation(dst, z[:].rearrange("p t n -> p n t"), ACT.Gelu_apprx_tanh)
 
-        s_psum = psum.tile([P, P], F32, name="s_psum")
+        s_psum = psum.tile([P, P], F32, name="s_psum", offset=0)
         nc.tensor.transpose(s_psum[:], s_rows[:], ident[:])
         s_cols = s_psum[:, 0 : 2 * TILES].rearrange("p (x t) -> p x t", t=SLOTS)
         s_sb = keep.tile([P, 2 * PASSES, SLOTS], F32, name="s_sb")
         nc.scalar.copy(s_sb[:], s_cols)
 
-        gel_b = []
+        on_gpsimd = [(1, 1), (2, 0), (2, 1)]
+        gel_b = {}
         for g in range(GROUPS - 1):
-            gel = keep.tile([P, PASSES, GB, SLOTS], F32, name="gel_b%d" % g)
             for ps in range(PASSES):
-                for h in range(GB // NB):
-                    hidden(wb_tile, ps, gb[g], h * NB, gel[:, ps, h * NB : (h + 1) * NB, :])
-            gel_b.append(gel)
+                if (g, ps) in on_gpsimd:
+                    if (g, ps) == on_gpsimd[-1]:
+                        gel = shared.tile([P, 1, GB, SLOTS], F32, name="gel_held", offset=at_codes, align_bytes=64)
+                    else:
+                        gel = keep.tile([P, 1, GB, SLOTS], F32, name="gel_b%d%d" % (g, ps))
+                    for h in range(2):
+                        hidden(wb_tile, ps, b_entries(g * GB + h * NB, NB), gel[:, 0, h * NB : (h + 1) * NB])
+                else:
+                    gel = keep.tile([P, 2, GB, 2], F32, name="gel_b%d%d" % (g, ps))
+                    hidden_pairs(wb_tile, ps, b_entries(g * GB, GB), gel)
+                gel_b[(g, ps)] = gel
 
-        end = A_TILES - 1
-        gel_a = keep.tile([P, end, PASSES, NB, SLOTS], F32, name="gel_a")
-        gel_a_end = [keep.tile([P, 1, NB, SLOTS], F32, name="gel_a_end%d" % ps, tag="after_multiplies" if ps == 0 else "", align_bytes=64) for ps in range(PASSES)]
-        for mt in range(A_TILES):
+        gel_a = {}
+        for ag in range(2):
             for ps in range(PASSES):
-                hidden(wa_tile, ps, ga, mt * NB, gel_a[:, mt, ps] if mt < end else gel_a_end[ps][:, 0])
+                gel = keep.tile([P, 2, GB, 2], F32, name="gel_a%d%d" % (ag, ps))
+                hidden_pairs(wa_tile, ps, a_entries(ag * GB, GB), gel)
+                gel_a[(ag, ps)] = gel
         gel_last = keep.tile([P, GB // NB, PASSES, NB, SLOTS], F32, name="gel_last")
         for h in range(GB // NB):
             for ps in range(PASSES):
-                hidden(wb_tile, ps, gb[GROUPS - 1], h * NB, gel_last[:, h, ps])
+                hidden(wb_tile, ps, b_entries(last_group + h * NB, NB), gel_last[:, h, ps])
 
-        for t in range(KEEP_WARM):
-            unread = psum.tile([P, M], F32, name="unread", tag="z", bufs=Z_BANKS)
-            w, ws = wa_tile(0, t)
-            nc.tensor.matmul_mx(out=unread[:], lhsT=w, lhsT_scale=ws, rhs=ga[0].bitcast(FP8X4), rhs_scale=ga[1], start=True, stop=True)
+        for t in range(3):
+            unread = z_bank([P, M])
+            first_layer(unread[:], wa_tile, 0, t, a_entries(0, M))
 
         def scale(eng, dst, src, side, ps0):
             factors = s_sb[:] if eng is nc.gpsimd else s_cols
@@ -176,21 +199,30 @@ def tile_list_biaff_gelu_exp_kernel(tc, tab_words, tab_scales, tab2_words, tab2_
             x = side * PASSES + ps0
             eng.tensor_tensor(dst, src, factors[:, x : x + count, :].unsqueeze(2).to_broadcast([P, count, n, SLOTS]), MULT)
 
-        hb16 = keep.tile([P, PASSES * last_group, SLOTS], BF16, name="hb16", tag="after_gathers", align_bytes=64)
+        def scale_pairs(dst, gel, side, ps):
+            factors = s_cols[:, side * PASSES + ps, :].rearrange("p (h t) -> p h t", t=2)
+            nc.vector.tensor_tensor(
+                dst.rearrange("p n (h t) -> p n h t", t=2), gel[:].rearrange("p h n t -> p n h t"),
+                factors.unsqueeze(1).to_broadcast([P, GB, 2, 2]), MULT,
+            )
+
+        hb16 = shared.tile([P, PASSES * last_group, SLOTS], BF16, name="hb16", offset=at_wa_s, align_bytes=64)
         hb16_wide = hb16[:, : PASSES * BANK].rearrange("p (ps j) t -> p ps j t", ps=PASSES)
         hb16_next = hb16[:, PASSES * BANK :].rearrange("p (ps j) t -> p ps j t", ps=PASSES)
-        ha16 = keep.tile([P, A_TILES, PASSES, NB, SLOTS], BF16, name="ha16", align_bytes=64)
-        pieces = [(g, ps) for ps in range(PASSES) for g in range(BANK // GB)]
-        for g, ps in pieces:
-            eng = nc.vector if (g, ps) == pieces[-1] else nc.gpsimd
-            scale(eng, hb16_wide[:, ps : ps + 1, g * GB : (g + 1) * GB], gel_b[g][:, ps : ps + 1], B_SIDE, ps)
-        for ps in range(PASSES):
-            scale(nc.vector, hb16_next[:, ps : ps + 1], gel_b[BANK // GB][:, ps : ps + 1], B_SIDE, ps)
-        for mt in range(end):
-            scale(nc.vector, ha16[:, mt], gel_a[:, mt], A_SIDE, 0)
-        scale(nc.vector, ha16[:, end, 0:1], gel_a_end[0][:], A_SIDE, 0)
+        ha16 = keep.tile([P, 2, PASSES, GB, SLOTS], BF16, name="ha16", align_bytes=64)
 
-        codes = keep.tile([P, PASSES * (J + M)], U32, name="codes", tag="after_multiplies", align_bytes=64)
+        for g, ps in sorted(gel_b):
+            gel = gel_b[(g, ps)]
+            dst = hb16_wide[:, ps : ps + 1, g * GB : (g + 1) * GB] if g < 2 else hb16_next[:, ps : ps + 1]
+            if (g, ps) in on_gpsimd:
+                scale(nc.gpsimd, dst, gel[:], B_SIDE, ps)
+            else:
+                scale_pairs(dst[:, 0], gel, B_SIDE, ps)
+        for ag, ps in sorted(gel_a):
+            scale_pairs(ha16[:, ag, ps], gel_a[(ag, ps)], A_SIDE, ps)
+
+
+        codes = shared.tile([P, PASSES * (J + M)], U32, name="codes", offset=at_codes, align_bytes=64)
         planes = keep.tile([P, PASSES * (J + M)], U8, name="planes", align_bytes=64)
 
         def columns(c0, n):
@@ -199,60 +231,55 @@ def tile_list_biaff_gelu_exp_kernel(tc, tab_words, tab_scales, tab2_words, tab2_
         def hb(j0, n, ps, count=1):
             return columns(PASSES * j0 + ps * n, count * n)
 
-        def ha(mt, ps, count=1):
-            return columns(PASSES * J + (PASSES * mt + ps) * P, count * P)
+        def ha(mt, ps):
+            return columns(PASSES * J + ((mt // 2) * PASSES + ps) * GB + (mt % 2) * P, P)
 
         def quantize(dst, src):
             nc.vector.quantize_mx(out=dst[0], scales=dst[1], in_=src)
 
-        def quantize_a(m0, m1):
-            quantize(ha(m0, 0, PASSES * (m1 - m0)), ha16[:, m0:m1].rearrange("p m ps n t -> p (m ps n t)"))
+        def quantize_a(ag, ps0, count):
+            quantize(columns(PASSES * J + (ag * PASSES + ps0) * GB, count * GB), ha16[:, ag, ps0 : ps0 + count].rearrange("p ps n t -> p (ps n t)"))
 
         def score(dst, mt, j0, n, ps, start, stop):
             nc.tensor.matmul_mx(out=dst, lhsT=ha(mt, ps)[0], lhsT_scale=ha(mt, ps)[1], rhs=hb(j0, n, ps)[0], rhs_scale=hb(j0, n, ps)[1], start=start, stop=stop)
 
-        def new_bank():
-            return psum.tile([P, BANK], F32, name="y", tag="y", bufs=Y_BANKS)
+        def new_bank(bank, count=1):
+            return psum.tile([P, count * BANK], F32, name="y%d" % bank, offset=bank * BANK_BYTES)
 
         out_rows = out.rearrange("(m p) j -> p m j", p=P)
 
         def finish(y, m0, j0, n):
-            res = keep.tile([P, BANK], F32, name="res%d_%d" % (m0, j0))
+            res = keep.tile([P, y.shape[1]], F32, name="res%d_%d" % (m0, j0))
             nc.scalar.activation(res[:], y[:], ACT.Exp, scale=1.0 / 64)
-            nc.sync.dma_start(out_rows[:, m0 : m0 + BANK // n, j0 : j0 + n], res[:].rearrange("p (m j) -> p m j", j=n))
+            nc.sync.dma_start(out_rows[:, m0 : m0 + y.shape[1] // n, j0 : j0 + n], res[:].rearrange("p (m j) -> p m j", j=n))
 
-        def scores(m0, j0, n):
-            y = new_bank()
-            for place in range(BANK // n):
+        def scores(y, m0, j0, n):
+            for place in range(y.shape[1] // n):
                 for ps in range(PASSES):
                     score(y[:, place * n : (place + 1) * n], m0 + place, j0, n, ps, ps == 0, ps == PASSES - 1)
             finish(y, m0, j0, n)
 
-        early = 2
-        quantize_a(0, early)
-        first = [new_bank() for mt in range(early)]
+        quantize_a(0, 0, PASSES)
+        first = [new_bank(5), new_bank(6)]
         for ps in range(PASSES):
             quantize(hb(0, BANK, ps), hb16_wide[:, ps].rearrange("p j t -> p (j t)"))
-            for mt in range(early):
+            for mt in range(2):
                 score(first[mt][:], mt, 0, BANK, ps, ps == 0, ps == PASSES - 1)
-        for mt in range(early):
+        for mt in range(2):
             finish(first[mt], mt, 0, BANK)
-        quantize_a(early, end)
-        scores(early, 0, BANK)
-        scale(nc.vector, ha16[:, end, 1:2], gel_a_end[1][:], A_SIDE, 1)
-        quantize(hb(BANK, GB, 0, PASSES), hb16_next.rearrange("p ps j t -> p (ps j t)"))
-        quantize_a(end, A_TILES)
-        scores(end, 0, BANK)
-        for m0 in range(0, A_TILES, BANK // GB):
-            scores(m0, BANK, GB)
-
-        hb16_last = keep.tile([P, GB // NB, PASSES, NB, SLOTS], BF16, name="hb16_last", tag="after_gathers", align_bytes=64)
+        quantize_a(1, 0, PASSES)
+        scores(new_bank(7), 2, 0, BANK)
+        scores(new_bank(1), 3, 0, BANK)
+        hb16_last = keep.tile([P, GB // NB, PASSES, NB, SLOTS], BF16, name="hb16_last", align_bytes=64)
         scale(nc.vector, hb16_last[:, 0], gel_last[:, 0], B_SIDE, 0)
+        quantize(hb(BANK, GB, 0, PASSES), hb16_next.rearrange("p ps j t -> p (ps j t)"))
+        scores(new_bank(2), 0, BANK, GB)
+        scores(new_bank(3), 2, BANK, GB)
         scale(nc.vector, hb16_last[:, 1, 0:1], gel_last[:, 1, 0:1], B_SIDE, 0)
         quantize(hb(last_group, NB, 0, PASSES), hb16_last[:, 0].rearrange("p ps j t -> p (ps j t)"))
-        scores(0, last_group, NB)
+        scores(new_bank(4), 0, last_group, NB)
         scale(nc.vector, hb16_last[:, 1, 1:2], gel_last[:, 1, 1:2], B_SIDE, 1)
-        y = new_bank()
+        y = psum.tile([P, BANK], F32, name="y_end", offset=5 * BANK_BYTES)
         for ps in range(PASSES):
             quantize(hb(J - NB, NB, ps), hb16_last[:, 1, ps].rearrange("p j t -> p (j t)"))
             for mt in range(A_TILES):

@@ -19,18 +19,24 @@ MULT = mybir.AluOpType.mult
 
 P = 128
 SLOTS = 4
+PAIR = 2
 RUN = 8
 PASSES = R // 512
 TILES = PASSES * SLOTS
 BANK = 512
-BANK_BYTES = 2048
+BANK_BYTES = 4 * BANK
 NB = BANK // SLOTS
-GB = 256
+GB = BANK // PAIR
 GROUPS = J // GB
 A_TILES = M // P
 PER_COLUMN = 16
+FACTOR_BANK = 0
 Z_BANKS = 4
+SCORE_BANKS = (5, 6, 7, 1, 2, 3, 4, 5)
+KEEP_WARM = Z_BANKS - 1
 A_SIDE, B_SIDE = 0, 1
+AT_WB_SCALES, AT_WA_SCALES, AT_CODES = 0, 4096, 20480
+ON_GPSIMD = ((0, 0), (0, 1), (1, 0))
 
 
 def tile_list_biaff_gelu_exp_kernel(tc, tab_words, tab_scales, tab2_words, tab2_scales, wa_words, wa_scales, wb_words, wb_scales, sa, sb, offs, offs2, out):
@@ -44,11 +50,10 @@ def tile_list_biaff_gelu_exp_kernel(tc, tab_words, tab_scales, tab2_words, tab2_
         offs_a = lists.tile([P, M // PER_COLUMN], U16, name="offs_a")
         offs_b = lists.tile([P, J // PER_COLUMN], U16, name="offs_b")
 
-        at_wb_s, at_wa_s, at_codes = 0, 4096, 20480
-        wb_s = shared.tile([P, R // 4], I32, name="wb_s", offset=at_wb_s, align_bytes=64)
+        wb_s = shared.tile([P, R // 4], I32, name="wb_s", offset=AT_WB_SCALES, align_bytes=64)
         tb_s = keep.tile([P, T // 4], I32, name="tb_s", align_bytes=64)
         ta_s = keep.tile([P, T // 4], I32, name="ta_s", align_bytes=64)
-        wa_s = shared.tile([P, R // 4], I32, name="wa_s", offset=at_wa_s, align_bytes=64)
+        wa_s = shared.tile([P, R // 4], I32, name="wa_s", offset=AT_WA_SCALES, align_bytes=64)
         s_rows = keep.tile([P, P], F32, name="s_rows")
         ident = keep.tile([P, P], F32, name="ident")
         nc.vector.memset(tb_s[:], 0)
@@ -59,13 +64,13 @@ def tile_list_biaff_gelu_exp_kernel(tc, tab_words, tab_scales, tab2_words, tab2_
         nc.vector.memset(ident[:], 0.0)
         make_identity(nc, ident[:], nomemset=True)
 
-        def load_scales(dst, src, quadrants=range(4)):
+        def load_scales(dst, src, quadrants=(0, 1, 2, 3)):
             rows = src[0].bitcast(I32)
             for quadrant in quadrants:
                 nc.sync.dma_start(dst[32 * quadrant : 32 * quadrant + 4, :], rows[4 * quadrant : 4 * quadrant + 4, :])
 
-        def load_words(dst, src, c0, c1):
-            nc.sync.dma_start(dst[:, c0:c1], src[0].rearrange("p c i -> p (c i)").bitcast(I32)[:, c0:c1])
+        def load_words(dst, src):
+            nc.sync.dma_start(dst[:], src[0].rearrange("p c i -> p (c i)").bitcast(I32))
 
         def load_factor(side, vec):
             nc.sync.dma_start(
@@ -80,14 +85,14 @@ def tile_list_biaff_gelu_exp_kernel(tc, tab_words, tab_scales, tab2_words, tab2_
         nc.sync.dma_start(wb_w[:], wb_words[0].bitcast(I32))
         nc.sync.dma_start(offs_b[:], offs2)
         load_scales(tb_s, tab2_scales, quadrants=(0, 2, 1, 3))
-        load_words(tb_w, tab2_words, 0, T)
+        load_words(tb_w, tab2_words)
         load_scales(wb_s, wb_scales)
         nc.sync.dma_start(offs_a[:], offs)
-        load_words(ta_w, tab_words, 0, T)
+        load_words(ta_w, tab_words)
         load_factor(A_SIDE, sa)
         load_factor(B_SIDE, sb)
         load_scales(ta_s, tab_scales)
-        load_words(wa_w, wa_words, 0, R)
+        load_words(wa_w, wa_words)
         load_scales(wa_s, wa_scales)
 
         def reorder(name, src, run):
@@ -102,15 +107,14 @@ def tile_list_biaff_gelu_exp_kernel(tc, tab_words, tab_scales, tab2_words, tab2_
             n1 = n0 + dst.shape[1]
             nc.vector.tensor_copy(dst[:], table[:].bitcast(dst.dtype).indirect(offsets[:, n0 // PER_COLUMN : n1 // PER_COLUMN]))
 
-        last_group = J - GB
         wb_wr = reorder("wb_wr", wb_w, RUN // 2)
         gb_s = keep.tile([P, J], U8, name="gb_s", align_bytes=64)
         gather(gb_s, tb_s, offs_b, 0)
-        gb_w0 = keep.tile([P, GB], U32, name="gb_w0", align_bytes=64)
-        gather(gb_w0, tb_w, offs_b, 0)
+        gb_first = keep.tile([P, GB], U32, name="gb_first", align_bytes=64)
+        gather(gb_first, tb_w, offs_b, 0)
         wb_sr = reorder("wb_sr", wb_s, RUN // 4)
-        gb_w1 = shared.tile([P, J - GB], U32, name="gb_w1", offset=at_wb_s, align_bytes=64)
-        gather(gb_w1, tb_w, offs_b, GB)
+        gb_rest = shared.tile([P, J - GB], U32, name="gb_rest", offset=AT_WB_SCALES, align_bytes=64)
+        gather(gb_rest, tb_w, offs_b, GB)
         ga_w = keep.tile([P, M], U32, name="ga_w", align_bytes=64)
         gather(ga_w, ta_w, offs_a, 0)
         ga_s = keep.tile([P, M], U8, name="ga_s", align_bytes=64)
@@ -122,7 +126,7 @@ def tile_list_biaff_gelu_exp_kernel(tc, tab_words, tab_scales, tab2_words, tab2_
             return ga_w[:, n0 : n0 + n].bitcast(FP8X4), ga_s[:, n0 : n0 + n]
 
         def b_entries(n0, n):
-            words = gb_w0[:, n0 : n0 + n] if n0 < GB else gb_w1[:, n0 - GB : n0 - GB + n]
+            words = gb_first[:, n0 : n0 + n] if n0 < GB else gb_rest[:, n0 - GB : n0 - GB + n]
             return words.bitcast(FP8X4), gb_s[:, n0 : n0 + n]
 
         def wb_tile(ps, t):
@@ -133,96 +137,87 @@ def tile_list_biaff_gelu_exp_kernel(tc, tab_words, tab_scales, tab2_words, tab2_
             c = (ps * SLOTS + t) * P
             return wa_wr[:, c : c + P].bitcast(FP8X4), wa_sr[:].bitcast(U8)[:, c : c + P]
 
-        used = []
+        z_tiles = []
 
         def z_bank(shape):
-            used.append(0)
-            return psum.tile(shape, F32, name="z%d" % len(used), offset=(1 + (len(used) - 1) % Z_BANKS) * BANK_BYTES)
+            bank = FACTOR_BANK + 1 + len(z_tiles) % Z_BANKS
+            z_tiles.append(psum.tile(shape, F32, name="z%d" % (len(z_tiles) + 1), offset=bank * BANK_BYTES))
+            return z_tiles[-1]
 
-        def first_layer(dst, weights, ps, t, moving):
+        def first_layer(dst, weights, ps, t, entries):
             w, ws = weights(ps, t)
-            nc.tensor.matmul_mx(out=dst, lhsT=w, lhsT_scale=ws, rhs=moving[0], rhs_scale=moving[1], start=True, stop=True)
+            nc.tensor.matmul_mx(out=dst, lhsT=w, lhsT_scale=ws, rhs=entries[0], rhs_scale=entries[1], start=True, stop=True)
 
-        def hidden_pairs(weights, ps, moving, dst):
-            for h in range(2):
-                z = z_bank([P, 2, GB])
-                for t in range(2):
-                    first_layer(z[:, t, :], weights, ps, 2 * h + t, moving)
+        def hidden_pairs(weights, ps, entries, dst):
+            for h in range(SLOTS // PAIR):
+                z = z_bank([P, PAIR, GB])
+                for t in range(PAIR):
+                    first_layer(z[:, t, :], weights, ps, PAIR * h + t, entries)
                 nc.scalar.activation(dst[:, h], z[:].rearrange("p t n -> p n t"), ACT.Gelu_apprx_tanh)
 
-        def hidden(weights, ps, moving, dst):
+        def hidden(weights, ps, entries, dst):
             z = z_bank([P, SLOTS, NB])
             for t in range(SLOTS):
-                first_layer(z[:, t, :], weights, ps, t, moving)
+                first_layer(z[:, t, :], weights, ps, t, entries)
             nc.scalar.activation(dst, z[:].rearrange("p t n -> p n t"), ACT.Gelu_apprx_tanh)
 
-        s_psum = psum.tile([P, P], F32, name="s_psum", offset=0)
+        s_psum = psum.tile([P, P], F32, name="s_psum", offset=FACTOR_BANK * BANK_BYTES)
         nc.tensor.transpose(s_psum[:], s_rows[:], ident[:])
         s_cols = s_psum[:, 0 : 2 * TILES].rearrange("p (x t) -> p x t", t=SLOTS)
-        s_sb = keep.tile([P, 2 * PASSES, SLOTS], F32, name="s_sb")
-        nc.scalar.copy(s_sb[:], s_cols)
+        s_sb = keep.tile([P, PASSES, SLOTS], F32, name="s_sb")
+        nc.scalar.copy(s_sb[:], s_cols[:, B_SIDE * PASSES :])
 
-        on_gpsimd = [(1, 1), (2, 0), (2, 1)]
         gel_b = {}
         for g in range(GROUPS - 1):
             for ps in range(PASSES):
-                if (g, ps) in on_gpsimd:
-                    if (g, ps) == on_gpsimd[-1]:
-                        gel = shared.tile([P, 1, GB, SLOTS], F32, name="gel_held", offset=at_codes, align_bytes=64)
-                    else:
-                        gel = keep.tile([P, 1, GB, SLOTS], F32, name="gel_b%d%d" % (g, ps))
-                    for h in range(2):
-                        hidden(wb_tile, ps, b_entries(g * GB + h * NB, NB), gel[:, 0, h * NB : (h + 1) * NB])
+                if (g, ps) == ON_GPSIMD[-1]:
+                    gel = shared.tile([P, SLOTS // PAIR, GB, PAIR], F32, name="gel_held", offset=AT_CODES, align_bytes=64)
                 else:
-                    gel = keep.tile([P, 2, GB, 2], F32, name="gel_b%d%d" % (g, ps))
-                    hidden_pairs(wb_tile, ps, b_entries(g * GB, GB), gel)
+                    gel = keep.tile([P, SLOTS // PAIR, GB, PAIR], F32, name="gel_b%d%d" % (g, ps))
+                hidden_pairs(wb_tile, ps, b_entries(g * GB, GB), gel)
                 gel_b[(g, ps)] = gel
 
         gel_a = {}
-        for ag in range(2):
+        for g in range(M // GB):
             for ps in range(PASSES):
-                gel = keep.tile([P, 2, GB, 2], F32, name="gel_a%d%d" % (ag, ps))
-                hidden_pairs(wa_tile, ps, a_entries(ag * GB, GB), gel)
-                gel_a[(ag, ps)] = gel
+                gel = keep.tile([P, SLOTS // PAIR, GB, PAIR], F32, name="gel_a%d%d" % (g, ps))
+                hidden_pairs(wa_tile, ps, a_entries(g * GB, GB), gel)
+                gel_a[(g, ps)] = gel
+        last_group = J - GB
         gel_last = keep.tile([P, GB // NB, PASSES, NB, SLOTS], F32, name="gel_last")
         for h in range(GB // NB):
             for ps in range(PASSES):
                 hidden(wb_tile, ps, b_entries(last_group + h * NB, NB), gel_last[:, h, ps])
 
-        for t in range(3):
+        for t in range(KEEP_WARM):
             unread = z_bank([P, M])
             first_layer(unread[:], wa_tile, 0, t, a_entries(0, M))
 
-        def scale(eng, dst, src, side, ps0):
-            factors = s_sb[:] if eng is nc.gpsimd else s_cols
+        def scale(dst, src, ps0):
             count, n = src.shape[1], src.shape[2]
-            x = side * PASSES + ps0
-            eng.tensor_tensor(dst, src, factors[:, x : x + count, :].unsqueeze(2).to_broadcast([P, count, n, SLOTS]), MULT)
+            x = B_SIDE * PASSES + ps0
+            nc.vector.tensor_tensor(dst, src, s_cols[:, x : x + count, :].unsqueeze(2).to_broadcast([P, count, n, SLOTS]), MULT)
 
-        def scale_pairs(dst, gel, side, ps):
-            factors = s_cols[:, side * PASSES + ps, :].rearrange("p (h t) -> p h t", t=2)
-            nc.vector.tensor_tensor(
-                dst.rearrange("p n (h t) -> p n h t", t=2), gel[:].rearrange("p h n t -> p n h t"),
-                factors.unsqueeze(1).to_broadcast([P, GB, 2, 2]), MULT,
+        def scale_pairs(eng, dst, gel, factors):
+            eng.tensor_tensor(
+                dst.rearrange("p n (h t) -> p n h t", t=PAIR), gel[:].rearrange("p h n t -> p n h t"),
+                factors.rearrange("p (h t) -> p h t", t=PAIR).unsqueeze(1).to_broadcast([P, GB, SLOTS // PAIR, PAIR]), MULT,
             )
 
-        hb16 = shared.tile([P, PASSES * last_group, SLOTS], BF16, name="hb16", offset=at_wa_s, align_bytes=64)
+        hb16 = shared.tile([P, PASSES * last_group, SLOTS], BF16, name="hb16", offset=AT_WA_SCALES, align_bytes=64)
         hb16_wide = hb16[:, : PASSES * BANK].rearrange("p (ps j) t -> p ps j t", ps=PASSES)
         hb16_next = hb16[:, PASSES * BANK :].rearrange("p (ps j) t -> p ps j t", ps=PASSES)
-        ha16 = keep.tile([P, 2, PASSES, GB, SLOTS], BF16, name="ha16", align_bytes=64)
-
+        ha16 = keep.tile([P, M // GB, PASSES, GB, SLOTS], BF16, name="ha16", align_bytes=64)
         for g, ps in sorted(gel_b):
-            gel = gel_b[(g, ps)]
-            dst = hb16_wide[:, ps : ps + 1, g * GB : (g + 1) * GB] if g < 2 else hb16_next[:, ps : ps + 1]
-            if (g, ps) in on_gpsimd:
-                scale(nc.gpsimd, dst, gel[:], B_SIDE, ps)
+            dst = hb16_wide[:, ps, g * GB : (g + 1) * GB] if g < BANK // GB else hb16_next[:, ps]
+            if (g, ps) in ON_GPSIMD:
+                scale_pairs(nc.gpsimd, dst, gel_b[(g, ps)], s_sb[:, ps])
             else:
-                scale_pairs(dst[:, 0], gel, B_SIDE, ps)
-        for ag, ps in sorted(gel_a):
-            scale_pairs(ha16[:, ag, ps], gel_a[(ag, ps)], A_SIDE, ps)
+                scale_pairs(nc.vector, dst, gel_b[(g, ps)], s_cols[:, B_SIDE * PASSES + ps])
+        for g, ps in sorted(gel_a):
+            scale_pairs(nc.vector, ha16[:, g, ps], gel_a[(g, ps)], s_cols[:, A_SIDE * PASSES + ps])
 
-
-        codes = shared.tile([P, PASSES * (J + M)], U32, name="codes", offset=at_codes, align_bytes=64)
+        codes = shared.tile([P, PASSES * (J + M)], U32, name="codes", offset=AT_CODES, align_bytes=64)
         planes = keep.tile([P, PASSES * (J + M)], U8, name="planes", align_bytes=64)
 
         def columns(c0, n):
@@ -232,54 +227,61 @@ def tile_list_biaff_gelu_exp_kernel(tc, tab_words, tab_scales, tab2_words, tab2_
             return columns(PASSES * j0 + ps * n, count * n)
 
         def ha(mt, ps):
-            return columns(PASSES * J + ((mt // 2) * PASSES + ps) * GB + (mt % 2) * P, P)
+            g, m0 = divmod(mt * P, GB)
+            return columns(PASSES * (J + g * GB) + ps * GB + m0, P)
 
         def quantize(dst, src):
             nc.vector.quantize_mx(out=dst[0], scales=dst[1], in_=src)
 
-        def quantize_a(ag, ps0, count):
-            quantize(columns(PASSES * J + (ag * PASSES + ps0) * GB, count * GB), ha16[:, ag, ps0 : ps0 + count].rearrange("p ps n t -> p (ps n t)"))
+        def quantize_a(g):
+            quantize(columns(PASSES * (J + g * GB), PASSES * GB), ha16[:, g].rearrange("p ps n t -> p (ps n t)"))
 
         def score(dst, mt, j0, n, ps, start, stop):
             nc.tensor.matmul_mx(out=dst, lhsT=ha(mt, ps)[0], lhsT_scale=ha(mt, ps)[1], rhs=hb(j0, n, ps)[0], rhs_scale=hb(j0, n, ps)[1], start=start, stop=stop)
 
-        def new_bank(bank, count=1):
-            return psum.tile([P, count * BANK], F32, name="y%d" % bank, offset=bank * BANK_BYTES)
+        y_tiles = []
+
+        def y_bank():
+            y_tiles.append(psum.tile([P, BANK], F32, name="y%d" % len(y_tiles), offset=SCORE_BANKS[len(y_tiles)] * BANK_BYTES))
+            return y_tiles[-1]
 
         out_rows = out.rearrange("(m p) j -> p m j", p=P)
 
         def finish(y, m0, j0, n):
-            res = keep.tile([P, y.shape[1]], F32, name="res%d_%d" % (m0, j0))
+            res = keep.tile([P, BANK], F32, name="res%d_%d" % (m0, j0))
             nc.scalar.activation(res[:], y[:], ACT.Exp, scale=1.0 / 64)
-            nc.sync.dma_start(out_rows[:, m0 : m0 + y.shape[1] // n, j0 : j0 + n], res[:].rearrange("p (m j) -> p m j", j=n))
+            nc.sync.dma_start(out_rows[:, m0 : m0 + BANK // n, j0 : j0 + n], res[:].rearrange("p (m j) -> p m j", j=n))
 
-        def scores(y, m0, j0, n):
-            for place in range(y.shape[1] // n):
+        def scores(m0, j0, n):
+            y = y_bank()
+            for place in range(BANK // n):
                 for ps in range(PASSES):
                     score(y[:, place * n : (place + 1) * n], m0 + place, j0, n, ps, ps == 0, ps == PASSES - 1)
             finish(y, m0, j0, n)
 
-        quantize_a(0, 0, PASSES)
-        first = [new_bank(5), new_bank(6)]
+        in_group = GB // P
+        quantize_a(0)
+        first = [y_bank() for mt in range(in_group)]
         for ps in range(PASSES):
             quantize(hb(0, BANK, ps), hb16_wide[:, ps].rearrange("p j t -> p (j t)"))
-            for mt in range(2):
+            for mt in range(in_group):
                 score(first[mt][:], mt, 0, BANK, ps, ps == 0, ps == PASSES - 1)
-        for mt in range(2):
+        for mt in range(in_group):
             finish(first[mt], mt, 0, BANK)
-        quantize_a(1, 0, PASSES)
-        scores(new_bank(7), 2, 0, BANK)
-        scores(new_bank(1), 3, 0, BANK)
+        quantize_a(1)
+        for mt in range(in_group, A_TILES):
+            scores(mt, 0, BANK)
+
         hb16_last = keep.tile([P, GB // NB, PASSES, NB, SLOTS], BF16, name="hb16_last", align_bytes=64)
-        scale(nc.vector, hb16_last[:, 0], gel_last[:, 0], B_SIDE, 0)
+        scale(hb16_last[:, 0], gel_last[:, 0], 0)
         quantize(hb(BANK, GB, 0, PASSES), hb16_next.rearrange("p ps j t -> p (ps j t)"))
-        scores(new_bank(2), 0, BANK, GB)
-        scores(new_bank(3), 2, BANK, GB)
-        scale(nc.vector, hb16_last[:, 1, 0:1], gel_last[:, 1, 0:1], B_SIDE, 0)
+        for m0 in range(0, A_TILES, BANK // GB):
+            scores(m0, BANK, GB)
+        scale(hb16_last[:, 1, 0:1], gel_last[:, 1, 0:1], 0)
         quantize(hb(last_group, NB, 0, PASSES), hb16_last[:, 0].rearrange("p ps j t -> p (ps j t)"))
-        scores(new_bank(4), 0, last_group, NB)
-        scale(nc.vector, hb16_last[:, 1, 1:2], gel_last[:, 1, 1:2], B_SIDE, 1)
-        y = psum.tile([P, BANK], F32, name="y_end", offset=5 * BANK_BYTES)
+        scores(0, last_group, NB)
+        scale(hb16_last[:, 1, 1:2], gel_last[:, 1, 1:2], 1)
+        y = y_bank()
         for ps in range(PASSES):
             quantize(hb(J - NB, NB, ps), hb16_last[:, 1, ps].rearrange("p j t -> p (j t)"))
             for mt in range(A_TILES):

@@ -56,13 +56,15 @@ def tile_list_biaff_gelu_exp_kernel(tc, tab_words, tab_scales, tab2_words, tab2_
         wa_s = shared.tile([P, R // 4], I32, name="wa_s", offset=AT_WA_SCALES, align_bytes=64)
         s_rows = keep.tile([P, P], F32, name="s_rows")
         ident = keep.tile([P, P], F32, name="ident")
+        zero = keep.tile([P, 1], F32, name="zero")
         nc.vector.memset(tb_s[:], 0)
         nc.vector.memset(wb_s[:], 0)
-        nc.vector.memset(s_rows[:], 0.0)
         nc.vector.memset(ta_s[:], 0)
         nc.vector.memset(wa_s[:], 0)
+        nc.vector.memset(zero[:], 0.0)
         nc.vector.memset(ident[:], 0.0)
         make_identity(nc, ident[:], nomemset=True)
+        nc.scalar.activation(s_rows[:], zero[:].to_broadcast([P, P]), ACT.Gelu_apprx_tanh)
 
         def load_scales(dst, src, quadrants=(0, 1, 2, 3)):
             rows = src[0].bitcast(I32)
@@ -95,11 +97,11 @@ def tile_list_biaff_gelu_exp_kernel(tc, tab_words, tab_scales, tab2_words, tab2_
         load_words(wa_w, wa_words)
         load_scales(wa_s, wa_scales)
 
-        def reorder(name, src, run):
-            dst = keep.tile([P, src.shape[1]], I32, name=name, align_bytes=64)
-            nc.vector.tensor_copy(
+        def reorder(copy, name, src, run):
+            dst = keep.tile([P, src.shape[1]], U32, name=name, align_bytes=64)
+            copy(
                 dst[:].rearrange("p (u q i) -> p u q i", u=TILES, i=run),
-                src[:].rearrange("p (q u i) -> p u q i", u=TILES, i=run),
+                src[:].bitcast(U32).rearrange("p (q u i) -> p u q i", u=TILES, i=run),
             )
             return dst
 
@@ -107,20 +109,20 @@ def tile_list_biaff_gelu_exp_kernel(tc, tab_words, tab_scales, tab2_words, tab2_
             n1 = n0 + dst.shape[1]
             nc.vector.tensor_copy(dst[:], table[:].bitcast(dst.dtype).indirect(offsets[:, n0 // PER_COLUMN : n1 // PER_COLUMN]))
 
-        wb_wr = reorder("wb_wr", wb_w, RUN // 2)
+        wb_wr = reorder(nc.scalar.copy, "wb_wr", wb_w, RUN // 2)
         gb_s = keep.tile([P, J], U8, name="gb_s", align_bytes=64)
         gather(gb_s, tb_s, offs_b, 0)
         gb_first = keep.tile([P, GB], U32, name="gb_first", align_bytes=64)
         gather(gb_first, tb_w, offs_b, 0)
-        wb_sr = reorder("wb_sr", wb_s, RUN // 4)
-        gb_rest = shared.tile([P, J - GB], U32, name="gb_rest", offset=AT_WB_SCALES, align_bytes=64)
+        wb_sr = reorder(nc.scalar.copy, "wb_sr", wb_s, RUN // 4)
+        gb_rest = keep.tile([P, J - GB], U32, name="gb_rest", align_bytes=64)
         gather(gb_rest, tb_w, offs_b, GB)
         ga_w = keep.tile([P, M], U32, name="ga_w", align_bytes=64)
         gather(ga_w, ta_w, offs_a, 0)
         ga_s = keep.tile([P, M], U8, name="ga_s", align_bytes=64)
         gather(ga_s, ta_s, offs_a, 0)
-        wa_wr = reorder("wa_wr", wa_w, RUN)
-        wa_sr = reorder("wa_sr", wa_s, RUN // 4)
+        wa_wr = reorder(nc.vector.tensor_copy, "wa_wr", wa_w, RUN)
+        wa_sr = reorder(nc.vector.tensor_copy, "wa_sr", wa_s, RUN // 4)
 
         def a_entries(n0, n):
             return ga_w[:, n0 : n0 + n].bitcast(FP8X4), ga_s[:, n0 : n0 + n]

@@ -32,7 +32,7 @@ A_TILES = M // P
 PER_COLUMN = 16
 FACTOR_BANK = 0
 Z_BANKS = 4
-SCORE_BANKS = (5, 6, 7, 1, 2, 3, 4, 5)
+SCORE_BANKS = (5, 6, 7, 1, 2, 3, 4, 5, 6)
 KEEP_WARM = Z_BANKS - 1
 A_SIDE, B_SIDE = 0, 1
 AT_WB_SCALES, AT_WA_SCALES, AT_CODES = 0, 4096, 20480
@@ -243,23 +243,24 @@ def tile_list_biaff_gelu_exp_kernel(tc, tab_words, tab_scales, tab2_words, tab2_
 
         y_tiles = []
 
-        def y_bank():
-            y_tiles.append(psum.tile([P, BANK], F32, name="y%d" % len(y_tiles), offset=SCORE_BANKS[len(y_tiles)] * BANK_BYTES))
+        def y_bank(width=BANK):
+            y_tiles.append(psum.tile([P, width], F32, name="y%d" % len(y_tiles), offset=SCORE_BANKS[len(y_tiles)] * BANK_BYTES))
             return y_tiles[-1]
 
         out_rows = out.rearrange("(m p) j -> p m j", p=P)
 
-        def finish(y, m0, j0, n):
-            res = keep.tile([P, BANK], F32, name="res%d_%d" % (m0, j0))
-            nc.scalar.activation(res[:], y[:], ACT.Exp, scale=1.0 / 64)
-            nc.sync.dma_start(out_rows[:, m0 : m0 + BANK // n, j0 : j0 + n], res[:].rearrange("p (m j) -> p m j", j=n))
+        def finish(y, m0, j0, n, queue=nc.sync):
+            width = y.shape[1]
+            res = keep.tile([P, width], F32, name="res%d_%d" % (m0, j0))
+            nc.scalar.activation(res[:], y, ACT.Exp, scale=1.0 / 64)
+            queue.dma_start(out_rows[:, m0 : m0 + width // n, j0 : j0 + n], res[:].rearrange("p (m j) -> p m j", j=n))
 
         def scores(m0, j0, n):
             y = y_bank()
             for place in range(BANK // n):
                 for ps in range(PASSES):
                     score(y[:, place * n : (place + 1) * n], m0 + place, j0, n, ps, ps == 0, ps == PASSES - 1)
-            finish(y, m0, j0, n)
+            finish(y[:], m0, j0, n)
 
         in_group = GB // P
         quantize_a(0)
@@ -268,8 +269,10 @@ def tile_list_biaff_gelu_exp_kernel(tc, tab_words, tab_scales, tab2_words, tab2_
             quantize(hb(0, BANK, ps), hb16_wide[:, ps].rearrange("p j t -> p (j t)"))
             for mt in range(in_group):
                 score(first[mt][:], mt, 0, BANK, ps, ps == 0, ps == PASSES - 1)
-        for mt in range(in_group):
-            finish(first[mt], mt, 0, BANK)
+        for j0 in range(0, BANK, GB):
+            finish(first[0][:, j0 : j0 + GB], 0, j0, GB)
+        for mt in range(1, in_group):
+            finish(first[mt][:], mt, 0, BANK)
         quantize_a(1)
         for mt in range(in_group, A_TILES):
             scores(mt, 0, BANK)
@@ -283,9 +286,11 @@ def tile_list_biaff_gelu_exp_kernel(tc, tab_words, tab_scales, tab2_words, tab2_
         quantize(hb(last_group, NB, 0, PASSES), hb16_last[:, 0].rearrange("p ps j t -> p (ps j t)"))
         scores(0, last_group, NB)
         scale(hb16_last[:, 1, 1:2], gel_last[:, 1, 1:2], 1)
-        y = y_bank()
+        ys = [y_bank(in_group * NB) for g in range(M // GB)]
         for ps in range(PASSES):
             quantize(hb(J - NB, NB, ps), hb16_last[:, 1, ps].rearrange("p j t -> p (j t)"))
             for mt in range(A_TILES):
-                score(y[:, mt * NB : (mt + 1) * NB], mt, J - NB, NB, ps, (ps, mt) == (0, 0), (ps, mt) == (PASSES - 1, A_TILES - 1))
-        finish(y, 0, J - NB, NB)
+                g, place = divmod(mt, in_group)
+                score(ys[g][:, place * NB : (place + 1) * NB], mt, J - NB, NB, ps, (ps, place) == (0, 0), (ps, place) == (PASSES - 1, in_group - 1))
+        finish(ys[0][:], 0, J - NB, NB)
+        finish(ys[1][:], in_group, J - NB, NB, nc.scalar)

@@ -32,11 +32,12 @@ A_TILES = M // P
 PER_COLUMN = 16
 FACTOR_BANK = 0
 Z_BANKS = 4
-SCORE_BANKS = (5, 6, 7, 1, 2, 3, 4, 5, 6)
+SCORE_BANKS = (5, 6, 7, 1, 2, 3, 4, 5)
 KEEP_WARM = Z_BANKS - 1
 A_SIDE, B_SIDE = 0, 1
 AT_WB_SCALES, AT_WA_SCALES, AT_CODES = 0, 4096, 20480
 ON_GPSIMD = ((0, 0), (0, 1), (1, 0))
+SPLIT_PIECE, SPLIT_AT = (1, 1), 96
 
 
 def tile_list_biaff_gelu_exp_kernel(tc, tab_words, tab_scales, tab2_words, tab2_scales, wa_words, wa_scales, wb_words, wb_scales, sa, sb, offs, offs2, out):
@@ -66,10 +67,10 @@ def tile_list_biaff_gelu_exp_kernel(tc, tab_words, tab_scales, tab2_words, tab2_
         make_identity(nc, ident[:], nomemset=True)
         nc.scalar.activation(s_rows[:], zero[:].to_broadcast([P, P]), ACT.Gelu_apprx_tanh)
 
-        def load_scales(dst, src, quadrants=(0, 1, 2, 3)):
+        def load_scales(dst, src):
             rows = src[0].bitcast(I32)
-            for quadrant in quadrants:
-                nc.sync.dma_start(dst[32 * quadrant : 32 * quadrant + 4, :], rows[4 * quadrant : 4 * quadrant + 4, :])
+            for row in range(4):
+                nc.sync.dma_start(dst[row:P:32, :], rows[row:16:4, :])
 
         def load_words(dst, src):
             nc.sync.dma_start(dst[:], src[0].rearrange("p c i -> p (c i)").bitcast(I32))
@@ -86,7 +87,7 @@ def tile_list_biaff_gelu_exp_kernel(tc, tab_words, tab_scales, tab2_words, tab2_
         wa_w = keep.tile([P, R], I32, name="wa_w", align_bytes=64)
         nc.sync.dma_start(wb_w[:], wb_words[0].bitcast(I32))
         nc.sync.dma_start(offs_b[:], offs2)
-        load_scales(tb_s, tab2_scales, quadrants=(0, 2, 1, 3))
+        load_scales(tb_s, tab2_scales)
         load_words(tb_w, tab2_words)
         load_scales(wb_s, wb_scales)
         nc.sync.dma_start(offs_a[:], offs)
@@ -97,12 +98,14 @@ def tile_list_biaff_gelu_exp_kernel(tc, tab_words, tab_scales, tab2_words, tab2_
         load_words(wa_w, wa_words)
         load_scales(wa_s, wa_scales)
 
-        def reorder(copy, name, src, run):
+        def reorder(copy, name, src, run, parts=1):
             dst = keep.tile([P, src.shape[1]], U32, name=name, align_bytes=64)
-            copy(
-                dst[:].rearrange("p (u q i) -> p u q i", u=TILES, i=run),
-                src[:].bitcast(U32).rearrange("p (q u i) -> p u q i", u=TILES, i=run),
-            )
+            for part in range(parts):
+                tiles = slice(part * TILES // parts, (part + 1) * TILES // parts)
+                copy(
+                    dst[:].rearrange("p (u q i) -> p u q i", u=TILES, i=run)[:, tiles],
+                    src[:].bitcast(U32).rearrange("p (q u i) -> p u q i", u=TILES, i=run)[:, tiles],
+                )
             return dst
 
         def gather(dst, table, offsets, n0):
@@ -112,11 +115,13 @@ def tile_list_biaff_gelu_exp_kernel(tc, tab_words, tab_scales, tab2_words, tab2_
         wb_wr = reorder(nc.scalar.copy, "wb_wr", wb_w, RUN // 2)
         gb_s = keep.tile([P, J], U8, name="gb_s", align_bytes=64)
         gather(gb_s, tb_s, offs_b, 0)
-        gb_first = keep.tile([P, GB], U32, name="gb_first", align_bytes=64)
+        gb_first = keep.tile([P, NB], U32, name="gb_first", align_bytes=64)
         gather(gb_first, tb_w, offs_b, 0)
-        wb_sr = reorder(nc.scalar.copy, "wb_sr", wb_s, RUN // 4)
-        gb_rest = keep.tile([P, J - GB], U32, name="gb_rest", align_bytes=64)
-        gather(gb_rest, tb_w, offs_b, GB)
+        gb_next = keep.tile([P, BANK - NB], U32, name="gb_next", align_bytes=64)
+        gather(gb_next, tb_w, offs_b, NB)
+        wb_sr = reorder(nc.scalar.copy, "wb_sr", wb_s, RUN // 4, PASSES)
+        gb_rest = keep.tile([P, J - BANK], U32, name="gb_rest", align_bytes=64)
+        gather(gb_rest, tb_w, offs_b, BANK)
         ga_w = keep.tile([P, M], U32, name="ga_w", align_bytes=64)
         gather(ga_w, ta_w, offs_a, 0)
         ga_s = keep.tile([P, M], U8, name="ga_s", align_bytes=64)
@@ -128,8 +133,8 @@ def tile_list_biaff_gelu_exp_kernel(tc, tab_words, tab_scales, tab2_words, tab2_
             return ga_w[:, n0 : n0 + n].bitcast(FP8X4), ga_s[:, n0 : n0 + n]
 
         def b_entries(n0, n):
-            words = gb_first[:, n0 : n0 + n] if n0 < GB else gb_rest[:, n0 - GB : n0 - GB + n]
-            return words.bitcast(FP8X4), gb_s[:, n0 : n0 + n]
+            tile, start = (gb_first, 0) if n0 < NB else (gb_next, NB) if n0 < BANK else (gb_rest, BANK)
+            return tile[:, n0 - start : n0 - start + n].bitcast(FP8X4), gb_s[:, n0 : n0 + n]
 
         def wb_tile(ps, t):
             c = (ps * SLOTS + t) * P
@@ -169,10 +174,14 @@ def tile_list_biaff_gelu_exp_kernel(tc, tab_words, tab_scales, tab2_words, tab2_
         s_sb = keep.tile([P, PASSES, SLOTS], F32, name="s_sb")
         nc.scalar.copy(s_sb[:], s_cols[:, B_SIDE * PASSES :])
 
-        gel_b = {}
-        for g in range(GROUPS - 1):
+        gel_first = keep.tile([P, PASSES, GB, SLOTS], F32, name="gel_first")
+        for h in range(GB // NB):
             for ps in range(PASSES):
-                if (g, ps) == ON_GPSIMD[-1]:
+                hidden(wb_tile, ps, b_entries(h * NB, NB), gel_first[:, ps, h * NB : (h + 1) * NB])
+        gel_b = {}
+        for g in range(1, GROUPS - 1):
+            for ps in range(PASSES):
+                if (g, ps) == SPLIT_PIECE:
                     gel = shared.tile([P, SLOTS // PAIR, GB, PAIR], F32, name="gel_held", offset=AT_CODES, align_bytes=64)
                 else:
                     gel = keep.tile([P, SLOTS // PAIR, GB, PAIR], F32, name="gel_b%d%d" % (g, ps))
@@ -200,24 +209,31 @@ def tile_list_biaff_gelu_exp_kernel(tc, tab_words, tab_scales, tab2_words, tab2_
             x = B_SIDE * PASSES + ps0
             nc.vector.tensor_tensor(dst, src, s_cols[:, x : x + count, :].unsqueeze(2).to_broadcast([P, count, n, SLOTS]), MULT)
 
-        def scale_pairs(eng, dst, gel, factors):
+        def scale_pairs(eng, dst, gel, factors, n0=0, n1=GB):
             eng.tensor_tensor(
-                dst.rearrange("p n (h t) -> p n h t", t=PAIR), gel[:].rearrange("p h n t -> p n h t"),
-                factors.rearrange("p (h t) -> p h t", t=PAIR).unsqueeze(1).to_broadcast([P, GB, SLOTS // PAIR, PAIR]), MULT,
+                dst[:, n0:n1].rearrange("p n (h t) -> p n h t", t=PAIR), gel[:, :, n0:n1].rearrange("p h n t -> p n h t"),
+                factors.rearrange("p (h t) -> p h t", t=PAIR).unsqueeze(1).to_broadcast([P, n1 - n0, SLOTS // PAIR, PAIR]), MULT,
             )
 
         hb16 = shared.tile([P, PASSES * last_group, SLOTS], BF16, name="hb16", offset=AT_WA_SCALES, align_bytes=64)
         hb16_wide = hb16[:, : PASSES * BANK].rearrange("p (ps j) t -> p ps j t", ps=PASSES)
         hb16_next = hb16[:, PASSES * BANK :].rearrange("p (ps j) t -> p ps j t", ps=PASSES)
         ha16 = keep.tile([P, M // GB, PASSES, GB, SLOTS], BF16, name="ha16", align_bytes=64)
+        nc.gpsimd.tensor_tensor(hb16_wide[:, :, 0:GB], gel_first[:], s_sb[:].unsqueeze(2).to_broadcast([P, PASSES, GB, SLOTS]), MULT)
         for g, ps in sorted(gel_b):
             dst = hb16_wide[:, ps, g * GB : (g + 1) * GB] if g < BANK // GB else hb16_next[:, ps]
             if (g, ps) in ON_GPSIMD:
                 scale_pairs(nc.gpsimd, dst, gel_b[(g, ps)], s_sb[:, ps])
+            elif (g, ps) == SPLIT_PIECE:
+                scale_pairs(nc.vector, dst, gel_b[(g, ps)], s_cols[:, B_SIDE * PASSES + ps], SPLIT_AT, GB)
+                scale_pairs(nc.gpsimd, dst, gel_b[(g, ps)], s_sb[:, ps], 0, SPLIT_AT)
             else:
                 scale_pairs(nc.vector, dst, gel_b[(g, ps)], s_cols[:, B_SIDE * PASSES + ps])
         for g, ps in sorted(gel_a):
             scale_pairs(nc.vector, ha16[:, g, ps], gel_a[(g, ps)], s_cols[:, A_SIDE * PASSES + ps])
+
+        hb16_last = keep.tile([P, GB // NB, PASSES, NB, SLOTS], BF16, name="hb16_last", align_bytes=64)
+        scale(hb16_last[:, 0, 0:1], gel_last[:, 0, 0:1], 0)
 
         codes = shared.tile([P, PASSES * (J + M)], U32, name="codes", offset=AT_CODES, align_bytes=64)
         planes = keep.tile([P, PASSES * (J + M)], U8, name="planes", align_bytes=64)
@@ -243,24 +259,23 @@ def tile_list_biaff_gelu_exp_kernel(tc, tab_words, tab_scales, tab2_words, tab2_
 
         y_tiles = []
 
-        def y_bank(width=BANK):
-            y_tiles.append(psum.tile([P, width], F32, name="y%d" % len(y_tiles), offset=SCORE_BANKS[len(y_tiles)] * BANK_BYTES))
+        def y_bank():
+            y_tiles.append(psum.tile([P, BANK], F32, name="y%d" % len(y_tiles), offset=SCORE_BANKS[len(y_tiles)] * BANK_BYTES))
             return y_tiles[-1]
 
         out_rows = out.rearrange("(m p) j -> p m j", p=P)
 
-        def finish(y, m0, j0, n, queue=nc.sync):
-            width = y.shape[1]
-            res = keep.tile([P, width], F32, name="res%d_%d" % (m0, j0))
-            nc.scalar.activation(res[:], y, ACT.Exp, scale=1.0 / 64)
-            queue.dma_start(out_rows[:, m0 : m0 + width // n, j0 : j0 + n], res[:].rearrange("p (m j) -> p m j", j=n))
+        def finish(y, m0, j0, n):
+            res = keep.tile([P, BANK], F32, name="res%d_%d" % (m0, j0))
+            nc.scalar.activation(res[:], y[:], ACT.Exp, scale=1.0 / 64)
+            nc.sync.dma_start(out_rows[:, m0 : m0 + BANK // n, j0 : j0 + n], res[:].rearrange("p (m j) -> p m j", j=n))
 
         def scores(m0, j0, n):
             y = y_bank()
             for place in range(BANK // n):
                 for ps in range(PASSES):
                     score(y[:, place * n : (place + 1) * n], m0 + place, j0, n, ps, ps == 0, ps == PASSES - 1)
-            finish(y[:], m0, j0, n)
+            finish(y, m0, j0, n)
 
         in_group = GB // P
         quantize_a(0)
@@ -269,16 +284,13 @@ def tile_list_biaff_gelu_exp_kernel(tc, tab_words, tab_scales, tab2_words, tab2_
             quantize(hb(0, BANK, ps), hb16_wide[:, ps].rearrange("p j t -> p (j t)"))
             for mt in range(in_group):
                 score(first[mt][:], mt, 0, BANK, ps, ps == 0, ps == PASSES - 1)
-        for j0 in range(0, BANK, GB):
-            finish(first[0][:, j0 : j0 + GB], 0, j0, GB)
-        for mt in range(1, in_group):
-            finish(first[mt][:], mt, 0, BANK)
+        for mt in range(in_group):
+            finish(first[mt], mt, 0, BANK)
         quantize_a(1)
         for mt in range(in_group, A_TILES):
             scores(mt, 0, BANK)
 
-        hb16_last = keep.tile([P, GB // NB, PASSES, NB, SLOTS], BF16, name="hb16_last", align_bytes=64)
-        scale(hb16_last[:, 0], gel_last[:, 0], 0)
+        scale(hb16_last[:, 0, 1:2], gel_last[:, 0, 1:2], 1)
         quantize(hb(BANK, GB, 0, PASSES), hb16_next.rearrange("p ps j t -> p (ps j t)"))
         for m0 in range(0, A_TILES, BANK // GB):
             scores(m0, BANK, GB)
@@ -286,11 +298,9 @@ def tile_list_biaff_gelu_exp_kernel(tc, tab_words, tab_scales, tab2_words, tab2_
         quantize(hb(last_group, NB, 0, PASSES), hb16_last[:, 0].rearrange("p ps j t -> p (ps j t)"))
         scores(0, last_group, NB)
         scale(hb16_last[:, 1, 1:2], gel_last[:, 1, 1:2], 1)
-        ys = [y_bank(in_group * NB) for g in range(M // GB)]
+        y = y_bank()
         for ps in range(PASSES):
             quantize(hb(J - NB, NB, ps), hb16_last[:, 1, ps].rearrange("p j t -> p (j t)"))
             for mt in range(A_TILES):
-                g, place = divmod(mt, in_group)
-                score(ys[g][:, place * NB : (place + 1) * NB], mt, J - NB, NB, ps, (ps, place) == (0, 0), (ps, place) == (PASSES - 1, in_group - 1))
-        finish(ys[0][:], 0, J - NB, NB)
-        finish(ys[1][:], in_group, J - NB, NB, nc.scalar)
+                score(y[:, mt * NB : (mt + 1) * NB], mt, J - NB, NB, ps, (ps, mt) == (0, 0), (ps, mt) == (PASSES - 1, A_TILES - 1))
+        finish(y, 0, J - NB, NB)

@@ -37,7 +37,6 @@ KEEP_WARM = Z_BANKS - 1
 A_SIDE, B_SIDE = 0, 1
 AT_WB_SCALES, AT_WA_SCALES, AT_CODES = 0, 4096, 20480
 ON_GPSIMD = ((0, 0), (0, 1), (1, 0))
-SPLIT_PIECE, SPLIT_AT = (1, 1), 96
 
 
 def tile_list_biaff_gelu_exp_kernel(tc, tab_words, tab_scales, tab2_words, tab2_scales, wa_words, wa_scales, wb_words, wb_scales, sa, sb, offs, offs2, out):
@@ -181,7 +180,7 @@ def tile_list_biaff_gelu_exp_kernel(tc, tab_words, tab_scales, tab2_words, tab2_
         gel_b = {}
         for g in range(1, GROUPS - 1):
             for ps in range(PASSES):
-                if (g, ps) == SPLIT_PIECE:
+                if (g, ps) == ON_GPSIMD[-1]:
                     gel = shared.tile([P, SLOTS // PAIR, GB, PAIR], F32, name="gel_held", offset=AT_CODES, align_bytes=64)
                 else:
                     gel = keep.tile([P, SLOTS // PAIR, GB, PAIR], F32, name="gel_b%d%d" % (g, ps))
@@ -209,31 +208,25 @@ def tile_list_biaff_gelu_exp_kernel(tc, tab_words, tab_scales, tab2_words, tab2_
             x = B_SIDE * PASSES + ps0
             nc.vector.tensor_tensor(dst, src, s_cols[:, x : x + count, :].unsqueeze(2).to_broadcast([P, count, n, SLOTS]), MULT)
 
-        def scale_pairs(eng, dst, gel, factors, n0=0, n1=GB):
+        def scale_pairs(eng, dst, gel, factors):
             eng.tensor_tensor(
-                dst[:, n0:n1].rearrange("p n (h t) -> p n h t", t=PAIR), gel[:, :, n0:n1].rearrange("p h n t -> p n h t"),
-                factors.rearrange("p (h t) -> p h t", t=PAIR).unsqueeze(1).to_broadcast([P, n1 - n0, SLOTS // PAIR, PAIR]), MULT,
+                dst.rearrange("p n (h t) -> p n h t", t=PAIR), gel[:].rearrange("p h n t -> p n h t"),
+                factors.rearrange("p (h t) -> p h t", t=PAIR).unsqueeze(1).to_broadcast([P, GB, SLOTS // PAIR, PAIR]), MULT,
             )
 
         hb16 = shared.tile([P, PASSES * last_group, SLOTS], BF16, name="hb16", offset=AT_WA_SCALES, align_bytes=64)
-        hb16_wide = hb16[:, : PASSES * BANK].rearrange("p (ps j) t -> p ps j t", ps=PASSES)
-        hb16_next = hb16[:, PASSES * BANK :].rearrange("p (ps j) t -> p ps j t", ps=PASSES)
+        hb16_first = hb16[:, : PASSES * GB].rearrange("p (ps j) t -> p ps j t", ps=PASSES)
+        hb16_wide = hb16[:, PASSES * GB :].rearrange("p (ps j) t -> p ps j t", ps=PASSES)
         ha16 = keep.tile([P, M // GB, PASSES, GB, SLOTS], BF16, name="ha16", align_bytes=64)
-        nc.gpsimd.tensor_tensor(hb16_wide[:, :, 0:GB], gel_first[:], s_sb[:].unsqueeze(2).to_broadcast([P, PASSES, GB, SLOTS]), MULT)
+        nc.gpsimd.tensor_tensor(hb16_first, gel_first[:], s_sb[:].unsqueeze(2).to_broadcast([P, PASSES, GB, SLOTS]), MULT)
         for g, ps in sorted(gel_b):
-            dst = hb16_wide[:, ps, g * GB : (g + 1) * GB] if g < BANK // GB else hb16_next[:, ps]
+            dst = hb16_wide[:, ps, (g - 1) * GB : g * GB]
             if (g, ps) in ON_GPSIMD:
                 scale_pairs(nc.gpsimd, dst, gel_b[(g, ps)], s_sb[:, ps])
-            elif (g, ps) == SPLIT_PIECE:
-                scale_pairs(nc.vector, dst, gel_b[(g, ps)], s_cols[:, B_SIDE * PASSES + ps], SPLIT_AT, GB)
-                scale_pairs(nc.gpsimd, dst, gel_b[(g, ps)], s_sb[:, ps], 0, SPLIT_AT)
             else:
                 scale_pairs(nc.vector, dst, gel_b[(g, ps)], s_cols[:, B_SIDE * PASSES + ps])
         for g, ps in sorted(gel_a):
             scale_pairs(nc.vector, ha16[:, g, ps], gel_a[(g, ps)], s_cols[:, A_SIDE * PASSES + ps])
-
-        hb16_last = keep.tile([P, GB // NB, PASSES, NB, SLOTS], BF16, name="hb16_last", align_bytes=64)
-        scale(hb16_last[:, 0, 0:1], gel_last[:, 0, 0:1], 0)
 
         codes = shared.tile([P, PASSES * (J + M)], U32, name="codes", offset=AT_CODES, align_bytes=64)
         planes = keep.tile([P, PASSES * (J + M)], U8, name="planes", align_bytes=64)
@@ -277,23 +270,16 @@ def tile_list_biaff_gelu_exp_kernel(tc, tab_words, tab_scales, tab2_words, tab2_
                     score(y[:, place * n : (place + 1) * n], m0 + place, j0, n, ps, ps == 0, ps == PASSES - 1)
             finish(y, m0, j0, n)
 
-        in_group = GB // P
         quantize_a(0)
-        first = [y_bank() for mt in range(in_group)]
-        for ps in range(PASSES):
-            quantize(hb(0, BANK, ps), hb16_wide[:, ps].rearrange("p j t -> p (j t)"))
-            for mt in range(in_group):
-                score(first[mt][:], mt, 0, BANK, ps, ps == 0, ps == PASSES - 1)
-        for mt in range(in_group):
-            finish(first[mt], mt, 0, BANK)
+        quantize(hb(0, GB, 0, PASSES), hb16_first.rearrange("p ps j t -> p (ps j t)"))
+        scores(0, 0, GB)
         quantize_a(1)
-        for mt in range(in_group, A_TILES):
-            scores(mt, 0, BANK)
-
-        scale(hb16_last[:, 0, 1:2], gel_last[:, 0, 1:2], 1)
-        quantize(hb(BANK, GB, 0, PASSES), hb16_next.rearrange("p ps j t -> p (ps j t)"))
-        for m0 in range(0, A_TILES, BANK // GB):
-            scores(m0, BANK, GB)
+        scores(GB // P, 0, GB)
+        quantize(hb(GB, BANK, 0, PASSES), hb16_wide.rearrange("p ps j t -> p (ps j t)"))
+        for mt in range(A_TILES):
+            scores(mt, GB, BANK)
+        hb16_last = keep.tile([P, GB // NB, PASSES, NB, SLOTS], BF16, name="hb16_last", align_bytes=64)
+        scale(hb16_last[:, 0], gel_last[:, 0], 0)
         scale(hb16_last[:, 1, 0:1], gel_last[:, 1, 0:1], 0)
         quantize(hb(last_group, NB, 0, PASSES), hb16_last[:, 0].rearrange("p ps j t -> p (ps j t)"))
         scores(0, last_group, NB)

@@ -33,7 +33,6 @@ PER_COLUMN = 16
 FACTOR_BANK = 0
 Z_BANKS = 4
 SCORE_BANKS = (5, 6, 7, 1, 2, 3, 4, 5)
-KEEP_WARM = Z_BANKS - 1
 A_SIDE, B_SIDE = 0, 1
 AT_WB_SCALES, AT_WA_SCALES, AT_CODES = 0, 4096, 20480
 ON_GPSIMD = ((0, 0), (0, 1), (1, 0))
@@ -198,10 +197,6 @@ def tile_list_biaff_gelu_exp_kernel(tc, tab_words, tab_scales, tab2_words, tab2_
         for h in range(GB // NB):
             for ps in range(PASSES):
                 hidden(wb_tile, ps, b_entries(last_group + h * NB, NB), gel_last[:, h, ps])
-
-        for t in range(KEEP_WARM):
-            unread = z_bank([P, M])
-            first_layer(unread[:], wa_tile, 0, t, a_entries(0, M))
 
         def scale(dst, src, ps0):
             count, n = src.shape[1], src.shape[2]

@@ -31,11 +31,13 @@ GROUPS = J // GB
 A_TILES = M // P
 PER_COLUMN = 16
 FACTOR_BANK = 0
+WARM_BANK, WARM_PASSES = 7, 4
 Z_BANKS = 4
 SCORE_BANKS = (5, 6, 7, 1, 2, 3, 4, 5)
 A_SIDE, B_SIDE = 0, 1
-AT_WB_SCALES, AT_WA_SCALES, AT_CODES = 0, 4096, 20480
-ON_GPSIMD = ((0, 0), (0, 1), (1, 0))
+SPLIT = 216
+AT_HA16 = 49152
+AT_WB_SCALES, AT_WA_SCALES, AT_TA_SCALES, AT_TAB, AT_CODES, AT_PLANES = 0, 4096, 8192, 16384, 20480, 36864
 
 
 def tile_list_biaff_gelu_exp_kernel(tc, tab_words, tab_scales, tab2_words, tab2_scales, wa_words, wa_scales, wb_words, wb_scales, sa, sb, offs, offs2, out):
@@ -51,7 +53,7 @@ def tile_list_biaff_gelu_exp_kernel(tc, tab_words, tab_scales, tab2_words, tab2_
 
         wb_s = shared.tile([P, R // 4], I32, name="wb_s", offset=AT_WB_SCALES, align_bytes=64)
         tb_s = keep.tile([P, T // 4], I32, name="tb_s", align_bytes=64)
-        ta_s = keep.tile([P, T // 4], I32, name="ta_s", align_bytes=64)
+        ta_s = shared.tile([P, T // 4], I32, name="ta_s", offset=AT_TA_SCALES, align_bytes=64)
         wa_s = shared.tile([P, R // 4], I32, name="wa_s", offset=AT_WA_SCALES, align_bytes=64)
         s_rows = keep.tile([P, P], F32, name="s_rows")
         ident = keep.tile([P, P], F32, name="ident")
@@ -61,6 +63,8 @@ def tile_list_biaff_gelu_exp_kernel(tc, tab_words, tab_scales, tab2_words, tab2_
         nc.vector.memset(ta_s[:], 0)
         nc.vector.memset(wa_s[:], 0)
         nc.vector.memset(zero[:], 0.0)
+        no_bias = shared.tile([P, 1], F32, name="no_bias", offset=AT_PLANES, align_bytes=64)
+        nc.vector.memset(no_bias[:], 0.0)
         nc.vector.memset(ident[:], 0.0)
         make_identity(nc, ident[:], nomemset=True)
         nc.scalar.activation(s_rows[:], zero[:].to_broadcast([P, P]), ACT.Gelu_apprx_tanh)
@@ -85,16 +89,22 @@ def tile_list_biaff_gelu_exp_kernel(tc, tab_words, tab_scales, tab2_words, tab2_
         wa_w = keep.tile([P, R], I32, name="wa_w", align_bytes=64)
         nc.sync.dma_start(wb_w[:], wb_words[0].bitcast(I32))
         nc.sync.dma_start(offs_b[:], offs2)
+        nc.sync.dma_start(offs_a[:], offs)
         load_scales(tb_s, tab2_scales)
         load_words(tb_w, tab2_words)
         load_scales(wb_s, wb_scales)
-        nc.sync.dma_start(offs_a[:], offs)
-        load_words(ta_w, tab_words)
+        load_words(wa_w, wa_words)
         load_factor(A_SIDE, sa)
         load_factor(B_SIDE, sb)
-        load_scales(ta_s, tab_scales)
-        load_words(wa_w, wa_words)
         load_scales(wa_s, wa_scales)
+        warm = psum.tile([P, BANK], F32, name="warm", offset=WARM_BANK * BANK_BYTES)
+        for rep in range(WARM_PASSES):
+            nc.tensor.matmul_mx(
+                out=warm[:], lhsT=ta_s[:, 0:P].bitcast(FP8X4), lhsT_scale=tb_s[:].bitcast(U8)[:, 0:P],
+                rhs=ta_s[:].bitcast(FP8X4), rhs_scale=tb_s[:].bitcast(U8)[:, 0:BANK], start=True, stop=True,
+            )
+        load_words(ta_w, tab_words)
+        load_scales(ta_s, tab_scales)
 
         def reorder(copy, name, src, run, parts=1):
             dst = keep.tile([P, src.shape[1]], U32, name=name, align_bytes=64)
@@ -108,22 +118,16 @@ def tile_list_biaff_gelu_exp_kernel(tc, tab_words, tab_scales, tab2_words, tab2_
 
         def gather(dst, table, offsets, n0):
             n1 = n0 + dst.shape[1]
-            nc.vector.tensor_copy(dst[:], table[:].bitcast(dst.dtype).indirect(offsets[:, n0 // PER_COLUMN : n1 // PER_COLUMN]))
+            nc.vector.tensor_copy(dst, table[:].bitcast(dst.dtype).indirect(offsets[:, n0 // PER_COLUMN : n1 // PER_COLUMN]))
 
         wb_wr = reorder(nc.scalar.copy, "wb_wr", wb_w, RUN // 2)
         gb_s = keep.tile([P, J], U8, name="gb_s", align_bytes=64)
-        gather(gb_s, tb_s, offs_b, 0)
-        gb_first = keep.tile([P, NB], U32, name="gb_first", align_bytes=64)
-        gather(gb_first, tb_w, offs_b, 0)
-        gb_next = keep.tile([P, BANK - NB], U32, name="gb_next", align_bytes=64)
-        gather(gb_next, tb_w, offs_b, NB)
+        gather(gb_s[:], tb_s, offs_b, 0)
+        gb_w = keep.tile([P, J], U32, name="gb_w", align_bytes=64)
+        gather(gb_w[:, 0:NB], tb_w, offs_b, 0)
+        gather(gb_w[:, NB:BANK], tb_w, offs_b, NB)
         wb_sr = reorder(nc.scalar.copy, "wb_sr", wb_s, RUN // 4, PASSES)
-        gb_rest = keep.tile([P, J - BANK], U32, name="gb_rest", align_bytes=64)
-        gather(gb_rest, tb_w, offs_b, BANK)
-        ga_w = keep.tile([P, M], U32, name="ga_w", align_bytes=64)
-        gather(ga_w, ta_w, offs_a, 0)
-        ga_s = keep.tile([P, M], U8, name="ga_s", align_bytes=64)
-        gather(ga_s, ta_s, offs_a, 0)
+        gather(gb_w[:, BANK:], tb_w, offs_b, BANK)
         wa_wr = reorder(nc.vector.tensor_copy, "wa_wr", wa_w, RUN)
         wa_sr = reorder(nc.vector.tensor_copy, "wa_sr", wa_s, RUN // 4)
 
@@ -131,8 +135,7 @@ def tile_list_biaff_gelu_exp_kernel(tc, tab_words, tab_scales, tab2_words, tab2_
             return ga_w[:, n0 : n0 + n].bitcast(FP8X4), ga_s[:, n0 : n0 + n]
 
         def b_entries(n0, n):
-            tile, start = (gb_first, 0) if n0 < NB else (gb_next, NB) if n0 < BANK else (gb_rest, BANK)
-            return tile[:, n0 - start : n0 - start + n].bitcast(FP8X4), gb_s[:, n0 : n0 + n]
+            return gb_w[:, n0 : n0 + n].bitcast(FP8X4), gb_s[:, n0 : n0 + n]
 
         def wb_tile(ps, t):
             c = (ps * SLOTS + t) * P
@@ -153,12 +156,12 @@ def tile_list_biaff_gelu_exp_kernel(tc, tab_words, tab_scales, tab2_words, tab2_
             w, ws = weights(ps, t)
             nc.tensor.matmul_mx(out=dst, lhsT=w, lhsT_scale=ws, rhs=entries[0], rhs_scale=entries[1], start=True, stop=True)
 
-        def hidden_pairs(weights, ps, entries, dst):
+        def hidden_pairs(weights, ps, entries, dst, bias=0.0):
             for h in range(SLOTS // PAIR):
                 z = z_bank([P, PAIR, GB])
                 for t in range(PAIR):
                     first_layer(z[:, t, :], weights, ps, PAIR * h + t, entries)
-                nc.scalar.activation(dst[:, h], z[:].rearrange("p t n -> p n t"), ACT.Gelu_apprx_tanh)
+                nc.scalar.activation(dst[:, h], z[:].rearrange("p t n -> p n t"), ACT.Gelu_apprx_tanh, bias=bias)
 
         def hidden(weights, ps, entries, dst):
             z = z_bank([P, SLOTS, NB])
@@ -169,34 +172,8 @@ def tile_list_biaff_gelu_exp_kernel(tc, tab_words, tab_scales, tab2_words, tab2_
         s_psum = psum.tile([P, P], F32, name="s_psum", offset=FACTOR_BANK * BANK_BYTES)
         nc.tensor.transpose(s_psum[:], s_rows[:], ident[:])
         s_cols = s_psum[:, 0 : 2 * TILES].rearrange("p (x t) -> p x t", t=SLOTS)
-        s_sb = keep.tile([P, PASSES, SLOTS], F32, name="s_sb")
-        nc.scalar.copy(s_sb[:], s_cols[:, B_SIDE * PASSES :])
-
-        gel_first = keep.tile([P, PASSES, GB, SLOTS], F32, name="gel_first")
-        for h in range(GB // NB):
-            for ps in range(PASSES):
-                hidden(wb_tile, ps, b_entries(h * NB, NB), gel_first[:, ps, h * NB : (h + 1) * NB])
-        gel_b = {}
-        for g in range(1, GROUPS - 1):
-            for ps in range(PASSES):
-                if (g, ps) == ON_GPSIMD[-1]:
-                    gel = shared.tile([P, SLOTS // PAIR, GB, PAIR], F32, name="gel_held", offset=AT_CODES, align_bytes=64)
-                else:
-                    gel = keep.tile([P, SLOTS // PAIR, GB, PAIR], F32, name="gel_b%d%d" % (g, ps))
-                hidden_pairs(wb_tile, ps, b_entries(g * GB, GB), gel)
-                gel_b[(g, ps)] = gel
-
-        gel_a = {}
-        for g in range(M // GB):
-            for ps in range(PASSES):
-                gel = keep.tile([P, SLOTS // PAIR, GB, PAIR], F32, name="gel_a%d%d" % (g, ps))
-                hidden_pairs(wa_tile, ps, a_entries(g * GB, GB), gel)
-                gel_a[(g, ps)] = gel
-        last_group = J - GB
-        gel_last = keep.tile([P, GB // NB, PASSES, NB, SLOTS], F32, name="gel_last")
-        for h in range(GB // NB):
-            for ps in range(PASSES):
-                hidden(wb_tile, ps, b_entries(last_group + h * NB, NB), gel_last[:, h, ps])
+        s_sb = shared.tile([P, PASSES, SLOTS], F32, name="s_sb", offset=AT_WA_SCALES, align_bytes=64)
+        nc.vector.tensor_copy(s_sb[:], s_cols[:, B_SIDE * PASSES :])
 
         def scale(dst, src, ps0):
             count, n = src.shape[1], src.shape[2]
@@ -205,26 +182,54 @@ def tile_list_biaff_gelu_exp_kernel(tc, tab_words, tab_scales, tab2_words, tab2_
 
         def scale_pairs(eng, dst, gel, factors):
             eng.tensor_tensor(
-                dst.rearrange("p n (h t) -> p n h t", t=PAIR), gel[:].rearrange("p h n t -> p n h t"),
-                factors.rearrange("p (h t) -> p h t", t=PAIR).unsqueeze(1).to_broadcast([P, GB, SLOTS // PAIR, PAIR]), MULT,
+                dst.rearrange("p n (h t) -> p n h t", t=PAIR), gel.rearrange("p h n t -> p n h t"),
+                factors.rearrange("p (h t) -> p h t", t=PAIR).unsqueeze(1).to_broadcast([P, dst.shape[1], SLOTS // PAIR, PAIR]), MULT,
             )
 
-        hb16 = shared.tile([P, PASSES * last_group, SLOTS], BF16, name="hb16", offset=AT_WA_SCALES, align_bytes=64)
-        hb16_first = hb16[:, : PASSES * GB].rearrange("p (ps j) t -> p ps j t", ps=PASSES)
-        hb16_wide = hb16[:, PASSES * GB :].rearrange("p (ps j) t -> p ps j t", ps=PASSES)
-        ha16 = keep.tile([P, M // GB, PASSES, GB, SLOTS], BF16, name="ha16", align_bytes=64)
-        nc.gpsimd.tensor_tensor(hb16_first, gel_first[:], s_sb[:].unsqueeze(2).to_broadcast([P, PASSES, GB, SLOTS]), MULT)
-        for g, ps in sorted(gel_b):
-            dst = hb16_wide[:, ps, (g - 1) * GB : g * GB]
-            if (g, ps) in ON_GPSIMD:
-                scale_pairs(nc.gpsimd, dst, gel_b[(g, ps)], s_sb[:, ps])
-            else:
-                scale_pairs(nc.vector, dst, gel_b[(g, ps)], s_cols[:, B_SIDE * PASSES + ps])
+        gel_first = [
+            shared.tile([P, 1, NB, SLOTS], F32, name="gel_first0", offset=AT_TAB, align_bytes=64),
+            keep.tile([P, 1, NB, SLOTS], F32, name="gel_first1"),
+        ]
+        for ps in range(PASSES):
+            hidden(wb_tile, ps, b_entries(0, NB), gel_first[ps][:, 0])
+        gel_second = keep.tile([P, PASSES, NB, SLOTS], F32, name="gel_second")
+        for ps in range(PASSES):
+            hidden(wb_tile, ps, b_entries(NB, NB), gel_second[:, ps])
+        gel_wide = shared.tile([P, PASSES, BANK, SLOTS], F32, name="gel_wide", offset=AT_CODES, align_bytes=64)
+        for h in range(BANK // NB):
+            for ps in range(PASSES):
+                hidden(wb_tile, ps, b_entries(GB + h * NB, NB), gel_wide[:, ps, h * NB : (h + 1) * NB])
+
+        hb16_first = keep.tile([P, PASSES, GB, SLOTS], BF16, name="hb16_first", align_bytes=64)
+        scale(hb16_first[:, 0:1, 0:NB], gel_first[0][:], 0)
+        nc.gpsimd.tensor_tensor(hb16_first[:, 1, 0:NB], gel_first[1][:, 0], s_sb[:, 1].unsqueeze(1).to_broadcast([P, NB, SLOTS]), MULT)
+        nc.gpsimd.tensor_tensor(hb16_first[:, :, NB:], gel_second[:], s_sb[:].unsqueeze(2).to_broadcast([P, PASSES, NB, SLOTS]), MULT)
+        ga_w = shared.tile([P, M], U32, name="ga_w", offset=AT_TAB, align_bytes=64)
+        ga_s = keep.tile([P, M], U8, name="ga_s", align_bytes=64)
+        gather(ga_w[:], ta_w, offs_a, 0)
+        gather(ga_s[:], ta_s, offs_a, 0)
+
+        gel_a = {}
+        for g in range(M // GB):
+            for ps in range(PASSES):
+                gel = keep.tile([P, SLOTS // PAIR, GB, PAIR], F32, name="gel_a%d%d" % (g, ps))
+                hidden_pairs(wa_tile, ps, a_entries(g * GB, GB), gel, no_bias[:] if (g, ps) == (1, 1) else 0.0)
+                gel_a[(g, ps)] = gel
+        last_group = J - GB
+        gel_last = keep.tile([P, GB // NB, PASSES, NB, SLOTS], F32, name="gel_last")
+        for h in range(GB // NB):
+            for ps in range(PASSES):
+                hidden(wb_tile, ps, b_entries(last_group + h * NB, NB), gel_last[:, h, ps])
+
+        hb16_wide = shared.tile([P, PASSES, BANK, SLOTS], BF16, name="hb16_wide", offset=AT_TA_SCALES, align_bytes=64)
+        ha16 = shared.tile([P, M // GB, PASSES, GB, SLOTS], BF16, name="ha16", offset=AT_HA16, align_bytes=64)
+        scale(hb16_wide[:, :, 0:SPLIT], gel_wide[:, :, 0:SPLIT], 0)
+        nc.gpsimd.tensor_tensor(hb16_wide[:, :, SPLIT:], gel_wide[:, :, SPLIT:], s_sb[:].unsqueeze(2).to_broadcast([P, PASSES, BANK - SPLIT, SLOTS]), MULT)
         for g, ps in sorted(gel_a):
-            scale_pairs(nc.vector, ha16[:, g, ps], gel_a[(g, ps)], s_cols[:, A_SIDE * PASSES + ps])
+            scale_pairs(nc.vector, ha16[:, g, ps], gel_a[(g, ps)][:], s_cols[:, A_SIDE * PASSES + ps])
 
         codes = shared.tile([P, PASSES * (J + M)], U32, name="codes", offset=AT_CODES, align_bytes=64)
-        planes = keep.tile([P, PASSES * (J + M)], U8, name="planes", align_bytes=64)
+        planes = shared.tile([P, PASSES * (J + M)], U8, name="planes", offset=AT_PLANES, align_bytes=64)
 
         def columns(c0, n):
             return codes[:, c0 : c0 + n].bitcast(FP8X4), planes[:, c0 : c0 + n]
@@ -266,14 +271,14 @@ def tile_list_biaff_gelu_exp_kernel(tc, tab_words, tab_scales, tab2_words, tab2_
             finish(y, m0, j0, n)
 
         quantize_a(0)
-        quantize(hb(0, GB, 0, PASSES), hb16_first.rearrange("p ps j t -> p (ps j t)"))
+        quantize(hb(0, GB, 0, PASSES), hb16_first[:].rearrange("p ps j t -> p (ps j t)"))
         scores(0, 0, GB)
         quantize_a(1)
         scores(GB // P, 0, GB)
-        quantize(hb(GB, BANK, 0, PASSES), hb16_wide.rearrange("p ps j t -> p (ps j t)"))
+        quantize(hb(GB, BANK, 0, PASSES), hb16_wide[:].rearrange("p ps j t -> p (ps j t)"))
         for mt in range(A_TILES):
             scores(mt, GB, BANK)
-        hb16_last = keep.tile([P, GB // NB, PASSES, NB, SLOTS], BF16, name="hb16_last", align_bytes=64)
+        hb16_last = shared.tile([P, GB // NB, PASSES, NB, SLOTS], BF16, name="hb16_last", offset=AT_HA16, align_bytes=64)
         scale(hb16_last[:, 0], gel_last[:, 0], 0)
         scale(hb16_last[:, 1, 0:1], gel_last[:, 1, 0:1], 0)
         quantize(hb(last_group, NB, 0, PASSES), hb16_last[:, 0].rearrange("p ps j t -> p (ps j t)"))

@@ -31,10 +31,12 @@ GROUPS = J // GB
 A_TILES = M // P
 PER_COLUMN = 16
 FACTOR_BANK = 0
-WARM_BANK, WARM_PASSES = 7, 4
+WARM_BANK, WARM_PASSES = 6, 4
+A_FACTOR_BANK = 7
 Z_BANKS = 4
 SCORE_BANKS = (5, 6, 7, 1, 2, 3, 4, 5)
 A_SIDE, B_SIDE = 0, 1
+ODD_CUTS = (0, 5, TILES)
 SPLIT = 216
 AT_HA16 = 49152
 AT_WB_SCALES, AT_WA_SCALES, AT_TA_SCALES, AT_TAB, AT_CODES, AT_PLANES = 0, 4096, 8192, 16384, 20480, 36864
@@ -53,9 +55,10 @@ def tile_list_biaff_gelu_exp_kernel(tc, tab_words, tab_scales, tab2_words, tab2_
 
         wb_s = shared.tile([P, R // 4], I32, name="wb_s", offset=AT_WB_SCALES, align_bytes=64)
         tb_s = keep.tile([P, T // 4], I32, name="tb_s", align_bytes=64)
-        ta_s = shared.tile([P, T // 4], I32, name="ta_s", offset=AT_TA_SCALES, align_bytes=64)
-        wa_s = shared.tile([P, R // 4], I32, name="wa_s", offset=AT_WA_SCALES, align_bytes=64)
-        s_rows = keep.tile([P, P], F32, name="s_rows")
+        ta_s = keep.tile([P, T // 4], I32, name="ta_s", align_bytes=64)
+        wa_s = shared.tile([P, R // 4], I32, name="wa_s", offset=AT_TA_SCALES, align_bytes=64)
+        sb_rows = keep.tile([P, P], F32, name="sb_rows")
+        sa_rows = keep.tile([P, P], F32, name="sa_rows")
         ident = keep.tile([P, P], F32, name="ident")
         zero = keep.tile([P, 1], F32, name="zero")
         nc.vector.memset(tb_s[:], 0)
@@ -67,7 +70,8 @@ def tile_list_biaff_gelu_exp_kernel(tc, tab_words, tab_scales, tab2_words, tab2_
         nc.vector.memset(no_bias[:], 0.0)
         nc.vector.memset(ident[:], 0.0)
         make_identity(nc, ident[:], nomemset=True)
-        nc.scalar.activation(s_rows[:], zero[:].to_broadcast([P, P]), ACT.Gelu_apprx_tanh)
+        nc.vector.memset(sa_rows[:], 0.0)
+        nc.scalar.activation(sb_rows[:], zero[:].to_broadcast([P, P]), ACT.Gelu_apprx_tanh)
 
         def load_scales(dst, src):
             rows = src[0].bitcast(I32)
@@ -77,16 +81,16 @@ def tile_list_biaff_gelu_exp_kernel(tc, tab_words, tab_scales, tab2_words, tab2_
         def load_words(dst, src):
             nc.sync.dma_start(dst[:], src[0].rearrange("p c i -> p (c i)").bitcast(I32))
 
-        def load_factor(side, vec):
+        def load_factor(rows, vec):
             nc.sync.dma_start(
-                s_rows[side * TILES : (side + 1) * TILES, :].rearrange("u (q i) -> u q i", i=RUN),
+                rows[0:TILES, :].rearrange("u (q i) -> u q i", i=RUN),
                 vec.rearrange("(q u i) -> u q i", u=TILES, i=RUN),
             )
 
         wb_w = keep.tile([P, R // 2], I32, name="wb_w", align_bytes=64)
         tb_w = keep.tile([P, T], I32, name="tb_w", align_bytes=64)
         ta_w = keep.tile([P, T], I32, name="ta_w", align_bytes=64)
-        wa_w = keep.tile([P, R], I32, name="wa_w", align_bytes=64)
+        wa_w = shared.tile([P, R], I32, name="wa_w", offset=AT_WA_SCALES, align_bytes=64)
         nc.sync.dma_start(wb_w[:], wb_words[0].bitcast(I32))
         nc.sync.dma_start(offs_b[:], offs2)
         nc.sync.dma_start(offs_a[:], offs)
@@ -94,9 +98,7 @@ def tile_list_biaff_gelu_exp_kernel(tc, tab_words, tab_scales, tab2_words, tab2_
         load_words(tb_w, tab2_words)
         load_scales(wb_s, wb_scales)
         load_words(wa_w, wa_words)
-        load_factor(A_SIDE, sa)
-        load_factor(B_SIDE, sb)
-        load_scales(wa_s, wa_scales)
+        load_factor(sb_rows, sb)
         warm = psum.tile([P, BANK], F32, name="warm", offset=WARM_BANK * BANK_BYTES)
         for rep in range(WARM_PASSES):
             nc.tensor.matmul_mx(
@@ -105,11 +107,13 @@ def tile_list_biaff_gelu_exp_kernel(tc, tab_words, tab_scales, tab2_words, tab2_
             )
         load_words(ta_w, tab_words)
         load_scales(ta_s, tab_scales)
+        load_factor(sa_rows, sa)
+        load_scales(wa_s, wa_scales)
 
-        def reorder(copy, name, src, run, parts=1):
+        def reorder(copy, name, src, run, cuts=(0, TILES)):
             dst = keep.tile([P, src.shape[1]], U32, name=name, align_bytes=64)
-            for part in range(parts):
-                tiles = slice(part * TILES // parts, (part + 1) * TILES // parts)
+            for u0, u1 in zip(cuts, cuts[1:]):
+                tiles = slice(u0, u1)
                 copy(
                     dst[:].rearrange("p (u q i) -> p u q i", u=TILES, i=run)[:, tiles],
                     src[:].bitcast(U32).rearrange("p (q u i) -> p u q i", u=TILES, i=run)[:, tiles],
@@ -126,10 +130,9 @@ def tile_list_biaff_gelu_exp_kernel(tc, tab_words, tab_scales, tab2_words, tab2_
         gb_w = keep.tile([P, J], U32, name="gb_w", align_bytes=64)
         gather(gb_w[:, 0:NB], tb_w, offs_b, 0)
         gather(gb_w[:, NB:BANK], tb_w, offs_b, NB)
-        wb_sr = reorder(nc.scalar.copy, "wb_sr", wb_s, RUN // 4, PASSES)
+        wb_sr = reorder(nc.scalar.copy, "wb_sr", wb_s, RUN // 4, (0, SLOTS, TILES))
         gather(gb_w[:, BANK:], tb_w, offs_b, BANK)
         wa_wr = reorder(nc.vector.tensor_copy, "wa_wr", wa_w, RUN)
-        wa_sr = reorder(nc.vector.tensor_copy, "wa_sr", wa_s, RUN // 4)
 
         def a_entries(n0, n):
             return ga_w[:, n0 : n0 + n].bitcast(FP8X4), ga_s[:, n0 : n0 + n]
@@ -169,16 +172,17 @@ def tile_list_biaff_gelu_exp_kernel(tc, tab_words, tab_scales, tab2_words, tab2_
                 first_layer(z[:, t, :], weights, ps, t, entries)
             nc.scalar.activation(dst, z[:].rearrange("p t n -> p n t"), ACT.Gelu_apprx_tanh)
 
-        s_psum = psum.tile([P, P], F32, name="s_psum", offset=FACTOR_BANK * BANK_BYTES)
-        nc.tensor.transpose(s_psum[:], s_rows[:], ident[:])
-        s_cols = s_psum[:, 0 : 2 * TILES].rearrange("p (x t) -> p x t", t=SLOTS)
+        s_cols = {}
+        for side, rows, bank in ((B_SIDE, sb_rows, FACTOR_BANK), (A_SIDE, sa_rows, A_FACTOR_BANK)):
+            turned = psum.tile([P, P], F32, name="turned%d" % side, offset=bank * BANK_BYTES)
+            nc.tensor.transpose(turned[:], rows[:], ident[:])
+            s_cols[side] = turned[:, 0:TILES].rearrange("p (ps t) -> p ps t", t=SLOTS)
         s_sb = shared.tile([P, PASSES, SLOTS], F32, name="s_sb", offset=AT_WA_SCALES, align_bytes=64)
-        nc.vector.tensor_copy(s_sb[:], s_cols[:, B_SIDE * PASSES :])
+        nc.vector.tensor_copy(s_sb[:], s_cols[B_SIDE])
 
         def scale(dst, src, ps0):
             count, n = src.shape[1], src.shape[2]
-            x = B_SIDE * PASSES + ps0
-            nc.vector.tensor_tensor(dst, src, s_cols[:, x : x + count, :].unsqueeze(2).to_broadcast([P, count, n, SLOTS]), MULT)
+            nc.vector.tensor_tensor(dst, src, s_cols[B_SIDE][:, ps0 : ps0 + count, :].unsqueeze(2).to_broadcast([P, count, n, SLOTS]), MULT)
 
         def scale_pairs(eng, dst, gel, factors):
             eng.tensor_tensor(
@@ -208,6 +212,7 @@ def tile_list_biaff_gelu_exp_kernel(tc, tab_words, tab_scales, tab2_words, tab2_
         ga_s = keep.tile([P, M], U8, name="ga_s", align_bytes=64)
         gather(ga_w[:], ta_w, offs_a, 0)
         gather(ga_s[:], ta_s, offs_a, 0)
+        wa_sr = reorder(nc.vector.tensor_copy, "wa_sr", wa_s, RUN // 4, ODD_CUTS)
 
         gel_a = {}
         for g in range(M // GB):
@@ -226,7 +231,7 @@ def tile_list_biaff_gelu_exp_kernel(tc, tab_words, tab_scales, tab2_words, tab2_
         scale(hb16_wide[:, :, 0:SPLIT], gel_wide[:, :, 0:SPLIT], 0)
         nc.gpsimd.tensor_tensor(hb16_wide[:, :, SPLIT:], gel_wide[:, :, SPLIT:], s_sb[:].unsqueeze(2).to_broadcast([P, PASSES, BANK - SPLIT, SLOTS]), MULT)
         for g, ps in sorted(gel_a):
-            scale_pairs(nc.vector, ha16[:, g, ps], gel_a[(g, ps)][:], s_cols[:, A_SIDE * PASSES + ps])
+            scale_pairs(nc.vector, ha16[:, g, ps], gel_a[(g, ps)][:], s_cols[A_SIDE][:, ps])
 
         codes = shared.tile([P, PASSES * (J + M)], U32, name="codes", offset=AT_CODES, align_bytes=64)
         planes = shared.tile([P, PASSES * (J + M)], U8, name="planes", offset=AT_PLANES, align_bytes=64)

@@ -34,8 +34,9 @@ FACTOR_BANK = 0
 WARM_BANK, WARM_PASSES = 6, 4
 A_FACTOR_BANK = 7
 Z_BANKS = 4
-SCORE_BANKS = (5, 6, 7, 1, 2, 3, 4, 5)
+SCORE_BANKS = (5, 6, 7, 3, 4, 1, 2, 5)
 A_SIDE, B_SIDE = 0, 1
+Z_TILES = TILES * (M + J) // BANK
 ODD_CUTS = (0, 5, TILES)
 SPLIT = 216
 AT_HA16 = 49152
@@ -152,6 +153,8 @@ def tile_list_biaff_gelu_exp_kernel(tc, tab_words, tab_scales, tab2_words, tab2_
 
         def z_bank(shape):
             bank = FACTOR_BANK + 1 + len(z_tiles) % Z_BANKS
+            if len(z_tiles) >= Z_TILES - PAIR:
+                bank -= PAIR
             z_tiles.append(psum.tile(shape, F32, name="z%d" % (len(z_tiles) + 1), offset=bank * BANK_BYTES))
             return z_tiles[-1]
 

from contextlib import ExitStack

import concourse.mybir as mybir
from concourse.masks import make_identity

K, R, T, M, J = 512, 1024, 2048, 512, 1024
FLOPS = 2 * K * R * M + 2 * K * R * J + 2 * R * M * J

F32 = mybir.dt.float32
BF16 = mybir.dt.bfloat16
I32 = mybir.dt.int32
U32 = mybir.dt.uint32
U16 = mybir.dt.uint16
U8 = mybir.dt.uint8
FP8X4 = mybir.dt.float8_e4m3fn_x4
FP4X4 = mybir.dt.float4_e2m1fn_x4
ACT = mybir.ActivationFunctionType
MULT = mybir.AluOpType.mult

P = 128
SLOTS = 4
PAIR = 2
RUN = 8
PASSES = R // 512
TILES = PASSES * SLOTS
BANK = 512
BANK_BYTES = 4 * BANK
NB = BANK // SLOTS
GB = BANK // PAIR
GROUPS = J // GB
A_TILES = M // P
PER_COLUMN = 16
FACTOR_BANK = 0
WARM_BANK, WARM_PASSES = 6, 4
A_FACTOR_BANK = 7
Z_BANKS = 4
SCORE_BANKS = (5, 6, 7, 3, 4, 1, 2, 5)
A_SIDE, B_SIDE = 0, 1
Z_TILES = TILES * (M + J) // BANK
ODD_CUTS = (0, 5, TILES)
SPLIT = 216
AT_HA16 = 49152
AT_WB_SCALES, AT_WA_SCALES, AT_TA_SCALES, AT_TAB, AT_CODES, AT_PLANES = 0, 4096, 8192, 16384, 20480, 36864


def tile_list_biaff_gelu_exp_kernel(tc, tab_words, tab_scales, tab2_words, tab2_scales, wa_words, wa_scales, wb_words, wb_scales, sa, sb, offs, offs2, out):
    nc = tc.nc
    with ExitStack() as ctx:
        lists = ctx.enter_context(tc.tile_pool(name="lists", bufs=1))
        keep = ctx.enter_context(tc.tile_pool(name="keep", bufs=1))
        shared = ctx.enter_context(tc.tile_pool(name="shared", bufs=1))
        psum = ctx.enter_context(tc.psum_pool(name="psum", bufs=1))

        offs_a = lists.tile([P, M // PER_COLUMN], U16, name="offs_a")
        offs_b = lists.tile([P, J // PER_COLUMN], U16, name="offs_b")

        wb_s = shared.tile([P, R // 4], I32, name="wb_s", offset=AT_WB_SCALES, align_bytes=64)
        tb_s = keep.tile([P, T // 4], I32, name="tb_s", align_bytes=64)
        ta_s = keep.tile([P, T // 4], I32, name="ta_s", align_bytes=64)
        wa_s = shared.tile([P, R // 4], I32, name="wa_s", offset=AT_TA_SCALES, align_bytes=64)
        sb_rows = keep.tile([P, P], F32, name="sb_rows")
        sa_rows = keep.tile([P, P], F32, name="sa_rows")
        ident = keep.tile([P, P], F32, name="ident")
        zero = keep.tile([P, 1], F32, name="zero")
        nc.vector.memset(tb_s[:], 0)
        nc.vector.memset(wb_s[:], 0)
        nc.vector.memset(ta_s[:], 0)
        nc.vector.memset(wa_s[:], 0)
        nc.vector.memset(zero[:], 0.0)
        no_bias = shared.tile([P, 1], F32, name="no_bias", offset=AT_PLANES, align_bytes=64)
        nc.vector.memset(no_bias[:], 0.0)
        nc.vector.memset(ident[:], 0.0)
        make_identity(nc, ident[:], nomemset=True)
        nc.vector.memset(sa_rows[:], 0.0)
        nc.scalar.activation(sb_rows[:], zero[:].to_broadcast([P, P]), ACT.Gelu_apprx_tanh)

        def load_scales(dst, src):
            rows = src[0].bitcast(I32)
            for row in range(4):
                nc.sync.dma_start(dst[row:P:32, :], rows[row:16:4, :])

        def load_words(dst, src):
            nc.sync.dma_start(dst[:], src[0].rearrange("p c i -> p (c i)").bitcast(I32))

        def load_factor(rows, vec):
            nc.sync.dma_start(
                rows[0:TILES, :].rearrange("u (q i) -> u q i", i=RUN),
                vec.rearrange("(q u i) -> u q i", u=TILES, i=RUN),
            )

        wb_w = keep.tile([P, R // 2], I32, name="wb_w", align_bytes=64)
        tb_w = keep.tile([P, T], I32, name="tb_w", align_bytes=64)
        ta_w = keep.tile([P, T], I32, name="ta_w", align_bytes=64)
        wa_w = shared.tile([P, R], I32, name="wa_w", offset=AT_WA_SCALES, align_bytes=64)
        nc.sync.dma_start(wb_w[:], wb_words[0].bitcast(I32))
        nc.sync.dma_start(offs_b[:], offs2)
        nc.sync.dma_start(offs_a[:], offs)
        load_scales(tb_s, tab2_scales)
        load_words(tb_w, tab2_words)
        load_scales(wb_s, wb_scales)
        load_words(wa_w, wa_words)
        load_factor(sb_rows, sb)
        warm = psum.tile([P, BANK], F32, name="warm", offset=WARM_BANK * BANK_BYTES)
        for rep in range(WARM_PASSES):
            nc.tensor.matmul_mx(
                out=warm[:], lhsT=ta_s[:, 0:P].bitcast(FP8X4), lhsT_scale=tb_s[:].bitcast(U8)[:, 0:P],
                rhs=ta_s[:].bitcast(FP8X4), rhs_scale=tb_s[:].bitcast(U8)[:, 0:BANK], start=True, stop=True,
            )
        load_words(ta_w, tab_words)
        load_scales(ta_s, tab_scales)
        load_factor(sa_rows, sa)
        load_scales(wa_s, wa_scales)

        def reorder(copy, name, src, run, cuts=(0, TILES)):
            dst = keep.tile([P, src.shape[1]], U32, name=name, align_bytes=64)
            for u0, u1 in zip(cuts, cuts[1:]):
                tiles = slice(u0, u1)
                copy(
                    dst[:].rearrange("p (u q i) -> p u q i", u=TILES, i=run)[:, tiles],
                    src[:].bitcast(U32).rearrange("p (q u i) -> p u q i", u=TILES, i=run)[:, tiles],
                )
            return dst

        def gather(dst, table, offsets, n0):
            n1 = n0 + dst.shape[1]
            nc.vector.tensor_copy(dst, table[:].bitcast(dst.dtype).indirect(offsets[:, n0 // PER_COLUMN : n1 // PER_COLUMN]))

        wb_wr = reorder(nc.scalar.copy, "wb_wr", wb_w, RUN // 2)
        gb_s = keep.tile([P, J], U8, name="gb_s", align_bytes=64)
        gather(gb_s[:], tb_s, offs_b, 0)
        gb_w = keep.tile([P, J], U32, name="gb_w", align_bytes=64)
        gather(gb_w[:, 0:NB], tb_w, offs_b, 0)
        gather(gb_w[:, NB:BANK], tb_w, offs_b, NB)
        wb_sr = reorder(nc.scalar.copy, "wb_sr", wb_s, RUN // 4, (0, SLOTS, TILES))
        gather(gb_w[:, BANK:], tb_w, offs_b, BANK)
        wa_wr = reorder(nc.vector.tensor_copy, "wa_wr", wa_w, RUN)

        def a_entries(n0, n):
            return ga_w[:, n0 : n0 + n].bitcast(FP8X4), ga_s[:, n0 : n0 + n]

        def b_entries(n0, n):
            return gb_w[:, n0 : n0 + n].bitcast(FP8X4), gb_s[:, n0 : n0 + n]

        def wb_tile(ps, t):
            c = (ps * SLOTS + t) * P
            return wb_wr[:].bitcast(U8)[:, 2 * c : 2 * c + 2 * P].bitcast(FP4X4), wb_sr[:].bitcast(U8)[:, c : c + P]

        def wa_tile(ps, t):
            c = (ps * SLOTS + t) * P
            return wa_wr[:, c : c + P].bitcast(FP8X4), wa_sr[:].bitcast(U8)[:, c : c + P]

        z_tiles = []

        def z_bank(shape):
            bank = FACTOR_BANK + 1 + len(z_tiles) % Z_BANKS
            if len(z_tiles) >= Z_TILES - PAIR:
                bank -= PAIR
            z_tiles.append(psum.tile(shape, F32, name="z%d" % (len(z_tiles) + 1), offset=bank * BANK_BYTES))
            return z_tiles[-1]

        def first_layer(dst, weights, ps, t, entries):
            w, ws = weights(ps, t)
            nc.tensor.matmul_mx(out=dst, lhsT=w, lhsT_scale=ws, rhs=entries[0], rhs_scale=entries[1], start=True, stop=True)

        def hidden_pairs(weights, ps, entries, dst, bias=0.0):
            for h in range(SLOTS // PAIR):
                z = z_bank([P, PAIR, GB])
                for t in range(PAIR):
                    first_layer(z[:, t, :], weights, ps, PAIR * h + t, entries)
                nc.scalar.activation(dst[:, h], z[:].rearrange("p t n -> p n t"), ACT.Gelu_apprx_tanh, bias=bias)

        def hidden(weights, ps, entries, dst):
            z = z_bank([P, SLOTS, NB])
            for t in range(SLOTS):
                first_layer(z[:, t, :], weights, ps, t, entries)
            nc.scalar.activation(dst, z[:].rearrange("p t n -> p n t"), ACT.Gelu_apprx_tanh)

        s_cols = {}
        for side, rows, bank in ((B_SIDE, sb_rows, FACTOR_BANK), (A_SIDE, sa_rows, A_FACTOR_BANK)):
            turned = psum.tile([P, P], F32, name="turned%d" % side, offset=bank * BANK_BYTES)
            nc.tensor.transpose(turned[:], rows[:], ident[:])
            s_cols[side] = turned[:, 0:TILES].rearrange("p (ps t) -> p ps t", t=SLOTS)
        s_sb = shared.tile([P, PASSES, SLOTS], F32, name="s_sb", offset=AT_WA_SCALES, align_bytes=64)
        nc.vector.tensor_copy(s_sb[:], s_cols[B_SIDE])

        def scale(dst, src, ps0):
            count, n = src.shape[1], src.shape[2]
            nc.vector.tensor_tensor(dst, src, s_cols[B_SIDE][:, ps0 : ps0 + count, :].unsqueeze(2).to_broadcast([P, count, n, SLOTS]), MULT)

        def scale_pairs(eng, dst, gel, factors):
            eng.tensor_tensor(
                dst.rearrange("p n (h t) -> p n h t", t=PAIR), gel.rearrange("p h n t -> p n h t"),
                factors.rearrange("p (h t) -> p h t", t=PAIR).unsqueeze(1).to_broadcast([P, dst.shape[1], SLOTS // PAIR, PAIR]), MULT,
            )

        gel_first = [
            shared.tile([P, 1, NB, SLOTS], F32, name="gel_first0", offset=AT_TAB, align_bytes=64),
            keep.tile([P, 1, NB, SLOTS], F32, name="gel_first1"),
        ]
        for ps in range(PASSES):
            hidden(wb_tile, ps, b_entries(0, NB), gel_first[ps][:, 0])
        gel_second = keep.tile([P, PASSES, NB, SLOTS], F32, name="gel_second")
        for ps in range(PASSES):
            hidden(wb_tile, ps, b_entries(NB, NB), gel_second[:, ps])
        gel_wide = shared.tile([P, PASSES, BANK, SLOTS], F32, name="gel_wide", offset=AT_CODES, align_bytes=64)
        for h in range(BANK // NB):
            for ps in range(PASSES):
                hidden(wb_tile, ps, b_entries(GB + h * NB, NB), gel_wide[:, ps, h * NB : (h + 1) * NB])

        hb16_first = keep.tile([P, PASSES, GB, SLOTS], BF16, name="hb16_first", align_bytes=64)
        scale(hb16_first[:, 0:1, 0:NB], gel_first[0][:], 0)
        nc.gpsimd.tensor_tensor(hb16_first[:, 1, 0:NB], gel_first[1][:, 0], s_sb[:, 1].unsqueeze(1).to_broadcast([P, NB, SLOTS]), MULT)
        nc.gpsimd.tensor_tensor(hb16_first[:, :, NB:], gel_second[:], s_sb[:].unsqueeze(2).to_broadcast([P, PASSES, NB, SLOTS]), MULT)
        ga_w = shared.tile([P, M], U32, name="ga_w", offset=AT_TAB, align_bytes=64)
        ga_s = keep.tile([P, M], U8, name="ga_s", align_bytes=64)
        gather(ga_w[:], ta_w, offs_a, 0)
        gather(ga_s[:], ta_s, offs_a, 0)
        wa_sr = reorder(nc.vector.tensor_copy, "wa_sr", wa_s, RUN // 4, ODD_CUTS)

        gel_a = {}
        for g in range(M // GB):
            for ps in range(PASSES):
                gel = keep.tile([P, SLOTS // PAIR, GB, PAIR], F32, name="gel_a%d%d" % (g, ps))
                hidden_pairs(wa_tile, ps, a_entries(g * GB, GB), gel, no_bias[:] if (g, ps) == (1, 1) else 0.0)
                gel_a[(g, ps)] = gel
        last_group = J - GB
        gel_last = keep.tile([P, GB // NB, PASSES, NB, SLOTS], F32, name="gel_last")
        for h in range(GB // NB):
            for ps in range(PASSES):
                hidden(wb_tile, ps, b_entries(last_group + h * NB, NB), gel_last[:, h, ps])

        hb16_wide = shared.tile([P, PASSES, BANK, SLOTS], BF16, name="hb16_wide", offset=AT_TA_SCALES, align_bytes=64)
        ha16 = shared.tile([P, M // GB, PASSES, GB, SLOTS], BF16, name="ha16", offset=AT_HA16, align_bytes=64)
        scale(hb16_wide[:, :, 0:SPLIT], gel_wide[:, :, 0:SPLIT], 0)
        nc.gpsimd.tensor_tensor(hb16_wide[:, :, SPLIT:], gel_wide[:, :, SPLIT:], s_sb[:].unsqueeze(2).to_broadcast([P, PASSES, BANK - SPLIT, SLOTS]), MULT)
        for g, ps in sorted(gel_a):
            scale_pairs(nc.vector, ha16[:, g, ps], gel_a[(g, ps)][:], s_cols[A_SIDE][:, ps])

        codes = shared.tile([P, PASSES * (J + M)], U32, name="codes", offset=AT_CODES, align_bytes=64)
        planes = shared.tile([P, PASSES * (J + M)], U8, name="planes", offset=AT_PLANES, align_bytes=64)

        def columns(c0, n):
            return codes[:, c0 : c0 + n].bitcast(FP8X4), planes[:, c0 : c0 + n]

        def hb(j0, n, ps, count=1):
            return columns(PASSES * j0 + ps * n, count * n)

        def ha(mt, ps):
            g, m0 = divmod(mt * P, GB)
            return columns(PASSES * (J + g * GB) + ps * GB + m0, P)

        def quantize(dst, src):
            nc.vector.quantize_mx(out=dst[0], scales=dst[1], in_=src)

        def quantize_a(g):
            quantize(columns(PASSES * (J + g * GB), PASSES * GB), ha16[:, g].rearrange("p ps n t -> p (ps n t)"))

        def score(dst, mt, j0, n, ps, start, stop):
            nc.tensor.matmul_mx(out=dst, lhsT=ha(mt, ps)[0], lhsT_scale=ha(mt, ps)[1], rhs=hb(j0, n, ps)[0], rhs_scale=hb(j0, n, ps)[1], start=start, stop=stop)

        y_tiles = []

        def y_bank():
            y_tiles.append(psum.tile([P, BANK], F32, name="y%d" % len(y_tiles), offset=SCORE_BANKS[len(y_tiles)] * BANK_BYTES))
            return y_tiles[-1]

        out_rows = out.rearrange("(m p) j -> p m j", p=P)

        def finish(y, m0, j0, n):
            res = keep.tile([P, BANK], F32, name="res%d_%d" % (m0, j0))
            nc.scalar.activation(res[:], y[:], ACT.Exp, scale=1.0 / 64)
            nc.sync.dma_start(out_rows[:, m0 : m0 + BANK // n, j0 : j0 + n], res[:].rearrange("p (m j) -> p m j", j=n))

        def scores(m0, j0, n):
            y = y_bank()
            for place in range(BANK // n):
                for ps in range(PASSES):
                    score(y[:, place * n : (place + 1) * n], m0 + place, j0, n, ps, ps == 0, ps == PASSES - 1)
            finish(y, m0, j0, n)

        quantize_a(0)
        quantize(hb(0, GB, 0, PASSES), hb16_first[:].rearrange("p ps j t -> p (ps j t)"))
        scores(0, 0, GB)
        quantize_a(1)
        scores(GB // P, 0, GB)
        quantize(hb(GB, BANK, 0, PASSES), hb16_wide[:].rearrange("p ps j t -> p (ps j t)"))
        for mt in range(A_TILES):
            scores(mt, GB, BANK)
        hb16_last = shared.tile([P, GB // NB, PASSES, NB, SLOTS], BF16, name="hb16_last", offset=AT_HA16, align_bytes=64)
        scale(hb16_last[:, 0], gel_last[:, 0], 0)
        scale(hb16_last[:, 1, 0:1], gel_last[:, 1, 0:1], 0)
        quantize(hb(last_group, NB, 0, PASSES), hb16_last[:, 0].rearrange("p ps j t -> p (ps j t)"))
        scores(0, last_group, NB)
        scale(hb16_last[:, 1, 1:2], gel_last[:, 1, 1:2], 1)
        y = y_bank()
        for ps in range(PASSES):
            quantize(hb(J - NB, NB, ps), hb16_last[:, 1, ps].rearrange("p j t -> p (j t)"))
            for mt in range(A_TILES):
                score(y[:, mt * NB : (mt + 1) * NB], mt, J - NB, NB, ps, (ps, mt) == (0, 0), (ps, mt) == (PASSES - 1, A_TILES - 1))
        finish(y, 0, J - NB, NB)
